import numpy as np, ml_dtypes
CORES = [2,3,42,43,82,83,122,123]
N = 8
BF = ml_dtypes.bfloat16
def gentries(a):
    return np.ascontiguousarray(a.reshape(8, 16, -1).transpose(0, 2, 1)).reshape(8, -1)
def gtable(e):
    e = np.asarray(e); return np.ascontiguousarray(e.reshape(8, -1, 16).transpose(0, 2, 1)).reshape(128, -1).astype(np.int32)
V, L, SH, EPS, RO = 4096, 256, 1, 3, 5
Q = 256 >> SH; LQ = 8 - SH; E = 16 * Q
TIGHT = (2 ** SH - 1 - EPS, EPS)
def labels(rng):
    slot = np.argsort(rng.random((8, 16, 16)), axis=-1); size = rng.permutation(np.array([6, 7, 8, 8, 10, 12, 14, 16]))[:, None, None]
    high = 8 + np.argsort(rng.random((8, 16, 8)), axis=-1); slot[..., :8] = np.where(size == 8, high, slot[..., :8])
    u = (rng.random((N, 8, 16, V)) * size).astype(np.int64)
    return 16 * np.take_along_axis(np.ascontiguousarray(np.broadcast_to(slot, (N, 8, 16, 16))), u, 3) + 8 + rng.integers(-3, 4, (N, 8, 16, V))
def inverse(rng, s, near, lo, hi):
    near = np.broadcast_to(near, (N, 8, 16, Q, 16)); out = np.empty((N, 8, 16, Q, 16), np.int64); base = np.arange(Q) << SH
    order = np.argsort(s.astype(np.int16), axis=-1, kind="stable")
    for r in range(N):
        for g in range(8):
            for p in range(16):
                o = order[r, g, p]; v = s[r, g, p][o]
                a = np.searchsorted(v, base + lo, "left"); n = (np.searchsorted(v, base + hi, "right") - a)[:, None]
                fa = np.searchsorted(v, base - EPS, "left"); fb = np.searchsorted(v, base + 2 ** SH - 1 + EPS, "right")
                u = rng.random((Q, 16))
                far = (fb[:, None] + (u * (V - (fb - fa))[:, None]).astype(np.int64)) % V
                out[r, g, p] = o[np.where(near[r, g, p] & (n > 0), np.minimum(a[:, None] + (u * n).astype(np.int64), V - 1), far)]
    return np.ascontiguousarray(out.reshape(N, 8, E, 16).transpose(0, 1, 3, 2))
def starts(rng, s, share):
    p = rng.integers(0, 16, (N, 8, L)); c = rng.integers(0, V, (N, 8, L))
    y = s[np.arange(N)[:, None, None], np.arange(8)[None, :, None], p, c]
    return np.where(rng.random((N, 8, L)) < share, Q * p + (y >> SH), rng.integers(0, E, (N, 8, L)))
def pack(s, w, e):
    return {"st": np.ascontiguousarray(s.reshape(N, 128, V)).astype(np.float32).astype(BF), "iv": np.ascontiguousarray(w).reshape(N, 128, E).astype(np.int32), "e0": np.stack([gtable(x) for x in e])}
def setup_inputs(rng):
    s = labels(rng); near = rng.random((N, 8, 16, Q, 16)) < rng.choice(np.array([0.5, 0.7, 0.85, 0.95]), (N, 8, 1, 1, 1))
    return pack(s, inverse(rng, s, near, *TIGHT), starts(rng, s, 0.85))
def setup_inputs_spread(rng):
    pw = rng.permutation(np.array([1.0, 1.0, 1.0, 2.0, 3.0, 4.0, 6.0, 8.0]))[:, None, None]
    s = np.minimum((256 * rng.random((N, 8, 16, V)) ** pw).astype(np.int64), 255)
    s = np.where(rng.random((8, 16, 1)) < 0.5, 255 - s, s); near = rng.random((N, 8, 16, Q, 16)) < 0.6
    return pack(s, inverse(rng, s, near, *TIGHT), starts(rng, s, 0.5))
def setup_inputs_ends(rng):
    s = 255 * rng.integers(0, 2, (N, 8, 16, V))
    s[..., V - 1] = 255; s[..., V - 2] = 255 - EPS - 1; s[..., V - 4:V - 2] = 255 - 2 * EPS - 2; s[:, :, 15, V - 4:] = 255; s[::2, :, 14, V - 4:V - 2] -= 1
    s[..., 0] = 0; s[..., 1] = EPS + 1; s[..., 2] = 2 * EPS + 2; s[:, :, 0, :3] = 0
    w = np.where(rng.random((N, 8, 16, E)) < 0.75, (V - 1) * rng.integers(0, 2, (N, 8, 16, E)), rng.integers(0, V, (N, 8, 16, E)))
    alike = rng.integers(0, 2, (N, 8)); alike[:, 0] = 1; alike[:, 7] = 0
    third = V - 3 - rng.integers(0, 2, (N, 8)); third[0, 7] = V - 3; third[N - 1, 7] = V - 4
    hi = np.where(rng.random((N, 8, 16)) < 0.7, V - 1, 0); hi[:, :, 13] = V - 1; hi[:, :, 14] = V - 2; hi[:, :, 15] = third
    lo = np.where(rng.random((N, 8, 16)) < 0.7, 0, V - 1); lo[:, :, 13] = 0; lo[:, :, 14] = 1; lo[:, :, 15] = 2
    w[..., E - 1] = np.where(alike[:, :, None] == 1, V - 1, hi); w[..., 0] = np.where(alike[:, :, None] == 1, 0, lo)
    e = np.where(rng.random((N, 8, L)) < 0.85, (E - 1) * rng.integers(0, 2, (N, 8, L)), rng.integers(0, E, (N, 8, L)))
    e[:, :, 0] = 0; e[:, :, L - 1] = E - 1
    return pack(s, w, e)
def setup_inputs_corners(rng):
    s = labels(rng); lane = np.arange(L)
    s[:, 1] = rng.integers(0, 256, (16, 1)); s[:, 4] = rng.integers(0, 256, (N, 16, V))
    ta = rng.integers(0, 100, 16); ty = rng.integers(0, 2, (N, 1, V)) ^ (rng.random((N, 16, V)) < 0.03); ty[:, 5] = 0
    s[:, 5] = ta[None, :, None] + 120 * ty
    near = rng.random((N, 8, 16, Q, 16)) < 0.8
    near[:, 0] = False; near[:, 1] = True; near[:, 2] = np.arange(16) == 15; near[:, 3] = np.arange(16) == 0; near[:, 4] = True; near[:, 5] = True
    w = inverse(rng, s, near, *TIGHT); e = starts(rng, s, 0.9)
    w[:, 6] = np.where(rng.random((N, 1, E)) < 0.5, (V - 1) * rng.integers(0, 2, (N, 1, E)), w[:, 6])
    own = lane + L * rng.integers(0, E // L, (N, L)); pick = rng.integers(0, 4, (N, L))
    e[:, 5] = Q * 5 + (ta[5] >> SH)
    e[:, 6] = np.where(pick == 0, 0, np.where(pick == 1, E - 1, np.where(pick == 2, own, e[:, 6])))
    e[:, 7] = np.where(rng.random((N, L)) < 0.5, own, e[:, 7])
    return pack(s, w, e)
def setup_inputs_crowd(rng):
    s = labels(rng); t = rng.integers(0, 256, (6, 16))
    s[:, :6] = t[:, :, None]; s[:, :6, :8, 1::2] = ((t + 128) & 255)[:, :8, None]
    w = inverse(rng, s, rng.random((N, 8, 16, Q, 16)) < 0.8, *TIGHT); e = starts(rng, s, 0.8)
    cnt = (np.arange(6) % 3)[None, :, None, None]; place = np.argsort(rng.random((N, 6, 16, E)), axis=2)
    w[:, :6] = 2 * rng.integers(0, V // 2, (N, 6, 16, E)) + (place < cnt)
    p = rng.integers(8, 16, 6); p[5] = rng.integers(0, 8)
    e[:, :6] = (Q * p + (t[np.arange(6), p] >> SH))[None, :, None]
    for g in (1, 3, 5): e[np.arange(N), g, rng.integers(0, L, N)] = rng.integers(0, E, N)
    e[:, 6] = e[:, 6, :1]
    return pack(s, w, e)
def setup_inputs_ties(rng):
    kinds = rng.permutation(np.array([2, 3, 4, 5, 6, 7, 8, 8]))[:, None, None]
    shift = rng.integers(0, 30 - 2 * EPS, (8, 16, 1)); shift[:, 0] = 0; shift[:, 15] = 29 - 2 * EPS
    off = np.array([0, EPS, EPS + 1, 2 * EPS, 2 * EPS + 1, 2 * EPS + 2])
    s = 32 * (rng.random((N, 8, 16, V)) * kinds).astype(np.int64) + shift + off[rng.integers(0, 6, (N, 8, 16, V))]
    near = rng.random((N, 8, 16, Q, 16)) < 0.9
    return pack(s, inverse(rng, s, near, -EPS - 1, EPS + 2 ** SH), starts(rng, s, 0.95))
def check_inputs(d):
    bad = []
    for k, lo, hi in (("st", 0, 255), ("iv", 0, V - 1), ("e0", 0, E - 1)):
        a = np.asarray(d[k]).astype(np.float64)
        if not (np.min(a) >= lo and np.max(a) <= hi): bad.append("range of " + k)
        if np.any(a != np.floor(a)): bad.append("whole numbers in " + k)
    return bad
def carry(x):
    B = L // N
    return np.concatenate([np.roll(x[..., b * B:(b + 1) * B], b, axis=0) for b in range(N)], axis=-1)
def reference(st, iv, e0):
    s = st.astype(np.float32).astype(np.int64).reshape(N, 8, 16, V); w = iv.astype(np.int64).reshape(N, 8, 16, E)
    e = np.stack([gentries(x) for x in e0]).astype(np.int64)
    row = np.arange(16)[:, None]; lane = np.arange(L)
    core = row == (e >> LQ)[:, :, None]; kl = np.where(core, ((e & (Q - 1)) << SH)[:, :, None], 0)
    p0 = np.zeros((N, 8, 16, L), np.int64); p1 = np.zeros((N, 8, 16, L), np.int64); n = np.zeros((N, 8, L), np.int64); a = np.zeros((N, 8, L), np.int64)
    for step in range(RO):
        if step > 0: e, core, kl, p0, p1, n, a = [carry(x) for x in (e, core, kl, p0, p1, n, a)]
        c = np.take_along_axis(w, e[:, :, None], 3)
        y = np.take_along_axis(s[:, :, None], c[:, :, :, None], 4)
        el = np.all((np.abs(y - kl[:, :, None]) <= EPS) | ~core[:, :, None], axis=3)
        m = (np.abs(y - p0[:, :, None]) <= EPS) & (n > 0)[:, :, None, None]
        m = m | ((np.abs(y - p1[:, :, None]) <= EPS) & (n > 1)[:, :, None, None])
        m = m & ~core[:, :, None] & el[:, :, :, None]
        ok = el & ~np.any(m, axis=3)
        join = np.any(ok, axis=2); some = np.any(el, axis=2); grow = some & ~join; dead = ~some; full = join & (n == 2)
        pr = np.argmax(np.add.reduce(m.astype(np.int64), axis=2), axis=2)
        kr = np.argmax(np.take_along_axis(m, pr[:, :, None, None], 3)[:, :, :, 0], axis=2)
        j = np.where(join, np.argmax(ok, axis=2), kr)
        z = np.take_along_axis(y, j[:, :, None, None], 2)[:, :, 0]
        lab = np.take_along_axis(z, pr[:, :, None], 2)[:, :, 0]
        d = np.repeat((e - (e & (L - 1)) + lane)[:, :, None], 16, axis=2); old = np.take_along_axis(w, d, 3)
        new = (37 * np.take_along_axis(c, j[:, :, None], 2) + (e + a)[:, :, None]) & (V - 1)
        np.put_along_axis(w, d, np.where((row == j[:, :, None]) & join[:, :, None], new, old), 3)
        f = np.minimum(np.minimum(p0, p1), z); q = np.add.reduce(f, axis=2) & 15; lq = np.take_along_axis(f, q[:, :, None], 2)[:, :, 0]
        s0 = (n > 0) & (np.abs(np.take_along_axis(p0, pr[:, :, None], 2)[:, :, 0] - lab) <= EPS)
        s1 = (n > 1) & (np.abs(np.take_along_axis(p1, pr[:, :, None], 2)[:, :, 0] - lab) <= EPS)
        e = np.where(dead, (5 * e + 1 + a) & (E - 1), np.where(full, Q * q + (lq >> SH), np.where(grow, Q * pr + (lab >> SH), e)))
        again = dead | full; one = again[:, :, None]; enter = (row == pr[:, :, None]) & grow[:, :, None]; first = row == (e >> LQ)[:, :, None]
        core = np.where(one, first, core | enter)
        kl = np.where(one, np.where(dead, (e & (Q - 1)) << SH, lq)[:, :, None], np.where(enter, lab[:, :, None], kl))
        p0 = np.where((join & (n == 0))[:, :, None], z, np.where((grow & ~s0)[:, :, None], p1, p0))
        p1 = np.where((join & (n == 1))[:, :, None], z, p1)
        n = np.where(again, 0, np.where(join, n + 1, s0.astype(np.int64) + s1)); a = a + again
    yi = w
    return {"yk": np.where(core, kl, -1).reshape(N, 128, L).astype(np.float32).astype(BF), "y0": np.where((n > 0)[:, :, None], p0, -1).reshape(N, 128, L).astype(np.float32).astype(BF),
            "y1": np.where((n > 1)[:, :, None], p1, -1).reshape(N, 128, L).astype(np.float32).astype(BF), "ye": np.stack([gtable(x) for x in e]).astype(np.float32),
            "ya": np.stack([gtable(x) for x in a]).astype(np.float32), "yi": np.ascontiguousarray(yi).reshape(N, 128, -1).astype(np.float32)}

@@ -1,0 +1,684 @@
+import math
+from concourse.bass import DstId, RemoteDMATransfer
+from concourse.mybir import dt, AluOpType, AxisListType, ActivationFunctionType
+
+AL = AluOpType
+AF = ActivationFunctionType
+RO = 5
+W = 128
+NW = 60
+YE = ['ADAAAAAA', 'ADADAAAA', 'ADADAAAA', 'ADAAAAAD', 'ADADADAA']
+SEED = [6559, 0.1, 0.0, {'q1': -2.8, 'b1': -7.3, 'p1': 1.0, 'set': 2.9, 'q0': -1.1, 'p0': 0.5, 'b0': -0.3}]
+ROUNDS = [4]
+SCL = 1.25
+C8 = 100663304.0
+C1 = 12582912.0
+C16 = 201326592.0
+C11 = 25769803776.0
+
+SCRATCH = {
+    "stb": ("sbuf", [128, 4096], "bfloat16"), "ivi": ("sbuf", [128, 2048], "int32"), "ivf": ("sbuf", [128, 2048], "float32"),
+    "e0i": ("sbuf", [128, 16], "int32"), "e0p": ("sbuf", [128, 32], "int32"), "e0u": ("sbuf", [128, 16], "uint16"),
+    "sta": ("sbuf", [128, 10, 784], "bfloat16"), "snd": ("sbuf", [128, 10, 512], "bfloat16"),
+    "Wm": ("sbuf", [128, NW, 8, 16], "bfloat16"), "Z": ("sbuf", [128, 3, 144], "bfloat16"),
+    "ones": ("sbuf", [128, 128], "bfloat16"), "zer": ("sbuf", [128, 8, 16], "bfloat16"),
+    "cols": ("sbuf", [128, 16], "float32"), "colb": ("sbuf", [128, 8], "bfloat16"), "coli": ("sbuf", [128, 8], "int32"),
+    "E16": ("sbuf", [128, 16], "float32"),
+    "it1": ("sbuf", [128, 256], "float32"), "it2": ("sbuf", [128, 256], "float32"), "dm": ("sbuf", [128, 512], "bfloat16"),
+    "dcon": ("sbuf", [128, 256], "bfloat16"), "econ": ("sbuf", [128, 128], "bfloat16"), "seg": ("sbuf", [128, 256], "float32"),
+    "ofi": ("sbuf", [128, 32], "int32"), "ofu": ("sbuf", [128, 32], "uint16"), "X0": ("sbuf", [128, 512], "bfloat16"),
+    "O0": ("sbuf", [128, 2, 256], "bfloat16"),
+    "Y": ("sbuf", [128, 2, 2048], "bfloat16"), "mis": ("sbuf", [128, 3, 512], "bfloat16"), "mm": ("sbuf", [128, 3, 512], "bfloat16"),
+    "ab": ("sbuf", [128, 3, 512], "bfloat16"), "thr": ("sbuf", [128, 2, 512], "bfloat16"),
+    "c16": ("sbuf", [128, 2, 128], "uint16"), "lu": ("sbuf", [128, 2, 48], "uint16"),
+    "sf": ("sbuf", [128, 2, 12, 128], "float32"), "si": ("sbuf", [128, 2, 2, 128], "int32"),
+    "sb": ("sbuf", [128, 2, 18, 128], "bfloat16"), "sw": ("sbuf", [128, 2, 3, 256], "bfloat16"),
+    "scn": ("sbuf", [128, 2, 256], "float32"), "sc2": ("sbuf", [128, 2, 4, 256], "float32"),
+    "ok_": ("sbuf", [128, 256], "bfloat16"), "oy": ("sbuf", [128, 2, 256], "bfloat16"), "oyy": ("sbuf", [128, 2, 256], "bfloat16"),
+    "oe": ("sbuf", [128, 2, 16], "float32"),
+}
+for _b in range(8):
+    SCRATCH["ps%d" % _b] = ("psum", [128, 512], "float32")
+SEMAPHORES = ["sP", "sD", "sA", "sG", "le0", "liv", "lst", "out", "outA", "loc"] + ["ar%d" % _n for _n in range(2, 10)] + ["ap%d" % _n for _n in range(2, 10)]
+
+FAC = 1.25
+
+
+def build(g, core, T, topo):
+    ops = []
+    last_w = {}
+    readers = {}
+    phase = ["set"]
+    gate = []
+
+    def op(eng, fn, rd, wr, dur, banks=(), sem=None, lat=0.0):
+        n = len(ops)
+        deps = set()
+        for r in rd:
+            if r in last_w:
+                deps.add(last_w[r])
+        for w in wr:
+            if w in last_w:
+                deps.add(last_w[w])
+            deps.update(readers.get(w, ()))
+        for r in rd:
+            readers.setdefault(r, []).append(n)
+        for w in wr:
+            last_w[w] = n
+            readers[w] = []
+        deps.discard(n)
+        if phase[0] == "late" and gate:
+            deps.add(gate[0])
+        ops.append({"ph": phase[0], "eng": eng, "fn": fn, "deps": deps, "dur": dur, "banks": tuple(banks), "sem": sem, "lat": lat, "wr": wr})
+        return n
+
+    def bk(*names):
+        return tuple(sorted(set(int(x[2]) for x in names if x.startswith("ps"))))
+
+    def dv(fn, rd, wr, cyc):
+        return op("D", fn, rd, wr, 0.06 + max(cyc, 64) * 0.83e-3 * FAC, bk(*rd, *wr))
+
+    def ac(fn, rd, wr, cyc):
+        return op("A", fn, rd, wr, 0.08 + max(cyc, 64) * 0.83e-3 * FAC, bk(*rd, *wr))
+
+    def po(fn, rd, wr, n):
+        return op("G", fn, rd, wr, (0.17 + 2 * n * 0.83e-3) * FAC)
+
+    def ts(out, in0, s1, s2, o0, o1, rd, wr, cyc):
+        if o1 is None:
+            return dv(lambda: g.vector.tensor_scalar(out, in0, s1, None, o0), rd, wr, cyc)
+        return dv(lambda: g.vector.tensor_scalar(out, in0, s1, s2, o0, o1), rd, wr, cyc)
+
+    def tt(out, a, b, o, rd, wr, cyc):
+        return dv(lambda: g.vector.tensor_tensor(out, a, b, o), rd, wr, cyc)
+
+    def cp(out, a, rd, wr, cyc):
+        return dv(lambda: g.vector.tensor_copy(out, a), rd, wr, cyc)
+
+    def act(out, a, f, rd, wr, cyc, bias=0.0, scale=1.0):
+        return ac(lambda: g.scalar.activation(out, a, f, bias=bias, scale=scale), rd, wr, cyc)
+
+    def pe(items, rd, wr, first=True, final=True):
+        def fn():
+            r = None
+            for q, it in enumerate(items):
+                r = g.tensor.matmul(it[0], it[1], it[2], first and q == 0, final and q == len(items) - 1)
+            return r
+        cyc = sum(max(64, it[3]) for it in items)
+        return op("P", fn, list(rd) + [it[4] for it in items], wr, 0.03 + cyc * 0.417e-3 * FAC, bk(*wr))
+
+    op("S", lambda: g.sync.dma_start(T.e0i[:], T.e0[:]), [], ["e0i"], 0.1, sem=("le0", 16), lat=2.0)
+    op("S", lambda: g.sync.dma_start(T.ivi[:], T.iv[:]), [], ["ivi"], 0.1, sem=("liv", 16), lat=6.0)
+    op("A", lambda: g.scalar.dma_start(T.stb[:], T.st[:]), [], ["stb"], 0.1, sem=("lst", 16), lat=7.0)
+
+    slot = {}
+
+    def wm(name):
+        if name not in slot:
+            slot[name] = len(slot)
+        return T.Wm[:, slot[name]]
+
+    def Wt(name):
+        return (wm(name), "W" + name)
+
+    def ms(ap, v, wr, cyc):
+        return dv(lambda: g.vector.memset(ap, v), [], wr, cyc)
+
+    ms(T.ones[:], 1.0, ["ones"], 64)
+    ms(T.zer[:], 0.0, ["zer"], 64)
+    po(lambda: g.iota(T.coli[:, 0:1], [[0, 1]], 0, 1), [], ["coli0"], 1)
+    po(lambda: g.affine_select(wm("I"), T.ones[:], [[-1, 128]], AL.is_equal, 0.0, 0, 1), ["ones"], ["WI"], 128)
+    po(lambda: g.affine_select(wm("B0"), T.ones[:], [[-16, 8], [0, 16]], AL.is_ge, 0.0, 0, 1), ["ones"], ["WB0"], 128)
+    po(lambda: g.iota(T.it1[:], [[0, 16], [1, 16]], 0, 0, allow_small_or_imprecise_dtypes=True), [], ["it1"], 256)
+    po(lambda: g.affine_select(wm("B"), wm("B0"), [[16, 8], [0, 16]], AL.is_ge, 0.0, 15, -1), ["WB0"], ["WB"], 128)
+    po(lambda: g.iota(T.ofi[:], [[1, 32]], 0, 0), [], ["ofi"], 32)
+    po(lambda: g.iota(T.it2[:], [[1, 256]], 32768, 0, allow_small_or_imprecise_dtypes=True), [], ["it2"], 256)
+    po(lambda: g.affine_select(wm("L"), wm("B"), [[1, 128]], AL.is_gt, 0.0, 0, -1), ["WB"], ["WL"], 128)
+    ts(T.coli[:, 1:2], T.coli[:, 0:1], 15, None, AL.bitwise_and, None, ["coli0"], ["coli1"], 1)
+    pcol = T.cols[:, 0:1]
+    cp(pcol, T.coli[:, 1:2], ["coli1"], ["pcol"], 1)
+    cp(T.ofu[:], T.ofi[:], ["ofi"], ["ofu"], 32)
+    ts(T.dm[:, 0:256], T.it1[:], pcol, None, AL.is_equal, None, ["it1", "pcol"], ["dm0"], 256)
+    cp(T.dm[:, 256:512], T.dm[:, 0:256], ["dm0"], ["dm1"], 128)
+    ts(T.seg[:], T.it1[:], 0.5, None, AL.is_gt, None, ["it1"], ["seg"], 256)
+    tt(T.it2[:], T.it2[:], T.dm[:, 0:256], AL.mult, ["it2", "dm0"], ["it2"], 512)
+    ts(T.dcon[:], T.it2[:], -32768.0, None, AL.add, None, ["it2"], ["dcon"], 256)
+    ts(T.econ[:], T.dm[:, 0:128], 32768.0, -32768.0, AL.mult, AL.add, ["dm0"], ["econ"], 64)
+    ts(T.E16[:], T.it1[:, 0:16], pcol, None, AL.is_equal, None, ["it1", "pcol"], ["E16"], 16)
+    act(T.colb[:, 0:1], pcol, AF.Exp, ["pcol"], ["p2"], 1, scale=math.log(2.0))
+    act(T.colb[:, 1:2], pcol, AF.Exp, ["pcol"], ["p2n"], 1, scale=-math.log(2.0), bias=-math.log(2.0))
+    cp(T.cols[:, 1:2], T.colb[:, 0:1], ["p2"], ["p2f"], 1)
+    cp(T.cols[:, 2:3], T.colb[:, 1:2], ["p2n"], ["p2nf"], 1)
+    ts(T.cols[:, 3:4], pcol, -0.5, 0.5, AL.mult, AL.add, ["pcol"], ["cOg"], 1)
+    ts(T.cols[:, 4:5], pcol, -1.0, 0.5, AL.mult, AL.add, ["pcol"], ["cq"], 1)
+    ts(T.cols[:, 5:6], T.E16[:, 4:5], 1.0, 127.8, AL.mult, AL.add, ["E16"], ["cM0"], 1)
+    ts(T.cols[:, 6:7], T.E16[:, 9:10], -128.0, T.E16[:, 8:9], AL.mult, AL.add, ["E16"], ["cF"], 1)
+    flip = [0]
+
+    def scaled(name, base, v, rd=()):
+        if name not in ("B2", "n1024", "nI"):
+            act(wm(name), wm(base), AF.Identity, ["W" + base] + list(rd), ["W" + name], 128, scale=v)
+        else:
+            ts(wm(name), wm(base), v, None, AL.mult, None, ["W" + base] + list(rd), ["W" + name], 64)
+
+    for nm, v in (("nI", -1.0), ("hI", 0.5), ("nhI", -0.5), ("n1024", -1024.0), ("I16", 16.0), ("I2", 2.0), ("I256", 256.0),
+                  ("I512", 512.0), ("n512", -512.0), ("n20", -20.0), ("I448", 448.0), ("sI", SCL), ("nsI", -SCL), ("nqI", -0.25)):
+        scaled(nm, "I", v)
+    scaled("cqI", "I", T.cols[:, 4:5], ["cq"])
+    for nm, v in (("B2", 2.0), ("B4096", 4096.0), ("nB", -1.0), ("nqB", -0.25)):
+        scaled(nm, "B", v)
+    scaled("pB", "B", pcol, ["pcol"])
+    scaled("pwB", "B", T.cols[:, 2:3], ["p2nf"])
+    ts(wm("nCB"), wm("B"), T.cols[:, 1:2], -1.0, AL.mult, AL.mult, ["WB", "p2f"], ["WnCB"], 64)
+    tt(wm("IL"), wm("I"), wm("L"), AL.subtract, ["WI", "WL"], ["WIL"], 128)
+    scaled("hIL", "IL", 0.5)
+    scaled("I24", "I", 24.0)
+    tt(wm("S24"), wm("I24"), wm("B"), AL.subtract, ["WI24", "WB"], ["WS24"], 128)
+    G8 = T.Wm[:, slot["B"], :, 0]
+    ms(T.Z[:], 0.0, ["Z0", "Z1", "Z2"], 216)
+    cp(T.Z[:, 0, 15:128:16], G8, ["WB", "Z0"], ["Z0"], 8)
+    ts(T.Z[:, 1, 15:128:16], G8, -1.0, None, AL.mult, None, ["WB", "Z1"], ["Z1"], 8)
+    ts(T.Z[:, 2, 15:128:16], G8, T.cols[:, 1:2], None, AL.mult, None, ["WB", "Z2", "p2f"], ["Z2"], 8)
+
+    def Zs(which, r):
+        return (T.Z[:, which, 15 - r:143 - r], "Z%d" % which)
+
+    def colmat(name, ents):
+        act(wm(name), T.zer[:], AF.Identity, ["zer"], ["W" + name], 128)
+        for r, v in ents:
+            act(T.Wm[:, slot[name], :, r], G8, AF.Identity, ["WB", "pcol", "W" + name], ["W" + name], 8, scale=pcol if v is None else v)
+
+    colmat("M0a", [(0, 2.0), (1, 1.0)])
+    colmat("M0b", [(2, 2.0)])
+    colmat("Fd", [(1, 1.0), (6, None), (11, 1.0), (12, 1.0)])
+    colmat("Fg", [(0, 1.0), (6, None), (11, 1.0)])
+    colmat("Ff", [(6, None), (11, 1.0), (12, 1.0)])
+    scaled("Fn2", "I", T.E16[:, 10:11], ["E16"])
+
+    def entmat(name, ents, src=None):
+        wm(name)
+        k = slot[name]
+        for q, (r0, a, b, v) in enumerate(ents):
+            if q == 0 and (a, b) == (0, 16):
+                i_ap, rd = (T.zer[:], ["zer"]) if src is None else (wm(src), ["W" + src])
+            else:
+                if q == 0:
+                    act(wm(name), T.zer[:], AF.Identity, ["zer"], ["W" + name], 128)
+                i_ap, rd = T.Wm[:, k, :, a:b], ["W" + name]
+            po(lambda k=k, a=a, b=b, i_ap=i_ap, v=v, r0=r0: g.affine_select(T.Wm[:, k, :, a:b], i_ap, [[-16, 8], [0, b - a]], AL.not_equal, float(v), -r0, 1),
+               rd, ["W" + name], 8 * (b - a))
+
+    entmat("d", [(1, 0, 16, 256)])
+    entmat("e", [(0, 0, 16, 128), (2, 0, 16, 1)])
+    entmat("eA", [(3, 0, 16, 1)], src="e")
+    po(lambda: g.iota(wm("y0"), [[0, 8], [-1, 16]], -14, 0, allow_small_or_imprecise_dtypes=True), [], ["Wy0"], 128)
+    po(lambda: g.affine_select(wm("y1"), wm("y0"), [[-16, 8], [0, 16]], AL.is_equal, 0.0, -5, 1), ["Wy0"], ["Wy1"], 128)
+    entmat("y", [(0, 0, 16, 640), (2, 0, 16, 5), (3, 0, 16, 1), (6, 0, 16, 3.0 / 256)], src="y1")
+    entmat("Fm", [(4, 9, 10, 1)])
+    entmat("keep", [(8, 0, 16, 1), (12, 0, 16, -1)])
+    entmat("mM", [(8, 0, 4, 1), (11, 0, 3, -1)])
+    entmat("M", [(6, 0, 1, 2), (6, 1, 2, 1), (1, 2, 3, 256), (11, 0, 2, 256), (11, 2, 3, 255), (12, 3, 5, 2), (8, 4, 16, 256)])
+    entmat("K", [(12, 0, 16, -129)])
+    entmat("s0", [(9, 0, 16, 256), (12, 0, 16, 2048), (0, 0, 16, 1)])
+    entmat("s1", [(3, 0, 16, 255), (12, 0, 16, 2048), (0, 0, 16, -1)])
+
+    ms(T.sta[:, 0:8, 768:784], 200.0, ["S"], 64)
+    ms(T.sta[:, 8:10, 768:784], -129.0, ["SL"], 16)
+    ms(T.sta[:, 0:4, 513:768:2], 0.0, ["zq%d" % q for q in range(4)], 256)
+    phase[0] = "late"
+    gate.append(last_w["WM"])
+    entmat("s1L", [(3, 0, 16, 255), (12, 0, 16, 4096), (0, 0, 16, 6144), (9, 0, 16, 2048), (10, 0, 16, -2048)])
+    entmat("a", [(3, 0, 16, 1)])
+    scaled("nB2k", "B", -2048.0)
+    phase[0] = "set"
+    ms(T.sta[:, 0:2, 256:512], 200.0, ["P0", "P1"], 256)
+
+    cp(T.e0u[:], T.e0i[:], ["e0i"], ["e0u"], 16)
+    ts(T.e0p[:, 0:16], T.e0i[:], 7, None, AL.arith_shift_right, None, ["e0i"], ["e0p0"], 16)
+    ts(T.e0p[:, 16:32], T.e0i[:], 127, None, AL.bitwise_and, None, ["e0i"], ["e0p1"], 16)
+    tt(T.X0[:], T.e0p[:, 0:32].indirect(T.ofu[:, 0:32]), T.dm[:], AL.mult, ["e0p0", "e0p1", "ofu", "dm0", "dm1"], ["X0"], 800)
+    pe([(T.ps0[:, 0:256], wm("M0a"), T.X0[:, 0:256], 256, "WM0a"), (T.ps0[:, 0:256], wm("M0b"), T.X0[:, 256:512], 256, "WM0b")], ["X0"], ["ps0"])
+    pe([(T.ps1[:, 0:256], wm("B"), T.X0[:, 0:256], 256, "WB")], ["X0"], ["ps1"])
+    pe([(T.ps2[:, 0:256], wm("B2"), T.X0[:, 256:512], 256, "WB2")], ["X0"], ["ps2"])
+    ts(T.O0[:, 0], T.ps1[:, 0:256], pcol, None, AL.is_equal, None, ["ps1", "pcol"], ["O0"], 256)
+    act(T.O0[:, 1], T.ps2[:, 0:256], AF.Identity, ["ps2"], ["O1"], 256, bias=1.0)
+    tt(T.O0[:, 0], T.O0[:, 0], T.O0[:, 1], AL.mult, ["O0", "O1"], ["O0"], 512)
+    for ch in range(2):
+        act(T.sta[:, ch, 1:256:2], T.ps0[:, ch * W:ch * W + W], AF.Identity, ["ps0", "cM0"], ["M%d" % ch], W, bias=T.cols[:, 5:6], scale=0.5)
+        ts(T.sta[:, ch, 0:256:2], T.O0[:, 0, ch * W:ch * W + W], -129.0, None, AL.add, None, ["O0"], ["K%d" % ch], 64)
+    for q in range(4):
+        cp(T.ivf[:, q * 512:q * 512 + 512], T.ivi[:, q * 512:q * 512 + 512], ["ivi"], ["ivf%d" % q], 512)
+    IVF = ["ivf%d" % q for q in range(4)]
+
+    rank = T.rank_of(core)
+    cores = list(T.cores)
+    NR = len(cores)
+    tile = [0]
+
+    def masks(src, ch):
+        ds = [(b, cores[(src + b) % NR]) for b in range(4 * ch, 4 * ch + 4) if b % NR]
+        en = {b: topo.engines(cores[src], d) for b, d in ds}
+        few = min(len(v) for v in en.values())
+        far = [b for b, d in ds if len(en[b]) == few]
+        res = {}
+        pool = list(en[far[0]])
+        left = len(far)
+        for b in reversed(far):
+            n = 1
+            while 2 * n * left <= len(pool):
+                n *= 2
+            res[b] = pool[:n]
+            pool = pool[n:]
+            left -= 1
+        near = [b for b, d in ds if b not in far]
+        for b in near:
+            used = [e for v in res.values() for e in v]
+            free = [e for e in en[b] if e not in used and e not in en[far[0]]]
+            n = 1
+            while 2 * n * len(near) <= len(free):
+                n *= 2
+            res[b] = free[:n]
+        return res
+
+    def views(s, ch):
+        n = 2 * s + ch
+        c = str(ch)
+        a = T["ps%d" % (5 + ch)]
+        an = "ps%d" % (5 + ch)
+        v = {"n": n, "c": c, "a": [a[:, q * W:q * W + W] for q in range(4)], "an": [an + "r%d" % q for q in range(4)], "abuf": a,
+             "w": T.ps7[:, ch * 256:ch * 256 + 256], "wn": "ps7" + c, "w0": ch * 256}
+        return v
+
+    def sfv(ch, q):
+        return T.sf[:, ch, q]
+
+    def sbv(ch, q):
+        return T.sb[:, ch, q]
+
+    def scan(ch, src, n, rd):
+        dv(lambda: g.vector.tensor_tensor_scan(T.scn[:, ch, 0:n], T.seg[:, 0:n], src, 0.0, AL.mult, AL.max), list(rd) + ["seg"], ["scn%d" % ch], n)
+
+    def scan2(ch, src, n, rd, u):
+        dv(lambda: g.vector.tensor_tensor_scan(T.sc2[:, ch, u, 0:n], T.seg[:, 0:n], src, 0.0, AL.mult, AL.max), list(rd) + ["seg"], ["sc%d%d" % (u, ch)], n)
+
+    def prep(s, ch):
+        v = views(s, ch)
+        n, c, a, an = v["n"], v["c"], v["a"], v["an"]
+        N = str(n)
+        K, M, P0, P1 = T.sta[:, n, 0:256:2], T.sta[:, n, 1:256:2], T.sta[:, n, 256:512:2], T.sta[:, n, 257:512:2]
+        w0 = v["w0"]
+        wa, wb = T.ps7[:, w0:w0 + W], T.ps7[:, w0 + W:w0 + 256]
+        dc = T.dcon[:, ch * W:ch * W + W]
+        if s == 0:
+            pe([(wa, wm("d"), M, W, "Wd"), (wa, wm("I"), dc, W, "WI")], ["M" + N, "dcon"], [v["wn"]])
+            scan(ch, wa, W, [v["wn"]])
+            ts(T.lu[:, ch, 8:16], T.scn[:, ch, 15:128:16], -32768.0, None, AL.add, None, ["scn" + c], ["dl" + c], 8)
+            el, eln = T.e0u[:, 8 * ch:8 * ch + 8], "e0u"
+            cp(T.c16[:, ch], T.ivi[:, 0:2048].indirect(el), ["ivi", eln], ["c16" + c], 200)
+        else:
+            pe([(wa, wm("e"), M, W, "We"), (wa, wm("I"), T.econ[:], W, "WI")], ["M" + N, "econ"], [v["wn"]])
+            pe([(wb, wm("d"), M, W, "Wd"), (wb, wm("I"), dc, W, "WI")], ["M" + N, "dcon"], [v["wn"]])
+            scan(ch, v["w"], 256, [v["wn"]])
+            ts(T.lu[:, ch, 0:8], T.scn[:, ch, 15:128:16], -16512.0, None, AL.add, None, ["scn" + c], ["el" + c], 8)
+            ts(T.lu[:, ch, 8:16], T.scn[:, ch, 143:256:16], -32768.0, None, AL.add, None, ["scn" + c], ["dl" + c], 8)
+            el, eln = T.lu[:, ch, 0:8], "el" + c
+            cp(T.c16[:, ch], T.ivf[:, 0:2048].indirect(el), IVF + [eln], ["c16" + c], 200)
+        dl = T.lu[:, ch, 8:16]
+        for q in range(4):
+            src = T.stb[:, 0:4096].indirect(T.c16[:, ch, 32 * q:32 * q + 32])
+            if YE[s][4 * ch + q] == "D":
+                ts(T.Y[:, ch, 512 * q:512 * q + 512], src, -128.0, None, AL.add, None, ["stb", "c16" + c], ["Y%d" % q + c], 800)
+            else:
+                act(T.Y[:, ch, 512 * q:512 * q + 512], src, AF.Identity, ["stb", "c16" + c], ["Y%d" % q + c], 800, bias=-128.0)
+        ts(sbv(ch, 0), K, -128.5, None, AL.is_gt, None, ["K" + N], ["core" + c], 64)
+        if s > 0:
+            ts(sbv(ch, 15), K, -128.5, 1.0 / 128, AL.is_lt, AL.max, ["K" + N], ["thr" + c], 64)
+            pe([(a[0], wm("I448"), sbv(ch, 15), W, "WI448"), (a[1], wm("I448"), sbv(ch, 15), W, "WI448")], ["thr" + c], [an[0], an[1]])
+        if s > 1:
+            pe([(a[2], wm("hI"), P0, W, "WhI"), (a[2], wm("hI"), P1, W, "WhI"), (a[2], wm("n1024"), sbv(ch, 0), W, "Wn1024")], ["P" + N, "core" + c], [an[2]])
+        else:
+            pe([(a[2], wm("I"), P0, W, "WI"), (a[2], wm("n1024"), sbv(ch, 0), W, "Wn1024")], ["P" + N, "core" + c], [an[2]])
+        tt(sbv(ch, 1), a[2], K, AL.max, [an[2], "K" + N], ["mid" + c], W)
+        if s > 1:
+            pe([(a[3], wm("hI"), P0, W, "WhI"), (a[3], wm("nhI"), P1, W, "WnhI")], ["P" + N], [an[3]])
+            act(sbv(ch, 2), a[3], AF.Abs, [an[3]], ["h" + c], W)
+            pe([(a[3], wm("B"), sbv(ch, 2), W, "WB")], ["h" + c], [an[3]])
+            act(sbv(ch, 3), a[3], AF.Sign, [an[3]], ["n2" + c], W)
+            pe([(a[2], wm("hI"), P0, W, "WhI"), (a[2], wm("hI"), P1, W, "WhI"), (a[2], wm("nI"), sbv(ch, 2), W, "WnI")], ["P" + N, "h" + c], [an[2]])
+        act(sfv(ch, 0), T.ivf[:, 0:2048].indirect(el), AF.Identity, IVF + [eln], ["c37" + c], 200, scale=37.0, bias=-16640.0)
+        act(sfv(ch, 1), T.ivf[:, 0:2048].indirect(dl), AF.Identity, IVF + ["dl" + c], ["old" + c], 200)
+        pe([(wa, wm("eA"), M, W, "WeA"), (wb, wm("y"), M, W, "Wy")], ["M" + N], [v["wn"]])
+        tt(T.si[:, ch, 0], wa, sfv(ch, 0), AL.add, [v["wn"], "c37" + c], ["x" + c], W)
+        ts(T.si[:, ch, 1], T.si[:, ch, 0], 4095, None, AL.bitwise_and, None, ["x" + c], ["val" + c], W)
+        tt(sfv(ch, 2), T.ivf[:, 0:2048].indirect(dl), T.si[:, ch, 1], AL.subtract, IVF + ["dl" + c, "val" + c], ["diff" + c], 200)
+        ts(sbv(ch, 4), wb, C11, -C11, AL.add, AL.add, [v["wn"]], ["ry" + c], W)
+
+    def big(s, ch):
+        v = views(s, ch)
+        c, an = v["c"], v["an"]
+        Yn = ["Y%d" % q + c for q in range(4)]
+        for t in range(4):
+            b = tile[0] % 3
+            tile[0] += 1
+            ps, pn = T["ps%d" % b], "ps%d" % b
+            it = []
+            for kk in range(4):
+                o = ps[:, kk * W:kk * W + W]
+                it.append((o, wm("I"), T.Y[:, ch, 4 * t + kk:2048:16], W, "WI"))
+                it.append((o, wm("nI"), sbv(ch, 1), W, "WnI"))
+            pe(it, Yn + ["mid" + c], [pn])
+            m = T.mm[:, b]
+            if s == 0:
+                ts(m, ps[:], C8, C8, AL.add, AL.is_equal, [pn], ["mm%d" % b], 512)
+            else:
+                act(T.ab[:, b], ps[:], AF.Abs, [pn], ["ab%d" % b], 512)
+                for q in range(2):
+                    tt(T.mis[:, b, 256 * q:256 * q + 256], v["abuf"][:, 0:256], T.ab[:, b, 256 * q:256 * q + 256], AL.is_lt,
+                       [an[0], an[1], "ab%d" % b], ["mis%d%d" % (b, q)], 256)
+                it = [(ps[:], wm("sI"), T.ab[:, b], 512, "WsI")]
+                if s > 1:
+                    it += [(ps[:, kk * W:kk * W + W], wm("nsI"), sbv(ch, 2), W, "WnsI") for kk in range(4)]
+                pe(it, ["ab%d" % b, "h" + c], [pn], final=False)
+                pe([(ps[:], wm("B4096"), T.mis[:, b], 512, "WB4096")], ["mis%d0" % b, "mis%d1" % b], [pn], first=False)
+                ts(m, ps[:], C8, C8, AL.add, AL.is_equal, [pn], ["mm%d" % b], 512)
+            it = [(T.ps3[:, 0:W], wm("nCB"), sbv(ch, 0), W, "WnCB")] if t == 0 else []
+            it += [(T.ps3[:, 0:W], Zs(2, 4 * t + kk)[0], T.mm[:, b, kk * W:kk * W + W], W, "Z2") for kk in range(4)]
+            pe(it, ["mm%d" % b, "core" + c], ["ps3"], first=t == 0, final=t == 3)
+            if s > 0:
+                it = [(T.ps4[:, 0:W], wm("n20"), sbv(ch, 0), W, "Wn20")] if t == 0 else []
+                it += [(T.ps4[:, 0:W], wm("I"), T.mm[:, b, kk * W:kk * W + W], W, "WI") for kk in range(4)]
+                pe(it, ["mm%d" % b, "core" + c], ["ps4"], first=t == 0, final=t == 3)
+
+    def post(s, ch):
+        v = views(s, ch)
+        n, c, a, an = v["n"], v["c"], v["a"], v["an"]
+        N = str(n)
+        lastst = s == RO - 1
+        M = T.sta[:, n, 1:256:2]
+        z, f, Og, Oq = T.sta[:, n, 512:768:2], T.sta[:, n, 513:768:2], sbv(ch, 16), sbv(ch, 17)
+        okk, sel, oj, bit, wx, sg, g2, Od, F = (sbv(ch, q) for q in range(5, 14))
+        R = T.ps3[:, 0:W]
+        w0, wn = v["w0"], v["wn"]
+        ts(okk, R, 0.0, None, AL.is_equal, None, ["ps3"], ["ok" + c], W)
+        pe([(a[3], wm("IL"), okk, W, "WIL")], ["ok" + c], [an[3]])
+        act(sel, a[3], AF.Relu, [an[3]], ["sel" + c], W)
+        tt(sfv(ch, 3), sfv(ch, 2), sel, AL.mult, ["diff" + c, "sel" + c], ["ds" + c], 2 * W)
+        extra = ["yiA"] if lastst and ch == 1 else []
+        tt(T.ivf[:, 0:2048].indirect(T.lu[:, ch, 8:16]), sfv(ch, 1), sfv(ch, 3), AL.subtract, ["old" + c, "ds" + c, "dl" + c] + extra, IVF, 4 * W)
+        if lastst:
+            for b in range(8):
+                lo = 256 * b + W * ch
+                op("S", lambda lo=lo: g.sync.dma_start(T.yi[:, lo:lo + W], T.ivf[:, lo:lo + W]), IVF, ["yiA"] if (ch == 0 and b == 7) else [], 0.1,
+                   sem=("outA" if ch == 0 else "out", 16), lat=2.5)
+        zg = sbv(ch, 14)
+        wa, wb = T.ps7[:, w0:w0 + W], T.ps7[:, w0 + W:w0 + 256]
+        pe([(wa, wm("pB"), sel, W, "WpB"), (wa, wm("I16"), T.dcon[:, 0:W], W, "WI16")], ["sel" + c, "dcon"], [wn])
+        scan2(ch, wa, W, [wn], 1)
+        cp(T.lu[:, ch, 16:24], T.sc2[:, ch, 1, 15:128:16], ["sc1" + c], ["jl" + c], 8)
+        act(z, T.Y[:, ch, 0:2048].indirect(T.lu[:, ch, 16:24]), AF.Identity, ["Y%d" % q + c for q in range(4)] + ["jl" + c], ["z" + N], 200)
+        if s > 1:
+            tt(f, a[2], z, AL.min, [an[2], "z" + N], ["zq" + N], W)
+            pe([(wb, wm("B"), f, W, "WB"), (wb, wm("nqB"), sel, W, "WnqB"), (wb, wm("nqI"), sbv(ch, 3), W, "WnqI"), (wb, wm("cqI"), T.ones[:], W, "WcqI")],
+               ["zq" + N, "sel" + c, "n2" + c, "ones"], [wn])
+            ts(sfv(ch, 6), wb, C16, -C16, AL.add, AL.add, [wn], ["rq" + c], W)
+            tt(Oq, wb, sfv(ch, 6), AL.is_equal, [wn, "rq" + c], ["oq" + N], W)
+            pe([(a[2], wm("I"), f, W, "WI"), (a[2], wm("I512"), Oq, W, "WI512")], ["zq" + N, "oq" + N], [an[2]])
+            act(T.sw[:, ch, 0, W:256], a[2], AF.Relu, [an[2]], ["tf" + c], W, bias=-383.0)
+        if s > 0:
+            act(sfv(ch, 4), R, AF.Relu, ["ps3"], ["Rc" + c], W, bias=0.5)
+            act(wx, T.ps4[:, 0:W], AF.Exp, ["ps4"], ["wx" + c], W, scale=math.log(32.0))
+            pe([(a[0], wm("S24"), wx, W, "WS24")], ["wx" + c], [an[0]])
+            act(sg, a[0], AF.Sign, [an[0]], ["sg" + c], W, bias=-24.0)
+            pe([(a[1], wm("hIL"), sg, W, "WhIL"), (a[1], wm("nB"), okk, W, "WnB")], ["sg" + c, "ok" + c], [an[1]])
+            act(Og, a[1], AF.Relu, [an[1], "cOg"], ["og" + N], W, bias=T.cols[:, 3:4])
+            pe([(a[0], wm("pwB"), Og, W, "WpwB")], ["og" + N], [an[0]])
+            tt(sfv(ch, 5), a[0], sfv(ch, 4), AL.mult, [an[0], "Rc" + c], ["u" + c], W)
+            ts(a[1], sfv(ch, 5), C1, -C1, AL.add, AL.add, ["u" + c], [an[1]], W)
+            tt(bit, a[1], sfv(ch, 5), AL.is_gt, [an[1], "u" + c], ["bit" + c], W)
+            pe([(a[0], wm("IL"), bit, W, "WIL")], ["bit" + c], [an[0]])
+            act(oj, a[0], AF.Relu, [an[0]], ["oj" + c], W)
+            pe([(a[1], wm("pB"), oj, W, "WpB"), (a[1], wm("I16"), T.dcon[:, 0:W], W, "WI16")], ["oj" + c, "dcon"], [an[1]])
+            scan2(ch, a[1], W, [an[1]], 2)
+            cp(T.lu[:, ch, 40:48], T.sc2[:, ch, 2, 15:128:16], ["sc2" + c], ["gl" + c], 8)
+            act(zg, T.Y[:, ch, 0:2048].indirect(T.lu[:, ch, 40:48]), AF.Identity, ["Y%d" % q + c for q in range(4)] + ["gl" + c], ["zg" + c], 200)
+        it = [(a[3], wm("y"), M, W, "Wy"), (a[3], wm("nI"), sbv(ch, 4), W, "WnI"), (a[3], wm("B4096"), sel, W, "WB4096")]
+        if s > 0:
+            it += [(a[3], wm("B4096"), Og, W, "WB4096")]
+        pe(it, ["M" + N, "ry" + c, "sel" + c, "og" + N], [an[3]])
+        act(g2, a[3], AF.Relu, [an[3]], ["g2" + c], W, scale=-2.0, bias=-1792.0)
+        ts(Od, g2, 0.5, None, AL.is_gt, None, ["g2" + c], ["Od" + c], 64)
+        tg, tf = T.sw[:, ch, 0, 0:W], T.sw[:, ch, 0, W:256]
+        cc = T.sw[:, ch, 1]
+        it = [(a[3], wm("Fd"), Od, W, "WFd"), (a[3], Zs(0, 3)[0], sel, W, "Z0"), (a[3], wm("Fm"), M, W, "WFm")]
+        rd = ["Od" + c, "sel" + c, "M" + N]
+        if s > 0:
+            it += [(a[3], wm("Fg"), Og, W, "WFg")]
+            rd += ["og" + N]
+        if s > 1:
+            it += [(a[3], wm("Ff"), Oq, W, "WFf")]
+            rd += ["oq" + N]
+        if lastst:
+            it += [(a[3], wm("Fn2"), sbv(ch, 3), W, "WFn2")]
+            rd += ["n2" + c]
+        pe(it, rd, [an[3]])
+        act(F, a[3], AF.Identity, [an[3], "cF"], ["F" + c], W, bias=T.cols[:, 6:7])
+        we, wo = T.ps7[:, w0:w0 + 256:2], T.ps7[:, w0 + 1:w0 + 256:2]
+        pe([(we, wm("keep"), F, W, "Wkeep"), (wo, wm("mM"), F, W, "WmM")], ["F" + c], [wn])
+        km = T.sw[:, ch, 2]
+        tt(km, v["w"], T.sta[:, n, 0:256], AL.mult, [wn, "K" + N, "M" + N], ["km" + c], 256)
+        if s > 0:
+            pe([(a[0], wm("I512"), Og, W, "WI512"), (a[0], wm("I"), zg, W, "WI")], ["zg" + c, "og" + N], [an[0]])
+            act(tg, a[0], AF.Relu, [an[0]], ["tg" + c], W, bias=-383.0)
+        itm = [(a[2], wm("I2"), T.sw[:, ch, 2, 1:256:2], W, "WI2"), (a[2], wm("M"), F, W, "WM"), (a[2], Zs(1, 2)[0], g2, W, "Z1")]
+        itk = [(a[3], wm("I"), T.sw[:, ch, 2, 0:256:2], W, "WI"), (a[3], wm("I256"), Od, W, "WI256"), (a[3], wm("nI"), g2, W, "WnI"), (a[3], wm("K"), F, W, "WK")]
+        rd = ["km" + c, "Od" + c, "g2" + c, "F" + c]
+        for on, tx, nm in ((s > 1, tf, "tf"), (s > 0, tg, "tg")):
+            if on:
+                itm += [(a[2], Zs(0, 2)[0], tx, W, "Z0")]
+                itk += [(a[3], wm("I"), tx, W, "WI")]
+                rd += [nm + c]
+        pe(itm, rd, [an[2]])
+        act(T.snd[:, n, 1:256:2], a[2], AF.Identity, [an[2]], ["nM" + N], W, scale=0.5, bias=-0.2)
+        pe(itk, rd, [an[3]])
+        c0, c1, crd = Og, Og, "og" + N
+        if s > 1:
+            pe([(v["w"], wm("I"), T.sta[:, n, 256:512], 256, "WI"), (we, wm("n512"), Og, W, "Wn512"), (wo, wm("n512"), Og, W, "Wn512"),
+                (we, wm("nI"), zg, W, "WnI"), (wo, wm("nI"), zg, W, "WnI")], ["P" + N, "zg" + c, "og" + N], [wn])
+            ts(cc, v["w"], C8 + 512.0, C8, AL.add, AL.is_equal, [wn], ["cc" + c], 256)
+            c0, c1, crd = T.sw[:, ch, 1, 0:256:2], T.sw[:, ch, 1, 1:256:2], "cc" + c
+        s1 = "s1L" if lastst else "s1"
+        it = [(v["w"], wm("I"), T.dcon[:], 256, "WI"), (we, wm("s0"), F, W, "Ws0"), (wo, wm(s1), F, W, "W" + s1)]
+        if lastst:
+            it += [(we, wm("nB"), c0, W, "WnB"), (wo, wm("nB2k"), c0, W, "WnB2k"), (wo, wm("nB2k"), c1, W, "WnB2k")]
+        elif s > 0:
+            it += [(we, wm("nB"), c0, W, "WnB"), (wo, wm("B"), c1, W, "WB")]
+        pe(it, ["F" + c, "dcon", crd], [wn])
+        scan2(ch, v["w"], 256, [wn], 3)
+        ts(T.lu[:, ch, 24:40], T.sc2[:, ch, 3, 15:256:16], 512.0, None, AL.min, None, ["sc3" + c], ["pl" + c], 16)
+        win = T.sta[:, n, 256:784].indirect(T.lu[:, ch, 24:40])
+        wrd = ["P" + N, "z" + N, "zq" + N, "S", "SL", "pl" + c]
+        if not lastst:
+            act(T.snd[:, n, 0:256:2], a[3], AF.Identity, [an[3]], ["nK" + N], W)
+            act(T.snd[:, n, 256:512], win, AF.Identity, wrd, ["nP" + N], 400)
+            mk = masks(rank, ch)
+            n2 = n + 2
+            got = sum(len(masks((rank - b) % NR, ch)[b]) for b in mk)
+            sent = sum(len(x) for x in mk.values())
+            for base, sm, rd, nxt in ((0, "ar%d" % n2, ["nK" + N, "nM" + N], ["K%d" % n2, "M%d" % n2]), (256, "ap%d" % n2, ["nP" + N], ["P%d" % n2])):
+                def go(mk=mk, n=n, n2=n2, ch=ch, base=base, sm=sm):
+                    trs = []
+                    for b in sorted(mk):
+                        rid, pid, _ = topo.addr(cores[(rank + b) % NR])
+                        lo = base + 64 * (b - 4 * ch)
+                        trs.append(RemoteDMATransfer(dst_ids=[DstId(rid=rid, pnc=pid)], dma_engine_mask=sum(1 << e for e in mk[b]), remote_sem=T.sem[sm],
+                                                     src=T.snd[:, n, lo:lo + 64], dst=T.sta[:, n2, lo:lo + 64]))
+                    g.remote_dma_fused(trs, local_sem=T.sem.loc)
+                    return None
+                if ch == 0:
+                    op("S", lambda n=n, n2=n2, base=base: g.sync.dma_start(T.sta[:, n2, base:base + 64], T.snd[:, n, base:base + 64]), rd, [], 0.1,
+                       sem=(sm, 16), lat=2.0)
+                op("G", go, rd, nxt, 1.0, sem=(sm, got, sent), lat=3.2)
+        else:
+            lo = ch * W
+            act(T.oy[:, ch], win, AF.Identity, wrd, ["oy" + c], 400, bias=128.0)
+            for q in range(2):
+                cp(T.oyy[:, q, lo:lo + W], T.oy[:, ch, q:256:2], ["oy" + c], ["oyy%d" % q + c], 64)
+            act(T.ok_[:, lo:lo + W], a[3], AF.Identity, [an[3]], ["oK" + c], W, bias=128.0)
+            nM = T.snd[:, n, 1:256:2]
+            wa, wb = T.ps7[:, w0:w0 + W], T.ps7[:, w0 + W:w0 + 256]
+            pe([(wa, wm("e"), nM, W, "We"), (wa, wm("I"), T.econ[:], W, "WI")], ["nM" + N, "econ"], [wn])
+            pe([(wb, wm("a"), nM, W, "Wa"), (wb, wm("I"), T.econ[:], W, "WI")], ["nM" + N, "econ"], [wn])
+            scan(ch, v["w"], 256, [wn])
+            ts(T.oe[:, 0, 8 * ch:8 * ch + 8], T.scn[:, ch, 15:128:16], -16512.0, None, AL.add, None, ["scn" + c], ["oe" + c], 8)
+            ts(T.oe[:, 1, 8 * ch:8 * ch + 8], T.scn[:, ch, 143:256:16], -128.0, None, AL.add, None, ["scn" + c], ["oa" + c], 8)
+            if ch == 1:
+                for eng, q, dst, src, rd in (("A", g.scalar, T.yk, T.ok_[:], "oK"), ("S", g.sync, T.y0, T.oyy[:, 0], "oyy0"), ("A", g.scalar, T.y1, T.oyy[:, 1], "oyy1"),
+                                             ("S", g.sync, T.ye, T.oe[:, 0], "oe"), ("A", g.scalar, T.ya, T.oe[:, 1], "oa")):
+                    op(eng, lambda q=q, dst=dst, src=src: q.dma_start(dst[:], src), [rd + "0", rd + "1"], [], 0.1, sem=("out", 16), lat=2.0)
+
+    for s in range(RO):
+        for nm, fn, ch in (("p", prep, 0), ("p", prep, 1), ("b", big, 0), ("q", post, 0), ("b", big, 1), ("q", post, 1)):
+            phase[0] = nm + str(ch)
+            fn(s, ch)
+    assert len(slot) <= NW
+    return ops
+
+
+def schedule(ops):
+    n = len(ops)
+    succ = [[] for _ in range(n)]
+    for i, o in enumerate(ops):
+        for d in o["deps"]:
+            succ[d].append(i)
+    HOP = 0.12
+    pr = [0.0] * n
+    for i in range(n - 1, -1, -1):
+        pr[i] = ops[i]["dur"] + ops[i]["lat"] + max([pr[j] + HOP for j in succ[i]], default=0.0)
+    x, look, amp, bonus = SEED
+    for i in range(n):
+        x = (x * 1103515245 + 12345) % 2147483648
+        pr[i] += amp * x / 2147483648 + bonus.get(ops[i]["ph"], 0.0)
+    pred = [list(o["deps"]) for o in ops]
+
+    def run(before, after, prio, back):
+        left = [len(p) for p in before]
+        base = [0.0] * n
+        ready = [i for i in range(n) if left[i] == 0]
+        for i in ready:
+            base[i] = ops[i]["lat"] if back else 0.0
+        free = {}
+        done = [0.0] * n
+        bank = {}
+        order = []
+        extra = []
+        while ready:
+            st = {}
+            for i in ready:
+                o = ops[i]
+                t = max(base[i], free.get(o["eng"], 0.0))
+                for b in o["banks"]:
+                    for e, j in bank.get(b, {}).items():
+                        if e != o["eng"] and done[j] + HOP > t:
+                            t = done[j] + HOP
+                st[i] = t
+            t0 = min(st.values()) + look
+            i = max([q for q in ready if st[q] <= t0], key=lambda q: (prio[q], -q))
+            o = ops[i]
+            for b in o["banks"]:
+                extra.extend((i, j) for e, j in bank.get(b, {}).items() if e != o["eng"])
+                bank.setdefault(b, {})[o["eng"]] = i
+            free[o["eng"]] = st[i] + o["dur"]
+            done[i] = st[i] + o["dur"] + (0.0 if back else o["lat"])
+            order.append(i)
+            ready.remove(i)
+            for j in after[i]:
+                t = done[i] + (0.0 if (o["eng"] == "P" and ops[j]["eng"] == "P") else HOP) + (ops[j]["lat"] if back else 0.0)
+                if t > base[j]:
+                    base[j] = t
+                left[j] -= 1
+                if left[j] == 0:
+                    ready.append(j)
+        return order, done, extra
+    best = None
+    for rnd in range(ROUNDS[0] + 1):
+        order, done, extra = run(pred, succ, pr, False)
+        if best is None or max(done) < max(best[1]):
+            best = (order, done, extra)
+        if rnd < ROUNDS[0]:
+            pr = run(succ, pred, done, True)[1]
+    order, done, extra = best
+    for i, j in extra:
+        ops[i]["deps"].add(j)
+    for i in range(n):
+        ops[i]["t"] = done[i] - ops[i]["dur"] - ops[i]["lat"]
+    return order, max(done)
+
+
+def emit(g, T, ops, order):
+    qs = {"P": g.tensor, "D": g.vector, "A": g.scalar, "G": g, "S": g.sync}
+    total = {}
+    for o in ops:
+        if o["sem"]:
+            total[o["sem"][0]] = total.get(o["sem"][0], 0) + o["sem"][1]
+    pos = {i: k for k, i in enumerate(order)}
+    need = set()
+    seen = {}
+    plan = {}
+    for i in order:
+        o = ops[i]
+        best = {}
+        w = []
+        for d in o["deps"]:
+            p = ops[d]
+            if p["sem"]:
+                key = (o["eng"], p["sem"][0])
+                if key not in seen:
+                    seen[key] = 1
+                    w.append(("sem", p["sem"][0]))
+            elif not (o["eng"] == "P" and p["eng"] == "P"):
+                if pos[d] > best.get(p["eng"], (-1, 0))[0]:
+                    best[p["eng"]] = (pos[d], d)
+        for e, (k, d) in best.items():
+            key = (o["eng"], "q" + e)
+            if k > seen.get(key, -1):
+                seen[key] = k
+                need.add(d)
+                w.append(("op", d))
+        plan[i] = w
+    cnt = {}
+    val = {}
+    for i in order:
+        if i in need:
+            e = ops[i]["eng"]
+            cnt[e] = cnt.get(e, 0) + 1
+            val[i] = cnt[e]
+    sent = 0
+    for i in order:
+        o = ops[i]
+        q = qs[o["eng"]]
+        for kind, x in plan[i]:
+            if kind == "sem":
+                q.wait_ge(T.sem[x], total[x])
+            else:
+                q.wait_ge(T.sem["s" + ops[x]["eng"]], val[x])
+        r = o["fn"]()
+        if o["sem"]:
+            if r is not None:
+                r.then_inc(T.sem[o["sem"][0]], 16)
+            else:
+                sent += o["sem"][2]
+        elif i in need:
+            r.then_inc(T.sem["s" + o["eng"]], 1)
+    g.wait_ge(T.sem.loc, sent)
+    for e, c in cnt.items():
+        g.wait_ge(T.sem["s" + e], c)
+    for x in ("outA", "out"):
+        g.wait_ge(T.sem[x], total[x])
+
+
+def rank_program(g, core, T, topo):
+    if T.rank_of(core) is None:
+        return
+    ops = build(g, core, T, topo)
+    order, _ = schedule(ops)
+    emit(g, T, ops, order)

@@ -5,43 +5,63 @@ from concourse.mybir import dt, AluOpType, AxisListType, ActivationFunctionType
 AL = AluOpType
 AF = ActivationFunctionType
 RO = 5
-W = 128
-NW = 60
-YE = ['ADAAAAAA', 'ADADAAAA', 'ADADAAAA', 'ADAAAAAD', 'ADADADAA']
-SEED = [6559, 0.1, 0.0, {'q1': -2.8, 'b1': -7.3, 'p1': 1.0, 'set': 2.9, 'q0': -1.1, 'p0': 0.5, 'b0': -0.3}]
-ROUNDS = [4]
+NCH = 2
+W = 256 // NCH
+MU = W // 16
+NB = 8 // NCH
+WS = 64 + 6 * W
+NW = 36
+NT = 11
+YE = ['ADAAADAA', 'ADDAADAA', 'ADAAADAA', 'ADAAADAA', 'DADAAADA']
+SEED = [5158, 0.2, {'p0': 9.6, 'p1': 1.4, 'b0': 9.8, 'b1': -0.1, 'q0': 9.3, 'q1': 4.6, 'set': 11.9}]
+ROUNDS = [4, 3000]
+KEPT = []
 SCL = 1.25
 C8 = 100663304.0
 C1 = 12582912.0
 C16 = 201326592.0
-C11 = 25769803776.0
+KN = -2.0 ** 60
+AB = 32768.0
+ZN = -2.0 ** 23
+PB = 8192.0
+ALF = 2.0 ** -10
+CO = 1432.0
+TAU = 187.0
+LB = math.log(1.8)
+NTB = 4 if NCH == 2 else 3
 
 SCRATCH = {
     "stb": ("sbuf", [128, 4096], "bfloat16"), "ivi": ("sbuf", [128, 2048], "int32"), "ivf": ("sbuf", [128, 2048], "float32"),
-    "e0i": ("sbuf", [128, 16], "int32"), "e0p": ("sbuf", [128, 32], "int32"), "e0u": ("sbuf", [128, 16], "uint16"),
-    "sta": ("sbuf", [128, 10, 784], "bfloat16"), "snd": ("sbuf", [128, 10, 512], "bfloat16"),
-    "Wm": ("sbuf", [128, NW, 8, 16], "bfloat16"), "Z": ("sbuf", [128, 3, 144], "bfloat16"),
-    "ones": ("sbuf", [128, 128], "bfloat16"), "zer": ("sbuf", [128, 8, 16], "bfloat16"),
-    "cols": ("sbuf", [128, 16], "float32"), "colb": ("sbuf", [128, 8], "bfloat16"), "coli": ("sbuf", [128, 8], "int32"),
-    "E16": ("sbuf", [128, 16], "float32"),
-    "it1": ("sbuf", [128, 256], "float32"), "it2": ("sbuf", [128, 256], "float32"), "dm": ("sbuf", [128, 512], "bfloat16"),
-    "dcon": ("sbuf", [128, 256], "bfloat16"), "econ": ("sbuf", [128, 128], "bfloat16"), "seg": ("sbuf", [128, 256], "float32"),
-    "ofi": ("sbuf", [128, 32], "int32"), "ofu": ("sbuf", [128, 32], "uint16"), "X0": ("sbuf", [128, 512], "bfloat16"),
-    "O0": ("sbuf", [128, 2, 256], "bfloat16"),
-    "Y": ("sbuf", [128, 2, 2048], "bfloat16"), "mis": ("sbuf", [128, 3, 512], "bfloat16"), "mm": ("sbuf", [128, 3, 512], "bfloat16"),
-    "ab": ("sbuf", [128, 3, 512], "bfloat16"), "thr": ("sbuf", [128, 2, 512], "bfloat16"),
-    "c16": ("sbuf", [128, 2, 128], "uint16"), "lu": ("sbuf", [128, 2, 48], "uint16"),
-    "sf": ("sbuf", [128, 2, 12, 128], "float32"), "si": ("sbuf", [128, 2, 2, 128], "int32"),
-    "sb": ("sbuf", [128, 2, 18, 128], "bfloat16"), "sw": ("sbuf", [128, 2, 3, 256], "bfloat16"),
-    "scn": ("sbuf", [128, 2, 256], "float32"), "sc2": ("sbuf", [128, 2, 4, 256], "float32"),
-    "ok_": ("sbuf", [128, 256], "bfloat16"), "oy": ("sbuf", [128, 2, 256], "bfloat16"), "oyy": ("sbuf", [128, 2, 256], "bfloat16"),
-    "oe": ("sbuf", [128, 2, 16], "float32"),
+    "e0i": ("sbuf", [128, 16], "int32"), "e0u": ("sbuf", [128, 16], "uint16"),
+    "sta": ("sbuf", [128, 5 * NCH, MU, 4, 16], "bfloat16"), "snd": ("sbuf", [128, 4 * NCH, 4 * W], "bfloat16"),
+    "win": ("sbuf", [128, NCH // 2, 2 * WS + 4096], "bfloat16"),
+    "eL": ("sbuf", [128, 5 * NCH, 2 * MU], "uint16"), "eS": ("sbuf", [128, 4 * NCH, 2 * MU], "uint16"),
+    "Wm": ("sbuf", [128, NW, 8, 16], "bfloat16"), "Tm": ("sbuf", [128, NT, 2, 4, 32], "bfloat16"), "BP": ("sbuf", [128, 2, 4, 16], "bfloat16"),
+    "Z": ("sbuf", [128, 144], "bfloat16"), "I37": ("sbuf", [128, 2, 128], "float32"), "nI16": ("sbuf", [128, 128], "float16"),
+    "ones": ("sbuf", [128, 128], "bfloat16"), "cols": ("sbuf", [128, 40], "float32"), "colb": ("sbuf", [128, 8], "bfloat16"), "coli": ("sbuf", [128, 8], "int32"),
+    "E16": ("sbuf", [128, 16], "float32"), "NK": ("sbuf", [128, 16], "float32"),
+    "itr": ("sbuf", [128, 256], "bfloat16"), "itl": ("sbuf", [128, 256], "bfloat16"), "itm": ("sbuf", [128, W], "bfloat16"),
+    "TM": ("sbuf", [128, 2112], "bfloat16"), "M": ("sbuf", [128, NCH, 2 * W], "bfloat16"), "OHb": ("sbuf", [128, 16 * W + 16], "bfloat16"),
+    "lanec": ("sbuf", [128, W], "bfloat16"), "pat": ("sbuf", [128, W], "float32"), "seg": ("sbuf", [128, 2 * W], "bfloat16"),
+    "Y": ("sbuf", [128, NCH, 16 * W + 16], "bfloat16"), "tm": ("sbuf", [128, NCH, W, 16], "bfloat16"),
+    "mis": ("sbuf", [128, NTB, 64, 8], "bfloat16"), "ab": ("sbuf", [128, NTB, 64, 8], "bfloat16"), "mh": ("sbuf", [128, NCH, 2, W], "float16"),
+    "c16": ("sbuf", [128, NCH, W], "uint16"), "lu": ("sbuf", [128, NCH, 8, MU], "uint16"), "la": ("sbuf", [128, NCH, 4 * MU], "uint16"),
+    "nb": ("sbuf", [128, NCH, 2, W], "bfloat16"), "sj": ("sbuf", [128, NCH, 2, W], "float32"),
+    "tT": ("sbuf", [128, NCH, 2, MU, 32], "float32"), "tF": ("sbuf", [128, NCH, 2 * W], "float32"), "sF": ("sbuf", [128, NCH, 2 * W], "float32"),
+    "sf": ("sbuf", [128, NCH, 6, W], "float32"), "sb": ("sbuf", [128, NCH, 13, W], "bfloat16"), "cc": ("sbuf", [128, NCH, MU, 2, 16], "bfloat16"),
+    "ok_": ("sbuf", [128, 256], "bfloat16"), "oy": ("sbuf", [128, 2, 256], "bfloat16"), "oe": ("sbuf", [128, 3, 16], "float32"),
 }
-for _b in range(8):
-    SCRATCH["ps%d" % _b] = ("psum", [128, 512], "float32")
-SEMAPHORES = ["sP", "sD", "sA", "sG", "le0", "liv", "lst", "out", "outA", "loc"] + ["ar%d" % _n for _n in range(2, 10)] + ["ap%d" % _n for _n in range(2, 10)]
+for _b in range(NTB):
+    SCRATCH["ps%d" % _b] = ("psum", [128, 64, 8], "float32")
+for _b in range(NTB, 8):
+    SCRATCH["ps%d" % _b] = ("psum", [128, 512 // W, MU, 16], "float32")
+SEMAPHORES = ["sP", "sD", "sA", "sG", "le0", "liv", "lst", "out", "outA", "loc", "oh"] + ["wn%d" % _n for _n in range(5 * NCH)]
+SEMAPHORES += [_k + str(_n) for _k in ("ar", "ap", "aa")[:2 + (NCH == 2)] for _n in range(NCH, 5 * NCH)]
 
-FAC = 1.25
+FAC = 1.0
+LAT = 5.0
+HOP = 0.17
+GI = 1.0
 
 
 def build(g, core, T, topo):
@@ -49,7 +69,6 @@ def build(g, core, T, topo):
     last_w = {}
     readers = {}
     phase = ["set"]
-    gate = []
 
     def op(eng, fn, rd, wr, dur, banks=(), sem=None, lat=0.0):
         n = len(ops)
@@ -67,8 +86,6 @@ def build(g, core, T, topo):
             last_w[w] = n
             readers[w] = []
         deps.discard(n)
-        if phase[0] == "late" and gate:
-            deps.add(gate[0])
         ops.append({"ph": phase[0], "eng": eng, "fn": fn, "deps": deps, "dur": dur, "banks": tuple(banks), "sem": sem, "lat": lat, "wr": wr})
         return n
 
@@ -95,6 +112,9 @@ def build(g, core, T, topo):
     def cp(out, a, rd, wr, cyc):
         return dv(lambda: g.vector.tensor_copy(out, a), rd, wr, cyc)
 
+    def ms(ap, v, wr, cyc):
+        return dv(lambda: g.vector.memset(ap, v), [], wr, cyc)
+
     def act(out, a, f, rd, wr, cyc, bias=0.0, scale=1.0):
         return ac(lambda: g.scalar.activation(out, a, f, bias=bias, scale=scale), rd, wr, cyc)
 
@@ -105,147 +125,219 @@ def build(g, core, T, topo):
                 r = g.tensor.matmul(it[0], it[1], it[2], first and q == 0, final and q == len(items) - 1)
             return r
         cyc = sum(max(64, it[3]) for it in items)
-        return op("P", fn, list(rd) + [it[4] for it in items], wr, 0.03 + cyc * 0.417e-3 * FAC, bk(*wr))
+        n = op("P", fn, list(rd) + [it[4] for it in items], wr, 0.03 + cyc * 0.417e-3 * FAC, bk(*wr))
+        ops[n]["nmm"] = len(items)
+        return n
+
+    def iota(out, pat, base, cm, wr, n):
+        return po(lambda: g.iota(out, pat, base, cm, allow_small_or_imprecise_dtypes=True), [], wr, n)
+
+    GW = int(1.56 * W)
 
     op("S", lambda: g.sync.dma_start(T.e0i[:], T.e0[:]), [], ["e0i"], 0.1, sem=("le0", 16), lat=2.0)
     op("S", lambda: g.sync.dma_start(T.ivi[:], T.iv[:]), [], ["ivi"], 0.1, sem=("liv", 16), lat=6.0)
     op("A", lambda: g.scalar.dma_start(T.stb[:], T.st[:]), [], ["stb"], 0.1, sem=("lst", 16), lat=7.0)
 
     slot = {}
+    tslot = {}
 
     def wm(name):
         if name not in slot:
             slot[name] = len(slot)
         return T.Wm[:, slot[name]]
 
-    def Wt(name):
-        return (wm(name), "W" + name)
+    def tmx(name):
+        if name not in tslot:
+            tslot[name] = len(tslot)
+        return tslot[name]
 
-    def ms(ap, v, wr, cyc):
-        return dv(lambda: g.vector.memset(ap, v), [], wr, cyc)
+    ncol = [0]
+
+    def col():
+        ncol[0] += 1
+        return T.cols[:, ncol[0] - 1:ncol[0]]
+
+    def E(r):
+        return T.E16[:, r:r + 1]
+
+    def TN(name):
+        return ["T%s:%d" % (name, y) for y in range(32)]
 
     ms(T.ones[:], 1.0, ["ones"], 64)
-    ms(T.zer[:], 0.0, ["zer"], 64)
+    ms(T.Tm[:, 0:2], 0.0, TN("fF") + TN("pF"), 256)
+    tmx("fF")
+    tmx("pF")
+    one = T.ones[:, 0:W]
     po(lambda: g.iota(T.coli[:, 0:1], [[0, 1]], 0, 1), [], ["coli0"], 1)
+    iota(T.itr[:], [[0, 16], [1, 16]], 0, 0, ["itr"], 256)
     po(lambda: g.affine_select(wm("I"), T.ones[:], [[-1, 128]], AL.is_equal, 0.0, 0, 1), ["ones"], ["WI"], 128)
     po(lambda: g.affine_select(wm("B0"), T.ones[:], [[-16, 8], [0, 16]], AL.is_ge, 0.0, 0, 1), ["ones"], ["WB0"], 128)
-    po(lambda: g.iota(T.it1[:], [[0, 16], [1, 16]], 0, 0, allow_small_or_imprecise_dtypes=True), [], ["it1"], 256)
     po(lambda: g.affine_select(wm("B"), wm("B0"), [[16, 8], [0, 16]], AL.is_ge, 0.0, 15, -1), ["WB0"], ["WB"], 128)
-    po(lambda: g.iota(T.ofi[:], [[1, 32]], 0, 0), [], ["ofi"], 32)
-    po(lambda: g.iota(T.it2[:], [[1, 256]], 32768, 0, allow_small_or_imprecise_dtypes=True), [], ["it2"], 256)
-    po(lambda: g.affine_select(wm("L"), wm("B"), [[1, 128]], AL.is_gt, 0.0, 0, -1), ["WB"], ["WL"], 128)
+    iota(T.itl[:], [[1, 256]], -128, 0, ["itl"], 256)
     ts(T.coli[:, 1:2], T.coli[:, 0:1], 15, None, AL.bitwise_and, None, ["coli0"], ["coli1"], 1)
-    pcol = T.cols[:, 0:1]
+    pcol = col()
     cp(pcol, T.coli[:, 1:2], ["coli1"], ["pcol"], 1)
-    cp(T.ofu[:], T.ofi[:], ["ofi"], ["ofu"], 32)
-    ts(T.dm[:, 0:256], T.it1[:], pcol, None, AL.is_equal, None, ["it1", "pcol"], ["dm0"], 256)
-    cp(T.dm[:, 256:512], T.dm[:, 0:256], ["dm0"], ["dm1"], 128)
-    ts(T.seg[:], T.it1[:], 0.5, None, AL.is_gt, None, ["it1"], ["seg"], 256)
-    tt(T.it2[:], T.it2[:], T.dm[:, 0:256], AL.mult, ["it2", "dm0"], ["it2"], 512)
-    ts(T.dcon[:], T.it2[:], -32768.0, None, AL.add, None, ["it2"], ["dcon"], 256)
-    ts(T.econ[:], T.dm[:, 0:128], 32768.0, -32768.0, AL.mult, AL.add, ["dm0"], ["econ"], 64)
-    ts(T.E16[:], T.it1[:, 0:16], pcol, None, AL.is_equal, None, ["it1", "pcol"], ["E16"], 16)
-    act(T.colb[:, 0:1], pcol, AF.Exp, ["pcol"], ["p2"], 1, scale=math.log(2.0))
-    act(T.colb[:, 1:2], pcol, AF.Exp, ["pcol"], ["p2n"], 1, scale=-math.log(2.0), bias=-math.log(2.0))
-    cp(T.cols[:, 1:2], T.colb[:, 0:1], ["p2"], ["p2f"], 1)
-    cp(T.cols[:, 2:3], T.colb[:, 1:2], ["p2n"], ["p2nf"], 1)
-    ts(T.cols[:, 3:4], pcol, -0.5, 0.5, AL.mult, AL.add, ["pcol"], ["cOg"], 1)
-    ts(T.cols[:, 4:5], pcol, -1.0, 0.5, AL.mult, AL.add, ["pcol"], ["cq"], 1)
-    ts(T.cols[:, 5:6], T.E16[:, 4:5], 1.0, 127.8, AL.mult, AL.add, ["E16"], ["cM0"], 1)
-    ts(T.cols[:, 6:7], T.E16[:, 9:10], -128.0, T.E16[:, 8:9], AL.mult, AL.add, ["E16"], ["cF"], 1)
-    flip = [0]
+    ts(T.E16[:], T.itr[:, 0:16], pcol, None, AL.is_equal, None, ["itr", "pcol"], ["E16"], 16)
+    act(T.colb[:, 0:1], pcol, AF.Exp, ["pcol"], ["p2b"], 1, scale=math.log(2.0))
+    act(T.colb[:, 1:2], pcol, AF.Exp, ["pcol"], ["p2nb"], 1, scale=-math.log(2.0), bias=-math.log(2.0))
+    p2, p2n, p2k, cq, cx, cF, cF1, c256, r16 = (col() for _ in range(9))
+    act(p2, T.colb[:, 0:1], AF.Identity, ["p2b"], ["p2"], 1)
+    act(p2n, T.colb[:, 1:2], AF.Identity, ["p2nb"], ["p2n"], 1)
+    act(p2k, T.colb[:, 0:1], AF.Identity, ["p2b"], ["p2k"], 1, scale=2.0 ** -60)
+    act(cq, pcol, AF.Identity, ["pcol"], ["cq"], 1, scale=-1.0)
+    act(cx, pcol, AF.Identity, ["pcol"], ["cx"], 1, scale=-LB, bias=LB * (15 - 135.5 - 320))
+    act(cF, E(0), AF.Identity, ["E16"], ["cF"], 1, scale=393216.0 - 1022.5)
+    act(cF1, E(14), AF.Identity, ["E16", "cF"], ["cF1"], 1, bias=cF)
+    act(c256, pcol, AF.Identity, ["pcol"], ["c256"], 1, scale=256.0, bias=128.0)
+    act(r16, pcol, AF.Identity, ["pcol"], ["r16"], 1, scale=16.0, bias=4096.0)
 
-    def scaled(name, base, v, rd=()):
-        if name not in ("B2", "n1024", "nI"):
+    def scaled(name, base, v, rd=(), eng="A"):
+        if eng == "A":
             act(wm(name), wm(base), AF.Identity, ["W" + base] + list(rd), ["W" + name], 128, scale=v)
         else:
             ts(wm(name), wm(base), v, None, AL.mult, None, ["W" + base] + list(rd), ["W" + name], 64)
 
-    for nm, v in (("nI", -1.0), ("hI", 0.5), ("nhI", -0.5), ("n1024", -1024.0), ("I16", 16.0), ("I2", 2.0), ("I256", 256.0),
-                  ("I512", 512.0), ("n512", -512.0), ("n20", -20.0), ("I448", 448.0), ("sI", SCL), ("nsI", -SCL), ("nqI", -0.25)):
+    for nm, v in (("nI", -1.0), ("midK", -2.0 ** -44), ("midC", -65536.0), ("hI", 0.5), ("FM", 1.0)):
+        scaled(nm, "I", v, eng="D")
+    for nm, v in (("midC2", -131072.0), ("vK", 2.0 ** -37), ("vC", 2.0 ** 23), ("sI", SCL), ("cntK", -20 * 2.0 ** -60), ("n512", -512.0), ("I25", 2.5), ("nhI", -0.5)):
         scaled(nm, "I", v)
-    scaled("cqI", "I", T.cols[:, 4:5], ["cq"])
-    for nm, v in (("B2", 2.0), ("B4096", 4096.0), ("nB", -1.0), ("nqB", -0.25)):
+    scaled("cqI", "I", cq, ["cq"])
+    ts(T.nI16[:], wm("I"), -1.0, None, AL.mult, None, ["WI"], ["WnI16"], 64)
+    for nm, v, d in (("t1", -512.0, -2304.0), ("t2", -2.0, 219 * 256.0), ("v", TAU * 2.0 ** -22, -SCL)):
         scaled(nm, "B", v)
-    scaled("pB", "B", pcol, ["pcol"])
-    scaled("pwB", "B", T.cols[:, 2:3], ["p2nf"])
-    ts(wm("nCB"), wm("B"), T.cols[:, 1:2], -1.0, AL.mult, AL.mult, ["WB", "p2f"], ["WnCB"], 64)
-    tt(wm("IL"), wm("I"), wm("L"), AL.subtract, ["WI", "WL"], ["WIL"], 128)
-    scaled("hIL", "IL", 0.5)
-    scaled("I24", "I", 24.0)
-    tt(wm("S24"), wm("I24"), wm("B"), AL.subtract, ["WI24", "WB"], ["WS24"], 128)
+        po(lambda nm=nm, d=d: g.affine_select(wm(nm), wm(nm), [[-1, 128]], AL.not_equal, d, 0, 1), ["W" + nm], ["W" + nm], 128)
+    for q in range(2):
+        act(T.I37[:, q], wm("I"), AF.Identity, ["WI"], ["WI37"], 128, scale=37.0 - 74.0 * q)
+    tt(wm("S25"), wm("I25"), wm("B"), AL.subtract, ["WI25", "WB"], ["WS25"], 128)
     G8 = T.Wm[:, slot["B"], :, 0]
-    ms(T.Z[:], 0.0, ["Z0", "Z1", "Z2"], 216)
-    cp(T.Z[:, 0, 15:128:16], G8, ["WB", "Z0"], ["Z0"], 8)
-    ts(T.Z[:, 1, 15:128:16], G8, -1.0, None, AL.mult, None, ["WB", "Z1"], ["Z1"], 8)
-    ts(T.Z[:, 2, 15:128:16], G8, T.cols[:, 1:2], None, AL.mult, None, ["WB", "Z2", "p2f"], ["Z2"], 8)
+    ms(T.Z[:], 0.0, ["Z"], 72)
+    ts(T.Z[:, 15:128:16], G8, p2, None, AL.mult, None, ["WB", "Z", "p2"], ["Z"], 8)
 
-    def Zs(which, r):
-        return (T.Z[:, which, 15 - r:143 - r], "Z%d" % which)
-
-    def colmat(name, ents):
-        act(wm(name), T.zer[:], AF.Identity, ["zer"], ["W" + name], 128)
-        for r, v in ents:
-            act(T.Wm[:, slot[name], :, r], G8, AF.Identity, ["WB", "pcol", "W" + name], ["W" + name], 8, scale=pcol if v is None else v)
-
-    colmat("M0a", [(0, 2.0), (1, 1.0)])
-    colmat("M0b", [(2, 2.0)])
-    colmat("Fd", [(1, 1.0), (6, None), (11, 1.0), (12, 1.0)])
-    colmat("Fg", [(0, 1.0), (6, None), (11, 1.0)])
-    colmat("Ff", [(6, None), (11, 1.0), (12, 1.0)])
-    scaled("Fn2", "I", T.E16[:, 10:11], ["E16"])
-
-    def entmat(name, ents, src=None):
-        wm(name)
+    def ent(name, ents):
         k = slot[name]
-        for q, (r0, a, b, v) in enumerate(ents):
-            if q == 0 and (a, b) == (0, 16):
-                i_ap, rd = (T.zer[:], ["zer"]) if src is None else (wm(src), ["W" + src])
-            else:
-                if q == 0:
-                    act(wm(name), T.zer[:], AF.Identity, ["zer"], ["W" + name], 128)
-                i_ap, rd = T.Wm[:, k, :, a:b], ["W" + name]
-            po(lambda k=k, a=a, b=b, i_ap=i_ap, v=v, r0=r0: g.affine_select(T.Wm[:, k, :, a:b], i_ap, [[-16, 8], [0, b - a]], AL.not_equal, float(v), -r0, 1),
-               rd, ["W" + name], 8 * (b - a))
+        for r0, a, b, v in ents:
+            ap = T.Wm[:, k, :, a:b]
+            po(lambda ap=ap, a=a, b=b, v=v, r0=r0: g.affine_select(ap, ap, [[-16, 8], [0, b - a]], AL.not_equal, float(v), -r0, 1),
+               ["W" + name], ["W" + name], 8 * (b - a))
 
-    entmat("d", [(1, 0, 16, 256)])
-    entmat("e", [(0, 0, 16, 128), (2, 0, 16, 1)])
-    entmat("eA", [(3, 0, 16, 1)], src="e")
-    po(lambda: g.iota(wm("y0"), [[0, 8], [-1, 16]], -14, 0, allow_small_or_imprecise_dtypes=True), [], ["Wy0"], 128)
-    po(lambda: g.affine_select(wm("y1"), wm("y0"), [[-16, 8], [0, 16]], AL.is_equal, 0.0, -5, 1), ["Wy0"], ["Wy1"], 128)
-    entmat("y", [(0, 0, 16, 640), (2, 0, 16, 5), (3, 0, 16, 1), (6, 0, 16, 3.0 / 256)], src="y1")
-    entmat("Fm", [(4, 9, 10, 1)])
-    entmat("keep", [(8, 0, 16, 1), (12, 0, 16, -1)])
-    entmat("mM", [(8, 0, 4, 1), (11, 0, 3, -1)])
-    entmat("M", [(6, 0, 1, 2), (6, 1, 2, 1), (1, 2, 3, 256), (11, 0, 2, 256), (11, 2, 3, 255), (12, 3, 5, 2), (8, 4, 16, 256)])
-    entmat("K", [(12, 0, 16, -129)])
-    entmat("s0", [(9, 0, 16, 256), (12, 0, 16, 2048), (0, 0, 16, 1)])
-    entmat("s1", [(3, 0, 16, 255), (12, 0, 16, 2048), (0, 0, 16, -1)])
+    def tent(name, ents):
+        k = tmx(name)
+        for r0, sl, v in ents:
+            ap = T.Tm[:, k, :, :, sl]
+            nm = ["T%s:%d" % (name, y) for y in range(32)[sl]]
+            po(lambda ap=ap, n=len(nm), v=v, r0=r0: g.affine_select(ap, ap, [[-16, 2], [-32, 4], [0, n]], AL.not_equal, float(v), -r0, 1), nm, nm, 8 * len(nm))
 
-    ms(T.sta[:, 0:8, 768:784], 200.0, ["S"], 64)
-    ms(T.sta[:, 8:10, 768:784], -129.0, ["SL"], 16)
-    ms(T.sta[:, 0:4, 513:768:2], 0.0, ["zq%d" % q for q in range(4)], 256)
-    phase[0] = "late"
-    gate.append(last_w["WM"])
-    entmat("s1L", [(3, 0, 16, 255), (12, 0, 16, 4096), (0, 0, 16, 6144), (9, 0, 16, 2048), (10, 0, 16, -2048)])
-    entmat("a", [(3, 0, 16, 1)])
-    scaled("nB2k", "B", -2048.0)
-    phase[0] = "set"
-    ms(T.sta[:, 0:2, 256:512], 200.0, ["P0", "P1"], 256)
+    def lin(name, terms):
+        c = col()
+        for q, (r0, v) in enumerate(terms):
+            act(c, E(r0), AF.Identity, ["E16", name], [name], 1, scale=float(v), bias=c if q else 0.0)
+        return c
 
-    cp(T.e0u[:], T.e0i[:], ["e0i"], ["e0u"], 16)
-    ts(T.e0p[:, 0:16], T.e0i[:], 7, None, AL.arith_shift_right, None, ["e0i"], ["e0p0"], 16)
-    ts(T.e0p[:, 16:32], T.e0i[:], 127, None, AL.bitwise_and, None, ["e0i"], ["e0p1"], 16)
-    tt(T.X0[:], T.e0p[:, 0:32].indirect(T.ofu[:, 0:32]), T.dm[:], AL.mult, ["e0p0", "e0p1", "ofu", "dm0", "dm1"], ["X0"], 800)
-    pe([(T.ps0[:, 0:256], wm("M0a"), T.X0[:, 0:256], 256, "WM0a"), (T.ps0[:, 0:256], wm("M0b"), T.X0[:, 256:512], 256, "WM0b")], ["X0"], ["ps0"])
-    pe([(T.ps1[:, 0:256], wm("B"), T.X0[:, 0:256], 256, "WB")], ["X0"], ["ps1"])
-    pe([(T.ps2[:, 0:256], wm("B2"), T.X0[:, 256:512], 256, "WB2")], ["X0"], ["ps2"])
-    ts(T.O0[:, 0], T.ps1[:, 0:256], pcol, None, AL.is_equal, None, ["ps1", "pcol"], ["O0"], 256)
-    act(T.O0[:, 1], T.ps2[:, 0:256], AF.Identity, ["ps2"], ["O1"], 256, bias=1.0)
-    tt(T.O0[:, 0], T.O0[:, 0], T.O0[:, 1], AL.mult, ["O0", "O1"], ["O0"], 512)
-    for ch in range(2):
-        act(T.sta[:, ch, 1:256:2], T.ps0[:, ch * W:ch * W + W], AF.Identity, ["ps0", "cM0"], ["M%d" % ch], W, bias=T.cols[:, 5:6], scale=0.5)
-        ts(T.sta[:, ch, 0:256:2], T.O0[:, 0, ch * W:ch * W + W], -129.0, None, AL.add, None, ["O0"], ["K%d" % ch], 64)
+    S = slice
+    ZO, KO = 64 + 4 * W, 64 + 5 * W
+    ent("FM", [(1, 0, 1, 640), (2, 0, 1, 5), (4, 0, 1, 1)])
+    scaled("eA", "B", lin("ceA", [(1, 128), (2, 1), (4, 1)]), ["ceA"])
+    scaled("neA", "B", lin("cneA", [(1, -128), (2, -1), (4, -1), (7, 2048), (10, -0.5)]), ["cneA"])
+    for nm, v in (("c12", 1.5 * 2.0 ** 35), ("nc12", -1.5 * 2.0 ** 35), ("c4", C16), ("nc4", -C16)):
+        scaled(nm, "I", v)
+    scaled("nB", "B", -1.0)
+    scaled("ncqI", "I", pcol, ["pcol"])
+    tent("pF", [(3, S(16, 17), 256), (9, S(16, 17), 1)])
+    tent("fF", [(1, S(12, 13), 256), (1, S(15, 16), 1280), (2, S(12, 13), 2), (2, S(15, 16), 10), (4, S(15, 16), 2), (0, S(15, 16), -2),
+                (4, S(0, 4), 1), (4, S(8, 12), 1), (8, S(21, 23), 48), (8, S(30, 31), 48), (9, S(4, 6), 1), (9, S(20, 23), 1), (9, S(28, 31), 1),
+                (5, S(0, 1), PB), (5, S(20, 32, 8), PB), (12, S(1, 2), PB), (12, S(21, 32, 8), PB), (6, S(4, 13, 4), PB), (6, S(2, 3), -16), (13, S(10, 15, 4), PB),
+                (7, S(2, 3), -PB), (7, S(5, 14, 4), -PB), (7, S(22, 32, 8), -PB), (7, S(11, 16, 4), -2 * PB),
+                (10, S(0, 1), 2080), (10, S(1, 2), 2096), (10, S(2, 4), 2048), (10, S(4, 6), KO), (10, S(7, 8), 24), (10, S(12, 16), WS),
+                (10, S(20, 21), ZO), (10, S(21, 31, 9), 96), (10, S(22, 23), 112), (10, S(23, 32, 8), 16), (10, S(28, 30), ZO),
+                (11, S(3, 4), 1), (11, S(10, 12), 1), (11, S(15, 16), 786432), (15, S(15, 16), 2),
+                (14, S(4, 8), 4096), (14, S(12, 16), -WS), (14, S(20, 24), 4096), (14, S(28, 32), 4096)])
+    ms(T.Tm[:, 2:5], 0.0, TN("pK") + TN("fZ") + TN("fTg"), 128 * 3)
+    ms(T.Tm[:, 5:NT], 0.0, TN("wT") + TN("fOg") + TN("fC0") + TN("fC1") + TN("fOq") + TN("fTf"), 128 * (NT - 5))
+    for h in range(2):
+        act(T.BP[:, h], T.Wm[:, slot["B"], h:8:2], AF.Identity, ["WB"], ["BP%d" % h], 64)
+    cpF = lin("cpF", [(7, 65536), (10, -0.5)])
+    ea, ena = col(), col()
+    act(ea, E(0), AF.Identity, ["E16"], ["ea"], 1, scale=ALF)
+    act(ena, E(0), AF.Identity, ["E16"], ["ena"], 1, scale=-ALF)
+    for name, ents in (("pF", [(S(0, 16), cpF, "cpF")]), ("pK", [(S(0, 16), p2k, "p2k")]),
+                       ("fZ", [(S(0, 2), ea, "ea"), (S(4, 13, 4), ea, "ea"), (S(10, 15, 4), ea, "ea"), (S(20, 22), ea, "ea"), (S(28, 30), ea, "ea"),
+                               (S(2, 3), ena, "ena"), (S(5, 14, 4), ena, "ena"), (S(11, 16, 4), ena, "ena"), (S(22, 32, 8), ena, "ena")]),
+                       ("fTg", [(S(13, 14), 1.0, None), (S(2, 3), ALF, None), (S(5, 10, 4), ALF, None), (S(22, 32, 8), ALF, None), (S(11, 16, 4), -ALF, None)]),
+                       ("wT", [(S(0, 16), p2n, "p2n")]), ("fOg", [(S(13, 14), c256, "c256")]),
+                       ("fC0", [(S(2, 3), 16.0, None), (S(22, 23), -16.0, None)]), ("fC1", [(S(2, 31, 28), 16.0, None)]),
+                       ("fOq", [(S(14, 15), c256, "c256")]), ("fTf", [(S(14, 15), 1.0, None)])):
+        k = tmx(name)
+        for sl, v, nm in ents:
+            wn = ["T%s:%d" % (name, y) for y in range(32)[sl]]
+            act(T.Tm[:, k, :, :, sl], T.BP[:, :, :, 0:len(wn)], AF.Identity, ["BP0", "BP1"] + ([nm] if nm else []), wn, 8 * len(wn), scale=v)
+    scaled("Y0", "B", lin("cY0", [(7, -129), (5, -256)]), ["cY0"])
+    scaled("Y1", "B", lin("cY1", [(7, -129), (6, -256)]), ["cY1"])
+
+    ts(T.NK[:], T.E16[:], -1.0, -KN, AL.add, AL.mult, ["E16"], ["NK"], 16)
+    for q in range(16):
+        o = T.win[:, 0, WS + 256 * q:WS + 256 * q + 256]
+        if q % 3 == 2:
+            act(o, T.itl[:], AF.Identity, ["itl", "E16", "NK"], ["OH%d" % q], 256, scale=E(q), bias=T.NK[:, q:q + 1])
+        else:
+            ts(o, T.itl[:], E(q), T.NK[:, q:q + 1], AL.mult, AL.add, ["itl", "E16", "NK"], ["OH%d" % q], 128)
+    OHN = [["OH%d" % q for q in range(16)], ["OHc"]]
+    if NCH > 2:
+        op("S", lambda: g.sync.dma_start(T.win[:, 1, WS:WS + 4096], T.win[:, 0, WS:WS + 4096]), OHN[0] + ["stb"], ["OHc"], 0.1, sem=("oh", 16), lat=5.0)
+    d2, d4, d8 = col(), col(), col()
+    ts(d2, E(1), 2.0, E(3), AL.mult, AL.add, ["E16"], ["d2"], 1)
+    act(d4, d2, AF.Identity, ["d2"], ["d4"], 1, scale=2.0)
+    act(d8, d2, AF.Identity, ["d2"], ["d8"], 1, scale=4.0)
+    ts(T.TM[:, 0:128], T.itl[:, 128:256], E(2), None, AL.mult, None, ["itl", "E16"], ["TM"], 64)
+    for n, c, nm in ((128, E(1), "E16"), (256, d2, "d2"), (512, d4, "d4"), (1024, d8, "d8")):
+        ts(T.TM[:, n:2 * n], T.TM[:, 0:n], c, None, AL.add, None, ["TM", nm], ["TM"], n // 2)
+    ts(T.OHb[:, 0:256], T.itr[:], pcol, None, AL.is_equal, None, ["itr", "pcol"], ["OHb"], 128)
+    for n in (256, 512, 1024):
+        if n < 16 * W:
+            cp(T.OHb[:, n:2 * n], T.OHb[:, 0:n], ["OHb"], ["OHb"], n // 2)
+    ms(T.OHb[:, 16 * W:16 * W + 16], 0.0, ["OHz"], 16)
+    ms(T.Y[:, :, 16 * W:16 * W + 16], ZN, ["Yz"], 32)
+    ms(T.pat[:], 1.0, ["pat"], W)
+    ts(T.pat[:, 15:W:16], T.itr[:, 0:MU], 256.0, r16, AL.mult, AL.add, ["itr", "r16", "pat"], ["pat"], 8)
+    ms(T.seg[:], 1.0, ["seg"], W)
+    ms(T.seg[:, 0:2 * W:4], 0.0, ["seg"], 64)
+    iota(T.itm[:], [[1, MU], [0, 16]], 0, 0, ["itm"], W)
+    ts(T.lanec[:], T.itl[:, 128:128 + W], E(9), None, AL.mult, None, ["itl", "E16"], ["lanec"], 64)
+    ts(T.itm[:], T.itm[:], E(8), None, AL.mult, None, ["itm", "E16"], ["itm"], 64)
+    tt(T.lanec[:], T.lanec[:], T.itm[:], AL.add, ["itm", "lanec"], ["lanec"], W)
+    kb, k2, k0, k3 = (col() for _ in range(4))
+    ts(kb, E(7), E(10), E(11), AL.add, AL.add, ["E16"], ["kb"], 1)
+    ts(kb, kb, E(15), None, AL.add, None, ["E16", "kb"], ["kb"], 1)
+    ts(k0, kb, E(12), E(13), AL.subtract, AL.subtract, ["E16", "kb"], ["k0"], 1)
+    ts(k2, kb, E(5), E(13), AL.subtract, AL.subtract, ["E16", "kb"], ["k2"], 1)
+    ts(k3, kb, E(5), E(6), AL.subtract, AL.subtract, ["E16", "kb"], ["k3"], 1)
+    ts(k3, k3, E(12), None, AL.subtract, None, ["E16", "k3"], ["k3"], 1)
+    for q, c, nm in ((0, k0, "k0"), (1, k0, "k0"), (2, k2, "k2"), (3, k3, "k3")):
+        ts(T.TM[:, 2048 + 16 * q:2064 + 16 * q], T.itr[:, 0:16], E(4), c, AL.mult, AL.add, ["itr", "E16", nm], ["TA%d" % q], 16)
+    TAN = ["TM"] + ["TA%d" % q for q in range(4)]
+
+    def wn_(ch, a, b):
+        o = (WS + 4096) * (ch % 2)
+        return T.win[:, ch // 2, o + a:o + b]
+
+    for par in range(2):
+        o = (WS + 4096) * par
+        ms(T.win[:, :, o:o + 24], AB, ["wa%d" % par], 24)
+        ms(T.win[:, :, o + 24:o + 64], KN, ["wk%d" % par], 40)
+
+    def sfv(ch, q):
+        return T.sf[:, ch, q]
+
+    def sbv(ch, q):
+        return T.sb[:, ch, q]
+
+    ts(T.e0u[:], T.e0i[:], 2.0, None, AL.mult, None, ["e0i"], ["x0u"], 16)
+    cp(T.eL[:, 0:NCH, 0:MU], T.e0i[:], ["e0i"], ["e%d" % q for q in range(NCH)], 16)
+    ms(T.eL[:, 0:NCH, MU:2 * MU], 2048, ["a%d" % q for q in range(NCH)], 16)
+    ms(T.sb[:, :, 9], ZN / 16, ["tg%d" % q for q in range(NCH)], 128)
+    for ch in range(NCH):
+        c = str(ch)
+        act(wn_(ch, KO, WS), T.win[:, 0, WS:WS + 4096].indirect(T.e0u[:, MU * ch:MU * ch + MU]), AF.Identity, OHN[0] + ["x0u"], ["K" + c], GW)
+        ms(T.sta[:, ch], AB, ["P_" + c], 2 * W)
     for q in range(4):
         cp(T.ivf[:, q * 512:q * 512 + 512], T.ivi[:, q * 512:q * 512 + 512], ["ivi"], ["ivf%d" % q], 512)
     IVF = ["ivf%d" % q for q in range(4)]
@@ -255,363 +347,357 @@ def build(g, core, T, topo):
     NR = len(cores)
     tile = [0]
 
-    def masks(src, ch):
-        ds = [(b, cores[(src + b) % NR]) for b in range(4 * ch, 4 * ch + 4) if b % NR]
-        en = {b: topo.engines(cores[src], d) for b, d in ds}
-        few = min(len(v) for v in en.values())
-        far = [b for b, d in ds if len(en[b]) == few]
+    def masks(src, ch, copies):
+        ds = [(b, q) for b in range(NB * ch, NB * ch + NB) if b % NR for q in range(copies)]
+        en = {x: topo.engines(cores[src], cores[(src + x[0]) % NR]) for x in ds}
+        few = min(en.values(), key=len)
         res = {}
-        pool = list(en[far[0]])
-        left = len(far)
-        for b in reversed(far):
-            n = 1
-            while 2 * n * left <= len(pool):
-                n *= 2
-            res[b] = pool[:n]
-            pool = pool[n:]
-            left -= 1
-        near = [b for b, d in ds if b not in far]
-        for b in near:
-            used = [e for v in res.values() for e in v]
-            free = [e for e in en[b] if e not in used and e not in en[far[0]]]
-            n = 1
-            while 2 * n * len(near) <= len(free):
-                n *= 2
-            res[b] = free[:n]
+        for pool, xs in ((few, [x for x in ds if len(en[x]) == len(few)]), (None, [x for x in ds if len(en[x]) > len(few)])):
+            if xs:
+                pool = list(pool or [e for e in en[xs[0]] if e not in few])
+                left = len(xs)
+                for x in reversed(xs):
+                    n = 1
+                    while 2 * n * left <= len(pool):
+                        n *= 2
+                    res[x] = pool[:n]
+                    pool = pool[n:]
+                    left -= 1
         return res
 
     def views(s, ch):
-        n = 2 * s + ch
-        c = str(ch)
-        a = T["ps%d" % (5 + ch)]
-        an = "ps%d" % (5 + ch)
-        v = {"n": n, "c": c, "a": [a[:, q * W:q * W + W] for q in range(4)], "an": [an + "r%d" % q for q in range(4)], "abuf": a,
-             "w": T.ps7[:, ch * 256:ch * 256 + 256], "wn": "ps7" + c, "w0": ch * 256}
-        return v
+        n = NCH * s + ch
+        if NCH == 2:
+            place = {"R": (4 + ch, 0), "X": (4 + ch, 1), "T": (4 + ch, 2), "A": (6 + ch, 0), "B": (6 + ch, 1), "C": (6 + ch, 2), "N": (6 + ch, 3)}
+        else:
+            place = {"R": (4 + ch, 0), "X": (4 + ch, 1), "T": (4 + ch, 2), "A": (4 + ch, 4), "B": (4 + ch, 5), "C": (4 + ch, 6), "N": (3, 0)}
+        r = {k: T["ps%d" % b][:, q] for k, (b, q) in place.items()}
+        nm = {k: "ps%dq%d" % v for k, v in place.items()}
+        lk = {k: "lk%d" % v[0] for k, v in place.items()}
+        st = [wn_(ch, KO, WS), T.M[:, ch, W:2 * W], T.sta[:, n, :, 2], T.sta[:, n, :, 3]]
+        return n, str(ch), str(n), place, r, nm, lk, st
 
-    def sfv(ch, q):
-        return T.sf[:, ch, q]
-
-    def sbv(ch, q):
-        return T.sb[:, ch, q]
-
-    def scan(ch, src, n, rd):
-        dv(lambda: g.vector.tensor_tensor_scan(T.scn[:, ch, 0:n], T.seg[:, 0:n], src, 0.0, AL.mult, AL.max), list(rd) + ["seg"], ["scn%d" % ch], n)
-
-    def scan2(ch, src, n, rd, u):
-        dv(lambda: g.vector.tensor_tensor_scan(T.sc2[:, ch, u, 0:n], T.seg[:, 0:n], src, 0.0, AL.mult, AL.max), list(rd) + ["seg"], ["sc%d%d" % (u, ch)], n)
+    def turn(place, nm, lk, parts, ch, u):
+        bank, q = T["ps%d" % place["T"][0]], place["T"][1]
+        for i, (terms, rd) in enumerate(parts):
+            it = [(bank[:, q:q + 2, h:MU:2], T.Tm[:, tslot[x], h], rhs, W, "WI") for h in range(2) for x, rhs in terms]
+            rd = rd + [y for x, rhs in terms for y in TN(x)]
+            if len(parts) == 1:
+                pe(it, rd + [lk["T"]], [nm["T"]])
+            else:
+                pe(it, rd, [nm["T"], lk["T"]], first=i == 0, final=i == len(parts) - 1)
+        dv(lambda: g.vector.transpose(T.tT[:, ch, u] if u < 2 else T.tF[:, ch], bank[:, q:q + 2]), [nm["T"]], ["tT%d%d" % (u, ch)], 2 * W)
 
     def prep(s, ch):
-        v = views(s, ch)
-        n, c, a, an = v["n"], v["c"], v["a"], v["an"]
-        N = str(n)
-        K, M, P0, P1 = T.sta[:, n, 0:256:2], T.sta[:, n, 1:256:2], T.sta[:, n, 256:512:2], T.sta[:, n, 257:512:2]
-        w0 = v["w0"]
-        wa, wb = T.ps7[:, w0:w0 + W], T.ps7[:, w0 + W:w0 + 256]
-        dc = T.dcon[:, ch * W:ch * W + W]
+        n, c, N, place, r, nm, lk, (K, MA, P0, P1) = views(s, ch)
+        PN = "P_" + N
+        el, eln = T.eL[:, n, 0:MU], "e" + N
         if s == 0:
-            pe([(wa, wm("d"), M, W, "Wd"), (wa, wm("I"), dc, W, "WI")], ["M" + N, "dcon"], [v["wn"]])
-            scan(ch, wa, W, [v["wn"]])
-            ts(T.lu[:, ch, 8:16], T.scn[:, ch, 15:128:16], -32768.0, None, AL.add, None, ["scn" + c], ["dl" + c], 8)
-            el, eln = T.e0u[:, 8 * ch:8 * ch + 8], "e0u"
-            cp(T.c16[:, ch], T.ivi[:, 0:2048].indirect(el), ["ivi", eln], ["c16" + c], 200)
+            cp(T.c16[:, ch], T.ivi[:, 0:2048].indirect(el), ["ivi", eln], ["c16" + c], GW)
         else:
-            pe([(wa, wm("e"), M, W, "We"), (wa, wm("I"), T.econ[:], W, "WI")], ["M" + N, "econ"], [v["wn"]])
-            pe([(wb, wm("d"), M, W, "Wd"), (wb, wm("I"), dc, W, "WI")], ["M" + N, "dcon"], [v["wn"]])
-            scan(ch, v["w"], 256, [v["wn"]])
-            ts(T.lu[:, ch, 0:8], T.scn[:, ch, 15:128:16], -16512.0, None, AL.add, None, ["scn" + c], ["el" + c], 8)
-            ts(T.lu[:, ch, 8:16], T.scn[:, ch, 143:256:16], -32768.0, None, AL.add, None, ["scn" + c], ["dl" + c], 8)
-            el, eln = T.lu[:, ch, 0:8], "el" + c
-            cp(T.c16[:, ch], T.ivf[:, 0:2048].indirect(el), IVF + [eln], ["c16" + c], 200)
-        dl = T.lu[:, ch, 8:16]
-        for q in range(4):
+            cp(T.c16[:, ch], T.ivf[:, 0:2048].indirect(el), IVF + [eln], ["c16" + c], GW)
+        for q in range(NB):
             src = T.stb[:, 0:4096].indirect(T.c16[:, ch, 32 * q:32 * q + 32])
-            if YE[s][4 * ch + q] == "D":
+            if YE[s][NB * ch + q] == "D":
                 ts(T.Y[:, ch, 512 * q:512 * q + 512], src, -128.0, None, AL.add, None, ["stb", "c16" + c], ["Y%d" % q + c], 800)
             else:
                 act(T.Y[:, ch, 512 * q:512 * q + 512], src, AF.Identity, ["stb", "c16" + c], ["Y%d" % q + c], 800, bias=-128.0)
-        ts(sbv(ch, 0), K, -128.5, None, AL.is_gt, None, ["K" + N], ["core" + c], 64)
-        if s > 0:
-            ts(sbv(ch, 15), K, -128.5, 1.0 / 128, AL.is_lt, AL.max, ["K" + N], ["thr" + c], 64)
-            pe([(a[0], wm("I448"), sbv(ch, 15), W, "WI448"), (a[1], wm("I448"), sbv(ch, 15), W, "WI448")], ["thr" + c], [an[0], an[1]])
-        if s > 1:
-            pe([(a[2], wm("hI"), P0, W, "WhI"), (a[2], wm("hI"), P1, W, "WhI"), (a[2], wm("n1024"), sbv(ch, 0), W, "Wn1024")], ["P" + N, "core" + c], [an[2]])
+        op("S", lambda: g.sync.dma_start(wn_(ch, 64, ZO), T.sta[:, n]), [PN], ["win" + c], 0.1, sem=("wn" + N, 16), lat=2.0)
+        mid, hh, F, rr = (sbv(ch, q) for q in (0, 1, 3, 4))
+        it = [(r["A"], wm("hI"), P0, W, "WhI"), (r["A"], wm("hI"), P1, W, "WhI")] if s > 1 else [(r["A"], wm("I"), P0, W, "WI")]
+        if s == 0:
+            pe([(r["A"], wm("midK"), K, W, "WmidK"), (r["A"], wm("midC"), one, W, "WmidC")] + it, [PN, "K" + c, "ones", lk["A"]], [nm["A"]])
+            tt(mid, r["A"], K, AL.max, [nm["A"], "K" + c], ["mid" + c], W)
         else:
-            pe([(a[2], wm("I"), P0, W, "WI"), (a[2], wm("n1024"), sbv(ch, 0), W, "Wn1024")], ["P" + N, "core" + c], [an[2]])
-        tt(sbv(ch, 1), a[2], K, AL.max, [an[2], "K" + N], ["mid" + c], W)
+            Kk, Ox = T.sta[:, n, :, 0], T.sta[:, n, :, 1]
+            pe([(r["A"], wm("midK"), Kk, W, "WmidK"), (r["A"], wm("midK"), Ox, W, "WmidK"), (r["A"], wm("midC2"), one, W, "WmidC2")] + it,
+               [PN, "ones", lk["A"]], [nm["A"]])
+            tt(K, Kk, Ox, AL.max, [PN], ["K" + c], W)
+            ts(T.mh[:, ch, 0], K, -CO, -60000.0, AL.add, AL.max, ["K" + c], ["ko" + c], W // 2)
+            tt(T.mh[:, ch, 1], r["A"], T.mh[:, ch, 0], AL.max, [nm["A"], "ko" + c], ["mid" + c], W)
         if s > 1:
-            pe([(a[3], wm("hI"), P0, W, "WhI"), (a[3], wm("nhI"), P1, W, "WnhI")], ["P" + N], [an[3]])
-            act(sbv(ch, 2), a[3], AF.Abs, [an[3]], ["h" + c], W)
-            pe([(a[3], wm("B"), sbv(ch, 2), W, "WB")], ["h" + c], [an[3]])
-            act(sbv(ch, 3), a[3], AF.Sign, [an[3]], ["n2" + c], W)
-            pe([(a[2], wm("hI"), P0, W, "WhI"), (a[2], wm("hI"), P1, W, "WhI"), (a[2], wm("nI"), sbv(ch, 2), W, "WnI")], ["P" + N, "h" + c], [an[2]])
-        act(sfv(ch, 0), T.ivf[:, 0:2048].indirect(el), AF.Identity, IVF + [eln], ["c37" + c], 200, scale=37.0, bias=-16640.0)
-        act(sfv(ch, 1), T.ivf[:, 0:2048].indirect(dl), AF.Identity, IVF + ["dl" + c], ["old" + c], 200)
-        pe([(wa, wm("eA"), M, W, "WeA"), (wb, wm("y"), M, W, "Wy")], ["M" + N], [v["wn"]])
-        tt(T.si[:, ch, 0], wa, sfv(ch, 0), AL.add, [v["wn"], "c37" + c], ["x" + c], W)
-        ts(T.si[:, ch, 1], T.si[:, ch, 0], 4095, None, AL.bitwise_and, None, ["x" + c], ["val" + c], W)
-        tt(sfv(ch, 2), T.ivf[:, 0:2048].indirect(dl), T.si[:, ch, 1], AL.subtract, IVF + ["dl" + c, "val" + c], ["diff" + c], 200)
-        ts(sbv(ch, 4), wb, C11, -C11, AL.add, AL.add, [v["wn"]], ["ry" + c], W)
+            pe([(r["B"], wm("hI"), P0, W, "WhI"), (r["B"], wm("nhI"), P1, W, "WnhI")], [PN, lk["B"]], [nm["B"]])
+            act(hh, r["B"], AF.Abs, [nm["B"]], ["h" + c], W)
+            pe([(r["C"], wm("vK"), K, W, "WvK"), (r["C"], wm("vC"), one, W, "WvC"), (r["C"], wm("I"), hh, W, "WI")], ["K" + c, "ones", "h" + c, lk["C"]], [nm["C"]])
+            act(sbv(ch, 12), r["C"], AF.Identity, [nm["C"]], ["v" + c], W)
+        act(T.M[:, ch], T.TM[:, 0:2112].indirect(T.eL[:, n]), AF.Identity, TAN + [eln, "a" + N], ["M1" + c], 2 * GW)
+        pe([(r["X"], wm("FM"), T.M[:, ch, 0:W], W, "WFM"), (r["X"], wm("FM"), MA, W, "WFM"), (r["X"], wm("I"), T.lanec[:], W, "WI")],
+           ["M1" + c, "lanec", lk["X"]], [nm["X"]])
+        act(F, r["X"], AF.Identity, [nm["X"], "cF", "cF1"], ["F" + c], W, bias=(cF, cF1)[ch % 2])
+        turn(place, nm, lk, [([("pK", K), ("pF", F)], ["K" + c, "F" + c])], ch, 0)
+        dl = T.lu[:, ch, 0]
+        ts(dl, T.tT[:, ch, 0, :, 16], float(W * ch), None, AL.add, None, ["tT0" + c], ["dl" + c], 8)
+        act(sfv(ch, 0), T.ivf[:, 0:2048].indirect(el), AF.Identity, IVF + [eln], ["c32" + c], GW)
+        act(sfv(ch, 1), T.ivf[:, 0:2048].indirect(dl), AF.Identity, IVF + ["dl" + c], ["old" + c], GW)
+        pe([(r["X"], T.I37[:, 1], sfv(ch, 0), 4 * W, "WI37"), (r["X"], wm("neA"), F, W, "WneA"), (r["X"], wm("c12"), one, W, "Wc12"), (r["X"], wm("nc12"), one, W, "Wnc12"),
+            (r["X"], T.I37[:, 0], sfv(ch, 0), 4 * W, "WI37"), (r["X"], wm("eA"), F, W, "WeA")], ["c32" + c, "F" + c, "ones", lk["X"]], [nm["X"]])
+        tt(sfv(ch, 2), r["X"], sfv(ch, 1), AL.subtract, [nm["X"], "old" + c], ["diff" + c], W)
 
     def big(s, ch):
-        v = views(s, ch)
-        c, an = v["c"], v["an"]
-        Yn = ["Y%d" % q + c for q in range(4)]
-        for t in range(4):
-            b = tile[0] % 3
+        n, c, N, place, r, nm, lk, (K, MA, P0, P1) = views(s, ch)
+        for t in range(NB):
+            u = tile[0] % NTB
             tile[0] += 1
-            ps, pn = T["ps%d" % b], "ps%d" % b
-            it = []
-            for kk in range(4):
-                o = ps[:, kk * W:kk * W + W]
-                it.append((o, wm("I"), T.Y[:, ch, 4 * t + kk:2048:16], W, "WI"))
-                it.append((o, wm("nI"), sbv(ch, 1), W, "WnI"))
-            pe(it, Yn + ["mid" + c], [pn])
-            m = T.mm[:, b]
-            if s == 0:
-                ts(m, ps[:], C8, C8, AL.add, AL.is_equal, [pn], ["mm%d" % b], 512)
-            else:
-                act(T.ab[:, b], ps[:], AF.Abs, [pn], ["ab%d" % b], 512)
-                for q in range(2):
-                    tt(T.mis[:, b, 256 * q:256 * q + 256], v["abuf"][:, 0:256], T.ab[:, b, 256 * q:256 * q + 256], AL.is_lt,
-                       [an[0], an[1], "ab%d" % b], ["mis%d%d" % (b, q)], 256)
-                it = [(ps[:], wm("sI"), T.ab[:, b], 512, "WsI")]
-                if s > 1:
-                    it += [(ps[:, kk * W:kk * W + W], wm("nsI"), sbv(ch, 2), W, "WnsI") for kk in range(4)]
-                pe(it, ["ab%d" % b, "h" + c], [pn], final=False)
-                pe([(ps[:], wm("B4096"), T.mis[:, b], 512, "WB4096")], ["mis%d0" % b, "mis%d1" % b], [pn], first=False)
-                ts(m, ps[:], C8, C8, AL.add, AL.is_equal, [pn], ["mm%d" % b], 512)
-            it = [(T.ps3[:, 0:W], wm("nCB"), sbv(ch, 0), W, "WnCB")] if t == 0 else []
-            it += [(T.ps3[:, 0:W], Zs(2, 4 * t + kk)[0], T.mm[:, b, kk * W:kk * W + W], W, "Z2") for kk in range(4)]
-            pe(it, ["mm%d" % b, "core" + c], ["ps3"], first=t == 0, final=t == 3)
+            ps, pn = T["ps%d" % u], "ps%d" % u
+            lh, kh = t // 2, t % 2
+            lo, hi = 64 * lh, 64 * lh + 64
+            it = [(ps[:, :, 7 - kk], wm("I"), T.Y[:, ch, 16 * lo + 8 * kh + kk:16 * hi:16], 64, "WI") for kk in range(8)]
+            it += [(ps[:, :, j], wm("nI"), T.sb[:, ch, 0, lo:hi], 64, "WnI") if s == 0 else (ps[:, :, j], T.nI16[:], T.mh[:, ch, 1, lo:hi], 64, "WnI16")
+                   for j in range(8)]
+            pe(it, ["Y%d" % q + c for q in (2 * lh, 2 * lh + 1)] + ["mid" + c], [pn])
+            m, mn = T.tm[:, ch, lo:hi, 8 - 8 * kh:16 - 8 * kh], "tm%d" % t + c
             if s > 0:
-                it = [(T.ps4[:, 0:W], wm("n20"), sbv(ch, 0), W, "Wn20")] if t == 0 else []
-                it += [(T.ps4[:, 0:W], wm("I"), T.mm[:, b, kk * W:kk * W + W], W, "WI") for kk in range(4)]
-                pe(it, ["mm%d" % b, "core" + c], ["ps4"], first=t == 0, final=t == 3)
+                act(T.ab[:, u], ps[:], AF.Abs, [pn], ["ab%d" % u], 512)
+                ts(T.mis[:, u], T.ab[:, u], CO, TAU if s > 1 else 1.0, AL.is_equal, AL.mult, ["ab%d" % u], ["mis%d" % u], 256)
+                it = [(ps[:], wm("sI"), T.ab[:, u], 512, "WsI")]
+                if s > 1:
+                    it += [(ps[:, :, j], wm("v"), T.sb[:, ch, 12, lo:hi], 64, "Wv") for j in range(8)]
+                pe(it, ["ab%d" % u, "v" + c], [pn], final=False)
+                tn = "t2" if s > 1 else "t1"
+                pe([(ps[:], wm(tn), T.mis[:, u], 512, "W" + tn)], ["mis%d" % u], [pn], first=False)
+            ts(m, ps[:], C8 + (512.0 if s == 1 else 0.0), C8, AL.add, AL.is_equal, [pn], [mn], 512)
+            if s > 0:
+                b, q = place["N"]
+                it = [(r["N"], wm("cntK"), K, W, "WcntK")] if t == 0 else []
+                it += [(T["ps%d" % b][:, q, 4 * lh:4 * lh + 4], wm("I"), T.tm[:, ch, lo:hi, 8 - 8 * kh + j], 64, "WI") for j in range(8)]
+                pe(it, [mn, "K" + c], [nm["N"], lk["N"]], first=t == 0, final=t == NB - 1)
+            if kh:
+                b, q = place["R"]
+                o = T["ps%d" % b][:, q, 4 * lh:4 * lh + 4]
+                it = [(o, wm("hI"), T.ones[:, 0:64], 64, "WhI")]
+                it += [(o, T.Z[:, 15 - x:143 - x], T.tm[:, ch, lo + x:hi:16], 64, "Z") for x in range(16)]
+                pe(it, ["tm%d" % (t - 1) + c, mn, "ones", lk["R"]], [nm["R"] + "h%d" % lh])
+
+    def first(ch, u, rd, lst, nm):
+        dv(lambda: g.vector.tensor_tensor_scan(T.sj[:, ch, u], T.nb[:, ch, u], T.pat[:], 4096.0, AL.mult, AL.add), rd + ["pat"], ["sj%d%d" % (u, ch)], W)
+        ts(lst, T.sj[:, ch, u, 15:W:16], -4096.0, 16.0 * W, AL.add, AL.min, ["sj%d%d" % (u, ch)], [nm], 8)
 
     def post(s, ch):
-        v = views(s, ch)
-        n, c, a, an = v["n"], v["c"], v["a"], v["an"]
-        N = str(n)
+        n, c, N, place, r, nm, lk, (K, MA, P0, P1) = views(s, ch)
+        PN = "P_" + N
         lastst = s == RO - 1
-        M = T.sta[:, n, 1:256:2]
-        z, f, Og, Oq = T.sta[:, n, 512:768:2], T.sta[:, n, 513:768:2], sbv(ch, 16), sbv(ch, 17)
-        okk, sel, oj, bit, wx, sg, g2, Od, F = (sbv(ch, q) for q in range(5, 14))
-        R = T.ps3[:, 0:W]
-        w0, wn = v["w0"], v["wn"]
-        ts(okk, R, 0.0, None, AL.is_equal, None, ["ps3"], ["ok" + c], W)
-        pe([(a[3], wm("IL"), okk, W, "WIL")], ["ok" + c], [an[3]])
-        act(sel, a[3], AF.Relu, [an[3]], ["sel" + c], W)
-        tt(sfv(ch, 3), sfv(ch, 2), sel, AL.mult, ["diff" + c, "sel" + c], ["ds" + c], 2 * W)
-        extra = ["yiA"] if lastst and ch == 1 else []
-        tt(T.ivf[:, 0:2048].indirect(T.lu[:, ch, 8:16]), sfv(ch, 1), sfv(ch, 3), AL.subtract, ["old" + c, "ds" + c, "dl" + c] + extra, IVF, 4 * W)
-        if lastst:
-            for b in range(8):
-                lo = 256 * b + W * ch
-                op("S", lambda lo=lo: g.sync.dma_start(T.yi[:, lo:lo + W], T.ivf[:, lo:lo + W]), IVF, ["yiA"] if (ch == 0 and b == 7) else [], 0.1,
-                   sem=("outA" if ch == 0 else "out", 16), lat=2.5)
-        zg = sbv(ch, 14)
-        wa, wb = T.ps7[:, w0:w0 + W], T.ps7[:, w0 + W:w0 + 256]
-        pe([(wa, wm("pB"), sel, W, "WpB"), (wa, wm("I16"), T.dcon[:, 0:W], W, "WI16")], ["sel" + c, "dcon"], [wn])
-        scan2(ch, wa, W, [wn], 1)
-        cp(T.lu[:, ch, 16:24], T.sc2[:, ch, 1, 15:128:16], ["sc1" + c], ["jl" + c], 8)
-        act(z, T.Y[:, ch, 0:2048].indirect(T.lu[:, ch, 16:24]), AF.Identity, ["Y%d" % q + c for q in range(4)] + ["jl" + c], ["z" + N], 200)
+        Yn = ["Y%d" % q + c for q in range(NB)] + ["Yz"]
+        Rn = [nm["R"] + "h%d" % q for q in range(NB // 2)]
+        hh, F = sbv(ch, 1), sbv(ch, 3)
+        f, oq, tf, wx, tg, Og = (sbv(ch, q) for q in (5, 6, 7, 8, 9, 10))
+        z = wn_(ch, ZO, KO)
+        dl, jl, gl = (T.lu[:, ch, q] for q in range(3))
+        Yw = T.Y[:, ch]
+        tt(T.nb[:, ch, 0], r["R"], T.tT[:, ch, 0, :, 0:16], AL.not_equal, Rn + ["tT0" + c], ["nb" + c], W)
+        first(ch, 0, ["nb" + c], jl, "jl" + c)
+        tt(sfv(ch, 3), T.OHb[:].indirect(jl), sfv(ch, 2), AL.mult, ["OHb", "OHz", "jl" + c, "diff" + c], ["ds" + c], GW)
+        extra = ["yiA"] if lastst and ch == NCH - 1 else []
+        tt(T.ivf[:, 0:2048].indirect(dl), sfv(ch, 1), sfv(ch, 3), AL.add, ["old" + c, "ds" + c, "dl" + c] + extra, IVF, 4 * W)
+        if lastst and ch >= NCH - 2:
+            a, b = (0, 256 - W) if ch == NCH - 2 else (256 - W, 256)
+            for q in range(8):
+                op("S", lambda lo=256 * q + a, hi=256 * q + b: g.sync.dma_start(T.yi[:, lo:hi], T.ivf[:, lo:hi]), IVF, ["yiA"] if (a == 0 and q == 7) else [], 0.1,
+                   sem=("outA" if a == 0 else "out", 16), lat=2.5)
+        act(z, Yw.indirect(jl), AF.Identity, Yn + ["jl" + c], ["z" + c], GW)
+        parts = [([("fF", F), ("fZ", z)], ["F" + c, "z" + c])]
         if s > 1:
-            tt(f, a[2], z, AL.min, [an[2], "z" + N], ["zq" + N], W)
-            pe([(wb, wm("B"), f, W, "WB"), (wb, wm("nqB"), sel, W, "WnqB"), (wb, wm("nqI"), sbv(ch, 3), W, "WnqI"), (wb, wm("cqI"), T.ones[:], W, "WcqI")],
-               ["zq" + N, "sel" + c, "n2" + c, "ones"], [wn])
-            ts(sfv(ch, 6), wb, C16, -C16, AL.add, AL.add, [wn], ["rq" + c], W)
-            tt(Oq, wb, sfv(ch, 6), AL.is_equal, [wn, "rq" + c], ["oq" + N], W)
-            pe([(a[2], wm("I"), f, W, "WI"), (a[2], wm("I512"), Oq, W, "WI512")], ["zq" + N, "oq" + N], [an[2]])
-            act(T.sw[:, ch, 0, W:256], a[2], AF.Relu, [an[2]], ["tf" + c], W, bias=-383.0)
+            pe([(r["B"], wm("hI"), P0, W, "WhI"), (r["B"], wm("hI"), P1, W, "WhI"), (r["B"], wm("nI"), hh, W, "WnI")], [PN, "h" + c, lk["B"]], [nm["B"]])
+            tt(f, r["B"], z, AL.min, [nm["B"], "z" + c], ["f" + c], W)
+            pe([(r["A"], wm(x), y, W, "W" + x) for x, y in (("B", f), ("cqI", one), ("c4", one), ("nc4", one), ("nB", f), ("ncqI", one))],
+               ["f" + c, "ones", lk["A"]], [nm["A"]])
+            ts(oq, r["A"], 0.0, None, AL.is_equal, None, [nm["A"]], ["oq" + c], W)
+            tt(tf, oq, f, AL.mult, ["oq" + c, "f" + c], ["tf" + c], W)
+            parts += [([("fOq", oq), ("fTf", tf)], ["oq" + c, "tf" + c])]
         if s > 0:
-            act(sfv(ch, 4), R, AF.Relu, ["ps3"], ["Rc" + c], W, bias=0.5)
-            act(wx, T.ps4[:, 0:W], AF.Exp, ["ps4"], ["wx" + c], W, scale=math.log(32.0))
-            pe([(a[0], wm("S24"), wx, W, "WS24")], ["wx" + c], [an[0]])
-            act(sg, a[0], AF.Sign, [an[0]], ["sg" + c], W, bias=-24.0)
-            pe([(a[1], wm("hIL"), sg, W, "WhIL"), (a[1], wm("nB"), okk, W, "WnB")], ["sg" + c, "ok" + c], [an[1]])
-            act(Og, a[1], AF.Relu, [an[1], "cOg"], ["og" + N], W, bias=T.cols[:, 3:4])
-            pe([(a[0], wm("pwB"), Og, W, "WpwB")], ["og" + N], [an[0]])
-            tt(sfv(ch, 5), a[0], sfv(ch, 4), AL.mult, [an[0], "Rc" + c], ["u" + c], W)
-            ts(a[1], sfv(ch, 5), C1, -C1, AL.add, AL.add, ["u" + c], [an[1]], W)
-            tt(bit, a[1], sfv(ch, 5), AL.is_gt, [an[1], "u" + c], ["bit" + c], W)
-            pe([(a[0], wm("IL"), bit, W, "WIL")], ["bit" + c], [an[0]])
-            act(oj, a[0], AF.Relu, [an[0]], ["oj" + c], W)
-            pe([(a[1], wm("pB"), oj, W, "WpB"), (a[1], wm("I16"), T.dcon[:, 0:W], W, "WI16")], ["oj" + c, "dcon"], [an[1]])
-            scan2(ch, a[1], W, [an[1]], 2)
-            cp(T.lu[:, ch, 40:48], T.sc2[:, ch, 2, 15:128:16], ["sc2" + c], ["gl" + c], 8)
-            act(zg, T.Y[:, ch, 0:2048].indirect(T.lu[:, ch, 40:48]), AF.Identity, ["Y%d" % q + c for q in range(4)] + ["gl" + c], ["zg" + c], 200)
-        it = [(a[3], wm("y"), M, W, "Wy"), (a[3], wm("nI"), sbv(ch, 4), W, "WnI"), (a[3], wm("B4096"), sel, W, "WB4096")]
-        if s > 0:
-            it += [(a[3], wm("B4096"), Og, W, "WB4096")]
-        pe(it, ["M" + N, "ry" + c, "sel" + c, "og" + N], [an[3]])
-        act(g2, a[3], AF.Relu, [an[3]], ["g2" + c], W, scale=-2.0, bias=-1792.0)
-        ts(Od, g2, 0.5, None, AL.is_gt, None, ["g2" + c], ["Od" + c], 64)
-        tg, tf = T.sw[:, ch, 0, 0:W], T.sw[:, ch, 0, W:256]
-        cc = T.sw[:, ch, 1]
-        it = [(a[3], wm("Fd"), Od, W, "WFd"), (a[3], Zs(0, 3)[0], sel, W, "Z0"), (a[3], wm("Fm"), M, W, "WFm")]
-        rd = ["Od" + c, "sel" + c, "M" + N]
-        if s > 0:
-            it += [(a[3], wm("Fg"), Og, W, "WFg")]
-            rd += ["og" + N]
-        if s > 1:
-            it += [(a[3], wm("Ff"), Oq, W, "WFf")]
-            rd += ["oq" + N]
-        if lastst:
-            it += [(a[3], wm("Fn2"), sbv(ch, 3), W, "WFn2")]
-            rd += ["n2" + c]
-        pe(it, rd, [an[3]])
-        act(F, a[3], AF.Identity, [an[3], "cF"], ["F" + c], W, bias=T.cols[:, 6:7])
-        we, wo = T.ps7[:, w0:w0 + 256:2], T.ps7[:, w0 + 1:w0 + 256:2]
-        pe([(we, wm("keep"), F, W, "Wkeep"), (wo, wm("mM"), F, W, "WmM")], ["F" + c], [wn])
-        km = T.sw[:, ch, 2]
-        tt(km, v["w"], T.sta[:, n, 0:256], AL.mult, [wn, "K" + N, "M" + N], ["km" + c], 256)
-        if s > 0:
-            pe([(a[0], wm("I512"), Og, W, "WI512"), (a[0], wm("I"), zg, W, "WI")], ["zg" + c, "og" + N], [an[0]])
-            act(tg, a[0], AF.Relu, [an[0]], ["tg" + c], W, bias=-383.0)
-        itm = [(a[2], wm("I2"), T.sw[:, ch, 2, 1:256:2], W, "WI2"), (a[2], wm("M"), F, W, "WM"), (a[2], Zs(1, 2)[0], g2, W, "Z1")]
-        itk = [(a[3], wm("I"), T.sw[:, ch, 2, 0:256:2], W, "WI"), (a[3], wm("I256"), Od, W, "WI256"), (a[3], wm("nI"), g2, W, "WnI"), (a[3], wm("K"), F, W, "WK")]
-        rd = ["km" + c, "Od" + c, "g2" + c, "F" + c]
-        for on, tx, nm in ((s > 1, tf, "tf"), (s > 0, tg, "tg")):
-            if on:
-                itm += [(a[2], Zs(0, 2)[0], tx, W, "Z0")]
-                itk += [(a[3], wm("I"), tx, W, "WI")]
-                rd += [nm + c]
-        pe(itm, rd, [an[2]])
-        act(T.snd[:, n, 1:256:2], a[2], AF.Identity, [an[2]], ["nM" + N], W, scale=0.5, bias=-0.2)
-        pe(itk, rd, [an[3]])
-        c0, c1, crd = Og, Og, "og" + N
-        if s > 1:
-            pe([(v["w"], wm("I"), T.sta[:, n, 256:512], 256, "WI"), (we, wm("n512"), Og, W, "Wn512"), (wo, wm("n512"), Og, W, "Wn512"),
-                (we, wm("nI"), zg, W, "WnI"), (wo, wm("nI"), zg, W, "WnI")], ["P" + N, "zg" + c, "og" + N], [wn])
-            ts(cc, v["w"], C8 + 512.0, C8, AL.add, AL.is_equal, [wn], ["cc" + c], 256)
-            c0, c1, crd = T.sw[:, ch, 1, 0:256:2], T.sw[:, ch, 1, 1:256:2], "cc" + c
-        s1 = "s1L" if lastst else "s1"
-        it = [(v["w"], wm("I"), T.dcon[:], 256, "WI"), (we, wm("s0"), F, W, "Ws0"), (wo, wm(s1), F, W, "W" + s1)]
-        if lastst:
-            it += [(we, wm("nB"), c0, W, "WnB"), (wo, wm("nB2k"), c0, W, "WnB2k"), (wo, wm("nB2k"), c1, W, "WnB2k")]
-        elif s > 0:
-            it += [(we, wm("nB"), c0, W, "WnB"), (wo, wm("B"), c1, W, "WB")]
-        pe(it, ["F" + c, "dcon", crd], [wn])
-        scan2(ch, v["w"], 256, [wn], 3)
-        ts(T.lu[:, ch, 24:40], T.sc2[:, ch, 3, 15:256:16], 512.0, None, AL.min, None, ["sc3" + c], ["pl" + c], 16)
-        win = T.sta[:, n, 256:784].indirect(T.lu[:, ch, 24:40])
-        wrd = ["P" + N, "z" + N, "zq" + N, "S", "SL", "pl" + c]
+            act(wx, r["N"], AF.Exp, [nm["N"], "cx"], ["wx" + c], W, scale=16 * LB, bias=cx)
+            pe([(r["C"], wm("S25"), wx, W, "WS25")], ["wx" + c, lk["C"]], [nm["C"]])
+            ts(Og, r["C"], 0.0, None, AL.is_gt, None, [nm["C"]], ["Og" + c], W)
+            turn(place, nm, lk, [([("wT", Og)], ["Og" + c])], ch, 1)
+            tt(sfv(ch, 5), r["R"], T.tT[:, ch, 1, :, 0:16], AL.mult, Rn + ["tT1" + c], ["u" + c], W)
+            ts(r["C"], sfv(ch, 5), C1, -C1, AL.add, AL.add, ["u" + c], [nm["C"]], W)
+            tt(T.nb[:, ch, 1], r["C"], sfv(ch, 5), AL.is_le, [nm["C"], "u" + c], ["nb2" + c], W)
+            first(ch, 1, ["nb2" + c], gl, "gl" + c)
+            tt(tg, Yw.indirect(gl), Og, AL.mult, Yn + ["gl" + c, "Og" + c], ["tg" + c], GW)
+            k0, k1 = ("C", "N") if NCH == 2 else ("A", "B")
+            bank, q = T["ps%d" % place[k0][0]], place[k0][1]
+            it = [(bank[:, q:q + 2], wm("I"), T.sta[:, n, :, 2:4], 2 * W, "WI")]
+            it += [(bank[:, q:q + 2, h:MU:2], wm("n512"), Og, W, "Wn512") for h in range(2)]
+            pe(it, [PN, "Og" + c], [nm[k0], nm[k1], lk[k0]], final=False)
+            pe([(bank[:, q:q + 2, h:MU:2], wm("nI"), tg, W, "WnI") for h in range(2)], ["tg" + c], [nm[k0], nm[k1], lk[k0]], first=False)
+            ts(T.cc[:, ch], bank[:, q:q + 2], C8 + 512.0, C8, AL.add, AL.is_equal, [nm[k0], nm[k1]], ["cc" + c], 2 * W)
+            parts[0] = (parts[0][0] + [("fOg", Og)], parts[0][1] + ["Og" + c])
+            parts += [([("fTg", tg)], ["tg" + c]), ([("fC0", T.cc[:, ch, :, 0]), ("fC1", T.cc[:, ch, :, 1])], ["cc" + c])]
+            if NCH > 2:
+                parts = [(sum((x[0] for x in parts[:-1]), []), sum((x[1] for x in parts[:-1]), [])), parts[-1]]
+        else:
+            parts = [(parts[0][0] + [("fTg", tg)], parts[0][1] + ["tg" + c])]
+        turn(place, nm, lk, parts, ch, 2)
+        dv(lambda: g.vector.tensor_tensor_scan(T.sF[:, ch], T.seg[:], T.tF[:, ch], 0.0, AL.mult, AL.max), ["tT2" + c, "seg"], ["sF" + c], 2 * W)
+        x = T.sF[:, ch, 15:2 * W:32]
+        xo = -0.25 - (WS / 2, 0.0)[ch % 2]
+        wrd = ["win" + c, "z" + c, "K" + c, "wa%d" % (ch % 2), "wk%d" % (ch % 2)] + OHN[ch // 2]
+        Ww = T.win[:, ch // 2, WS * (ch % 2):WS * (ch % 2) + WS + 4096]
         if not lastst:
-            act(T.snd[:, n, 0:256:2], a[3], AF.Identity, [an[3]], ["nK" + N], W)
-            act(T.snd[:, n, 256:512], win, AF.Identity, wrd, ["nP" + N], 400)
-            mk = masks(rank, ch)
-            n2 = n + 2
-            got = sum(len(masks((rank - b) % NR, ch)[b]) for b in mk)
-            sent = sum(len(x) for x in mk.values())
-            for base, sm, rd, nxt in ((0, "ar%d" % n2, ["nK" + N, "nM" + N], ["K%d" % n2, "M%d" % n2]), (256, "ap%d" % n2, ["nP" + N], ["P%d" % n2])):
-                def go(mk=mk, n=n, n2=n2, ch=ch, base=base, sm=sm):
+            ts(T.eS[:, n, 0:MU], x, 0.5, xo, AL.mult, AL.add, ["sF" + c], ["eS" + N], 8)
+            cp(T.eS[:, n, MU:2 * MU], T.sF[:, ch, 3:2 * W:32], ["sF" + c], ["aS" + N], 8)
+            cp(T.la[:, ch], T.sF[:, ch, 7:2 * W:8], ["sF" + c], ["la" + c], 32)
+            act(T.snd[:, n], Ww.indirect(T.la[:, ch]), AF.Identity, wrd + ["la" + c], ["snd" + N], 4 * GW)
+            n2 = n + NCH
+            calls = [(T.eS, T.eL, 1, (0,), "ar%d" % n2, ["eS" + N], ["e%d" % n2]), (T.snd, T.sta, 64, (0,), "ap%d" % n2, ["snd" + N], ["P_%d" % n2]),
+                     (T.eS, T.eL, 1, (MU,), "aa%d" % n2, ["aS" + N], ["a%d" % n2])]
+            if NCH > 2:
+                calls = [(T.eS, T.eL, 1, (0, MU), "ar%d" % n2, ["eS" + N, "aS" + N], ["e%d" % n2, "a%d" % n2]), calls[1]]
+            for src, dst, u, offs, sm, rd, nxt in calls:
+                mk = masks(rank, ch, len(offs))
+                got = sum(len(masks((rank - y[0]) % NR, ch, len(offs))[y]) for y in mk)
+                sent = sum(len(v) for v in mk.values())
+
+                def go(src=src, dst=dst, u=u, offs=offs, sm=sm, mk=mk):
                     trs = []
-                    for b in sorted(mk):
+                    for b, q in sorted(mk):
                         rid, pid, _ = topo.addr(cores[(rank + b) % NR])
-                        lo = base + 64 * (b - 4 * ch)
-                        trs.append(RemoteDMATransfer(dst_ids=[DstId(rid=rid, pnc=pid)], dma_engine_mask=sum(1 << e for e in mk[b]), remote_sem=T.sem[sm],
-                                                     src=T.snd[:, n, lo:lo + 64], dst=T.sta[:, n2, lo:lo + 64]))
+                        lo = offs[q] + 2 * (b - NB * ch)
+                        trs.append(RemoteDMATransfer(dst_ids=[DstId(rid=rid, pnc=pid)], dma_engine_mask=sum(1 << e for e in mk[b, q]), remote_sem=T.sem[sm],
+                                                     src=src[:, n, u * lo:u * (lo + 2)], dst=dst[:, n2, lo:lo + 2]))
                     g.remote_dma_fused(trs, local_sem=T.sem.loc)
                     return None
                 if ch == 0:
-                    op("S", lambda n=n, n2=n2, base=base: g.sync.dma_start(T.sta[:, n2, base:base + 64], T.snd[:, n, base:base + 64]), rd, [], 0.1,
-                       sem=(sm, 16), lat=2.0)
-                op("G", go, rd, nxt, 1.0, sem=(sm, got, sent), lat=3.2)
+                    for o in offs:
+                        op("S", lambda src=src, dst=dst, u=u, o=o: g.sync.dma_start(dst[:, n2, o:o + 2], src[:, n, o:o + 2 * u]), rd, [], 0.1, sem=(sm, 16), lat=2.0)
+                op("G", go, rd, nxt, GI, sem=(sm, got, sent), lat=LAT)
         else:
             lo = ch * W
-            act(T.oy[:, ch], win, AF.Identity, wrd, ["oy" + c], 400, bias=128.0)
-            for q in range(2):
-                cp(T.oyy[:, q, lo:lo + W], T.oy[:, ch, q:256:2], ["oy" + c], ["oyy%d" % q + c], 64)
-            act(T.ok_[:, lo:lo + W], a[3], AF.Identity, [an[3]], ["oK" + c], W, bias=128.0)
-            nM = T.snd[:, n, 1:256:2]
-            wa, wb = T.ps7[:, w0:w0 + W], T.ps7[:, w0 + W:w0 + 256]
-            pe([(wa, wm("e"), nM, W, "We"), (wa, wm("I"), T.econ[:], W, "WI")], ["nM" + N, "econ"], [wn])
-            pe([(wb, wm("a"), nM, W, "Wa"), (wb, wm("I"), T.econ[:], W, "WI")], ["nM" + N, "econ"], [wn])
-            scan(ch, v["w"], 256, [wn])
-            ts(T.oe[:, 0, 8 * ch:8 * ch + 8], T.scn[:, ch, 15:128:16], -16512.0, None, AL.add, None, ["scn" + c], ["oe" + c], 8)
-            ts(T.oe[:, 1, 8 * ch:8 * ch + 8], T.scn[:, ch, 143:256:16], -128.0, None, AL.add, None, ["scn" + c], ["oa" + c], 8)
-            if ch == 1:
-                for eng, q, dst, src, rd in (("A", g.scalar, T.yk, T.ok_[:], "oK"), ("S", g.sync, T.y0, T.oyy[:, 0], "oyy0"), ("A", g.scalar, T.y1, T.oyy[:, 1], "oyy1"),
-                                             ("S", g.sync, T.ye, T.oe[:, 0], "oe"), ("A", g.scalar, T.ya, T.oe[:, 1], "oa")):
-                    op(eng, lambda q=q, dst=dst, src=src: q.dma_start(dst[:], src), [rd + "0", rd + "1"], [], 0.1, sem=("out", 16), lat=2.0)
+            for q, y, u, x2 in ((0, 3, 2, "kM"), (1, 23, 0, "mid"), (2, 31, 4, "rr"), (3, 7, 11, "kk"), (4, 15, 12, "v")):
+                ll = T.lu[:, ch, 3 + q]
+                cp(ll, T.sF[:, ch, y:2 * W:32], ["sF" + c], ["ll%d" % q + c], 8)
+                act(sbv(ch, u), (Ww if q else T.TM[:, 0:2112]).indirect(ll), AF.Identity, wrd + TAN + ["ll%d" % q + c], [x2 + c], GW, bias=128.0 if q > 2 else 0.0)
+            tt(sbv(ch, 11), sbv(ch, 11), sbv(ch, 12), AL.max, ["kk" + c, "v" + c], ["kk" + c], W)
+            ts(T.ok_[:, lo:lo + W], sbv(ch, 11), -1.0, None, AL.max, None, ["kk" + c], ["oK" + c], W // 2)
+            for q, u, x2, k in ((0, 0, "mid", "A"), (1, 4, "rr", "B")):
+                pe([(r[k], wm("Y%d" % q), sbv(ch, 2), W, "WY%d" % q)], ["kM" + c, lk[k]], [nm[k]])
+                tt(sbv(ch, 5 + q), r[k], sbv(ch, u), AL.min, [nm[k], x2 + c], [("f", "oq")[q] + c], W)
+                act(T.oy[:, q, lo:lo + W], sbv(ch, 5 + q), AF.Identity, [("f", "oq")[q] + c], ["oy%d" % q + c], W, bias=128.0)
+            o8 = slice(MU * ch, MU * ch + MU)
+            ts(T.oe[:, 2, o8], x, 0.5, xo, AL.mult, AL.add, ["sF" + c], ["oh" + c], 8)
+            ts(T.oe[:, 0, o8], T.oe[:, 2, o8], C1, -C1, AL.add, AL.add, ["oh" + c], ["oe" + c], 8)
+            ts(T.oe[:, 1, o8], T.sF[:, ch, 11:2 * W:32], C1, -C1, AL.add, AL.add, ["sF" + c], ["oa" + c], 8)
+            if ch == NCH - 1:
+                for eng, q, dst, src, rd in (("A", g.scalar, T.yk, T.ok_[:], "oK"), ("S", g.sync, T.y0, T.oy[:, 0], "oy0"), ("A", g.scalar, T.y1, T.oy[:, 1], "oy1"),
+                                             ("S", g.sync, T.ye, T.oe[:, 0], "oe"), ("S", g.sync, T.ya, T.oe[:, 1], "oa")):
+                    op(eng, lambda q=q, dst=dst, src=src: q.dma_start(dst[:], src), [rd + str(y) for y in range(NCH)], [], 0.1, sem=("out", 16), lat=2.0)
 
     for s in range(RO):
-        for nm, fn, ch in (("p", prep, 0), ("p", prep, 1), ("b", big, 0), ("q", post, 0), ("b", big, 1), ("q", post, 1)):
+        for nm, fn, ch in [("p", prep, ch) for ch in range(NCH)] + [x for ch in range(NCH) for x in (("b", big, ch), ("q", post, ch))]:
             phase[0] = nm + str(ch)
             fn(s, ch)
-    assert len(slot) <= NW
+    assert len(slot) <= NW and len(tslot) <= NT
     return ops
 
 
 def schedule(ops):
     n = len(ops)
+    pred = [sorted(o["deps"]) for o in ops]
     succ = [[] for _ in range(n)]
-    for i, o in enumerate(ops):
-        for d in o["deps"]:
-            succ[d].append(i)
-    HOP = 0.12
-    pr = [0.0] * n
-    for i in range(n - 1, -1, -1):
-        pr[i] = ops[i]["dur"] + ops[i]["lat"] + max([pr[j] + HOP for j in succ[i]], default=0.0)
-    x, look, amp, bonus = SEED
     for i in range(n):
-        x = (x * 1103515245 + 12345) % 2147483648
-        pr[i] += amp * x / 2147483648 + bonus.get(ops[i]["ph"], 0.0)
-    pred = [list(o["deps"]) for o in ops]
+        for d in pred[i]:
+            succ[d].append(i)
 
-    def run(before, after, prio, back):
+    def gap(i, j):
+        return ops[i]["lat"] + (0.0 if ops[i]["eng"] == "P" and ops[j]["eng"] == "P" else HOP)
+
+    def where(v, x):
+        lo, hi = 0, len(v)
+        while lo < hi:
+            m = (lo + hi) // 2
+            if v[m] < x:
+                lo = m + 1
+            else:
+                hi = m
+        return lo
+
+    def place(keys, back):
+        before, after = (succ, pred) if back else (pred, succ)
         left = [len(p) for p in before]
-        base = [0.0] * n
-        ready = [i for i in range(n) if left[i] == 0]
-        for i in ready:
-            base[i] = ops[i]["lat"] if back else 0.0
-        free = {}
-        done = [0.0] * n
-        bank = {}
-        order = []
-        extra = []
-        while ready:
-            st = {}
-            for i in ready:
-                o = ops[i]
-                t = max(base[i], free.get(o["eng"], 0.0))
-                for b in o["banks"]:
-                    for e, j in bank.get(b, {}).items():
-                        if e != o["eng"] and done[j] + HOP > t:
-                            t = done[j] + HOP
-                st[i] = t
-            t0 = min(st.values()) + look
-            i = max([q for q in ready if st[q] <= t0], key=lambda q: (prio[q], -q))
+        heap = sorted((keys[i], i) for i in range(n) if left[i] == 0)
+        busy = {}
+        st = [0.0] * n
+        while heap:
+            i = heap.pop(0)[1]
             o = ops[i]
-            for b in o["banks"]:
-                extra.extend((i, j) for e, j in bank.get(b, {}).items() if e != o["eng"])
-                bank.setdefault(b, {})[o["eng"]] = i
-            free[o["eng"]] = st[i] + o["dur"]
-            done[i] = st[i] + o["dur"] + (0.0 if back else o["lat"])
-            order.append(i)
-            ready.remove(i)
+            d = o["dur"]
+            t = o["lat"] if back else 0.0
+            for j in before[i]:
+                t = max(t, st[j] + ops[j]["dur"] + (gap(i, j) if back else gap(j, i)))
+            rows = [(busy.setdefault(o["eng"], []), 0.0)] + [(v, HOP) for b in o["banks"] for e, v in busy.setdefault(b, {}).items() if e != o["eng"]]
+            moved = True
+            while moved:
+                moved = False
+                for v, m in rows:
+                    k = where(v, (t - m,))
+                    if k and v[k - 1][1] + m > t + 1e-9:
+                        t = v[k - 1][1] + m
+                        moved = True
+                    elif k < len(v) and v[k][0] < t + d + m - 1e-9:
+                        t = v[k][1] + m
+                        moved = True
+            st[i] = t
+            for v in [busy[o["eng"]]] + [busy[b].setdefault(o["eng"], []) for b in o["banks"]]:
+                v.insert(where(v, (t, t + d)), (t, t + d))
             for j in after[i]:
-                t = done[i] + (0.0 if (o["eng"] == "P" and ops[j]["eng"] == "P") else HOP) + (ops[j]["lat"] if back else 0.0)
-                if t > base[j]:
-                    base[j] = t
                 left[j] -= 1
                 if left[j] == 0:
-                    ready.append(j)
-        return order, done, extra
-    best = None
-    for rnd in range(ROUNDS[0] + 1):
-        order, done, extra = run(pred, succ, pr, False)
-        if best is None or max(done) < max(best[1]):
-            best = (order, done, extra)
-        if rnd < ROUNDS[0]:
-            pr = run(succ, pred, done, True)[1]
-    order, done, extra = best
-    for i, j in extra:
-        ops[i]["deps"].add(j)
-    for i in range(n):
-        ops[i]["t"] = done[i] - ops[i]["dur"] - ops[i]["lat"]
-    return order, max(done)
+                    heap.insert(where(heap, (keys[j], j)), (keys[j], j))
+        return st, max(st[i] + ops[i]["dur"] + (0.0 if back else ops[i]["lat"]) for i in range(n))
+
+    seed = [SEED[0]]
+
+    def rnd():
+        seed[0] = (seed[0] * 1103515245 + 12345) % 2147483648
+        return seed[0] / 2147483648
+
+    def search():
+        keys = [0.0] * n
+        for i in range(n - 1, -1, -1):
+            keys[i] = min([keys[j] - ops[i]["lat"] - HOP for j in succ[i]], default=-ops[i]["lat"]) - ops[i]["dur"]
+        keys = [keys[i] - SEED[2].get(ops[i]["ph"], 0.0) for i in range(n)]
+        best = None
+        for r in range(ROUNDS[0]):
+            st, end = place(keys, False)
+            if best is None or end < best[1]:
+                best = (st, end)
+            sb = place([-(st[i] + ops[i]["dur"]) for i in range(n)], True)[0]
+            keys = [-(sb[i] + ops[i]["dur"]) + SEED[1] * rnd() for i in range(n)]
+        sends = [i for i in range(n) if ops[i]["eng"] == "G" and ops[i]["sem"]]
+        st, end = best
+        for r in range(ROUNDS[1]):
+            k = list(st)
+            kind = rnd()
+            if kind < 0.5:
+                for q in range(1 + int(3 * rnd())):
+                    k[int(n * rnd())] += 5 * rnd() - 2.5
+            elif kind < 0.8:
+                i, d = int(n * rnd()), 0.3 + 2.7 * rnd()
+                stack, seen = [i], set()
+                while stack:
+                    a = stack.pop()
+                    if a not in seen and st[a] >= st[i] - 2 * d:
+                        seen.add(a)
+                        k[a] -= d
+                        stack.extend(pred[a])
+            else:
+                a, d, amp = end * rnd(), 1 + 5 * rnd(), 0.4 + 0.8 * rnd()
+                k = [x + amp * (rnd() - 0.5) if a < x < a + d else x for x in k]
+            s2, e2 = place(k, False)
+            if e2 + 0.02 * sum(s2[i] for i in sends) <= end + 0.02 * sum(st[i] for i in sends):
+                st, end = s2, e2
+        return st, end
+
+    if not KEPT:
+        KEPT.append(search())
+    st, end = KEPT[0]
+    order = sorted(range(n), key=lambda i: (st[i], i))
+    bank = {}
+    for i in order:
+        ops[i]["t"] = st[i]
+        for b in ops[i]["banks"]:
+            ops[i]["deps"].update(j for e, j in bank.get(b, {}).items() if e != ops[i]["eng"])
+            bank.setdefault(b, {})[ops[i]["eng"]] = i
+    return order, end
 
 
 def emit(g, T, ops, order):

@@ -10,11 +10,11 @@ W = 256 // NCH
 MU = W // 16
 NB = 8 // NCH
 WS = 64 + 6 * W
-NW = 36
+NW = 34
 NT = 11
-YE = ['ADAAADAA', 'ADDAADAA', 'ADAAADAA', 'ADAAADAA', 'DADAAADA']
+YE = ['ADAAADAA'] * 5
 SEED = [5158, 0.2, {'p0': 9.6, 'p1': 1.4, 'b0': 9.8, 'b1': -0.1, 'q0': 9.3, 'q1': 4.6, 'set': 11.9}]
-ROUNDS = [4, 3000]
+ROUNDS = [6, 16000]
 KEPT = []
 SCL = 1.25
 C8 = 100663304.0
@@ -28,23 +28,23 @@ ALF = 2.0 ** -10
 CO = 1432.0
 TAU = 187.0
 LB = math.log(1.8)
-NTB = 4 if NCH == 2 else 3
+NTB = 4
 
 SCRATCH = {
     "stb": ("sbuf", [128, 4096], "bfloat16"), "ivi": ("sbuf", [128, 2048], "int32"), "ivf": ("sbuf", [128, 2048], "float32"),
     "e0i": ("sbuf", [128, 16], "int32"), "e0u": ("sbuf", [128, 16], "uint16"),
     "sta": ("sbuf", [128, 5 * NCH, MU, 4, 16], "bfloat16"), "snd": ("sbuf", [128, 4 * NCH, 4 * W], "bfloat16"),
-    "win": ("sbuf", [128, NCH // 2, 2 * WS + 4096], "bfloat16"),
+    "win": ("sbuf", [128, 2 * WS + 4096], "bfloat16"),
     "eL": ("sbuf", [128, 5 * NCH, 2 * MU], "uint16"), "eS": ("sbuf", [128, 4 * NCH, 2 * MU], "uint16"),
     "Wm": ("sbuf", [128, NW, 8, 16], "bfloat16"), "Tm": ("sbuf", [128, NT, 2, 4, 32], "bfloat16"), "BP": ("sbuf", [128, 2, 4, 16], "bfloat16"),
-    "Z": ("sbuf", [128, 144], "bfloat16"), "I37": ("sbuf", [128, 2, 128], "float32"), "nI16": ("sbuf", [128, 128], "float16"),
+    "Z": ("sbuf", [128, 144], "bfloat16"), "I37": ("sbuf", [128, 2, 128], "float16"), "nI16": ("sbuf", [128, 128], "float16"),
     "ones": ("sbuf", [128, 128], "bfloat16"), "cols": ("sbuf", [128, 40], "float32"), "colb": ("sbuf", [128, 8], "bfloat16"), "coli": ("sbuf", [128, 8], "int32"),
     "E16": ("sbuf", [128, 16], "float32"), "NK": ("sbuf", [128, 16], "float32"),
     "itr": ("sbuf", [128, 256], "bfloat16"), "itl": ("sbuf", [128, 256], "bfloat16"), "itm": ("sbuf", [128, W], "bfloat16"),
     "TM": ("sbuf", [128, 2112], "bfloat16"), "M": ("sbuf", [128, NCH, 2 * W], "bfloat16"), "OHb": ("sbuf", [128, 16 * W + 16], "bfloat16"),
     "lanec": ("sbuf", [128, W], "bfloat16"), "pat": ("sbuf", [128, W], "float32"), "seg": ("sbuf", [128, 2 * W], "bfloat16"),
     "Y": ("sbuf", [128, NCH, 16 * W + 16], "bfloat16"), "tm": ("sbuf", [128, NCH, W, 16], "bfloat16"),
-    "mis": ("sbuf", [128, NTB, 64, 8], "bfloat16"), "ab": ("sbuf", [128, NTB, 64, 8], "bfloat16"), "mh": ("sbuf", [128, NCH, 2, W], "float16"),
+    "mis": ("sbuf", [128, NTB, 64, 8], "bfloat16"), "ab": ("sbuf", [128, NTB, 64, 8], "bfloat16"), "mh": ("sbuf", [128, NCH, 3, W], "float16"),
     "c16": ("sbuf", [128, NCH, W], "uint16"), "lu": ("sbuf", [128, NCH, 8, MU], "uint16"), "la": ("sbuf", [128, NCH, 4 * MU], "uint16"),
     "nb": ("sbuf", [128, NCH, 2, W], "bfloat16"), "sj": ("sbuf", [128, NCH, 2, W], "float32"),
     "tT": ("sbuf", [128, NCH, 2, MU, 32], "float32"), "tF": ("sbuf", [128, NCH, 2 * W], "float32"), "sF": ("sbuf", [128, NCH, 2 * W], "float32"),
@@ -55,10 +55,9 @@ for _b in range(NTB):
     SCRATCH["ps%d" % _b] = ("psum", [128, 64, 8], "float32")
 for _b in range(NTB, 8):
     SCRATCH["ps%d" % _b] = ("psum", [128, 512 // W, MU, 16], "float32")
-SEMAPHORES = ["sP", "sD", "sA", "sG", "le0", "liv", "lst", "out", "outA", "loc", "oh"] + ["wn%d" % _n for _n in range(5 * NCH)]
-SEMAPHORES += [_k + str(_n) for _k in ("ar", "ap", "aa")[:2 + (NCH == 2)] for _n in range(NCH, 5 * NCH)]
+SEMAPHORES = ["sP", "sD", "sA", "sG", "le0", "liv", "lst", "out", "outA", "loc", "ohb"] + ["wn%d" % _n for _n in range(5 * NCH)]
+SEMAPHORES += [_k + str(_n) for _k in ("ar", "ap") for _n in range(NCH, 5 * NCH)]
 
-FAC = 1.0
 LAT = 5.0
 HOP = 0.17
 GI = 1.0
@@ -93,13 +92,13 @@ def build(g, core, T, topo):
         return tuple(sorted(set(int(x[2]) for x in names if x.startswith("ps"))))
 
     def dv(fn, rd, wr, cyc):
-        return op("D", fn, rd, wr, 0.06 + max(cyc, 64) * 0.83e-3 * FAC, bk(*rd, *wr))
+        return op("D", fn, rd, wr, 0.06 + max(cyc, 64) * 0.83e-3, bk(*rd, *wr))
 
     def ac(fn, rd, wr, cyc):
-        return op("A", fn, rd, wr, 0.08 + max(cyc, 64) * 0.83e-3 * FAC, bk(*rd, *wr))
+        return op("A", fn, rd, wr, 0.08 + max(cyc, 64) * 0.83e-3, bk(*rd, *wr))
 
     def po(fn, rd, wr, n):
-        return op("G", fn, rd, wr, (0.17 + 2 * n * 0.83e-3) * FAC)
+        return op("G", fn, rd, wr, 0.17 + 2 * n * 0.83e-3)
 
     def ts(out, in0, s1, s2, o0, o1, rd, wr, cyc):
         if o1 is None:
@@ -125,9 +124,7 @@ def build(g, core, T, topo):
                 r = g.tensor.matmul(it[0], it[1], it[2], first and q == 0, final and q == len(items) - 1)
             return r
         cyc = sum(max(64, it[3]) for it in items)
-        n = op("P", fn, list(rd) + [it[4] for it in items], wr, 0.03 + cyc * 0.417e-3 * FAC, bk(*wr))
-        ops[n]["nmm"] = len(items)
-        return n
+        return op("P", fn, list(rd) + [it[4] for it in items], wr, 0.03 + cyc * 0.417e-3, bk(*wr))
 
     def iota(out, pat, base, cm, wr, n):
         return po(lambda: g.iota(out, pat, base, cm, allow_small_or_imprecise_dtypes=True), [], wr, n)
@@ -135,8 +132,8 @@ def build(g, core, T, topo):
     GW = int(1.56 * W)
 
     op("S", lambda: g.sync.dma_start(T.e0i[:], T.e0[:]), [], ["e0i"], 0.1, sem=("le0", 16), lat=2.0)
-    op("S", lambda: g.sync.dma_start(T.ivi[:], T.iv[:]), [], ["ivi"], 0.1, sem=("liv", 16), lat=6.0)
-    op("A", lambda: g.scalar.dma_start(T.stb[:], T.st[:]), [], ["stb"], 0.1, sem=("lst", 16), lat=7.0)
+    op("S", lambda: g.sync.dma_start(T.ivi[:], T.iv[:]), [], ["ivi"], 0.1, sem=("liv", 16), lat=5.5)
+    op("S", lambda: g.sync.dma_start(T.stb[:], T.st[:]), [], ["stb"], 0.1, sem=("lst", 16), lat=6.8)
 
     slot = {}
     tslot = {}
@@ -197,17 +194,20 @@ def build(g, core, T, topo):
         else:
             ts(wm(name), wm(base), v, None, AL.mult, None, ["W" + base] + list(rd), ["W" + name], 64)
 
-    for nm, v in (("nI", -1.0), ("midK", -2.0 ** -44), ("midC", -65536.0), ("hI", 0.5), ("FM", 1.0)):
+    for nm, v in (("nI", -1.0), ("hI", 0.5), ("FM", 1.0)):
         scaled(nm, "I", v, eng="D")
-    for nm, v in (("midC2", -131072.0), ("vK", 2.0 ** -37), ("vC", 2.0 ** 23), ("sI", SCL), ("cntK", -20 * 2.0 ** -60), ("n512", -512.0), ("I25", 2.5), ("nhI", -0.5)):
+    for nm, v in (("midK", -2.0 ** -44), ("midC2", -131072.0), ("vK", 2.0 ** -37), ("vC", 2.0 ** 23), ("sI", SCL), ("cntK", -20 * 2.0 ** -60), ("n512", -512.0),
+                  ("I25", 2.5), ("nhI", -0.5), ("c12", 1.5 * 2.0 ** 35), ("nc12", -1.5 * 2.0 ** 35), ("c4", C16), ("nc4", -C16)):
         scaled(nm, "I", v)
     scaled("cqI", "I", cq, ["cq"])
+    scaled("ncqI", "I", pcol, ["pcol"])
+    scaled("nB", "B", -1.0)
     ts(T.nI16[:], wm("I"), -1.0, None, AL.mult, None, ["WI"], ["WnI16"], 64)
     for nm, v, d in (("t1", -512.0, -2304.0), ("t2", -2.0, 219 * 256.0), ("v", TAU * 2.0 ** -22, -SCL)):
         scaled(nm, "B", v)
         po(lambda nm=nm, d=d: g.affine_select(wm(nm), wm(nm), [[-1, 128]], AL.not_equal, d, 0, 1), ["W" + nm], ["W" + nm], 128)
     for q in range(2):
-        act(T.I37[:, q], wm("I"), AF.Identity, ["WI"], ["WI37"], 128, scale=37.0 - 74.0 * q)
+        ts(T.I37[:, q], wm("I"), 37.0 - 74.0 * q, None, AL.mult, None, ["WI"], ["WI37"], 64)
     tt(wm("S25"), wm("I25"), wm("B"), AL.subtract, ["WI25", "WB"], ["WS25"], 128)
     G8 = T.Wm[:, slot["B"], :, 0]
     ms(T.Z[:], 0.0, ["Z"], 72)
@@ -236,21 +236,20 @@ def build(g, core, T, topo):
     S = slice
     ZO, KO = 64 + 4 * W, 64 + 5 * W
     ent("FM", [(1, 0, 1, 640), (2, 0, 1, 5), (4, 0, 1, 1)])
-    scaled("eA", "B", lin("ceA", [(1, 128), (2, 1), (4, 1)]), ["ceA"])
-    scaled("neA", "B", lin("cneA", [(1, -128), (2, -1), (4, -1), (7, 2048), (10, -0.5)]), ["cneA"])
-    for nm, v in (("c12", 1.5 * 2.0 ** 35), ("nc12", -1.5 * 2.0 ** 35), ("c4", C16), ("nc4", -C16)):
-        scaled(nm, "I", v)
-    scaled("nB", "B", -1.0)
-    scaled("ncqI", "I", pcol, ["pcol"])
+    ceA = lin("ceA", [(1, 128), (2, 1), (4, 1), (11, 2048)])
+    scaled("eA", "B", ceA, ["ceA"])
+    cneA = lin("cneA", [(7, 2048), (10, -0.5)])
+    act(cneA, ceA, AF.Identity, ["ceA", "cneA"], ["cneA"], 1, scale=-1.0, bias=cneA)
+    scaled("neA", "B", cneA, ["cneA"])
     tent("pF", [(3, S(16, 17), 256), (9, S(16, 17), 1)])
     tent("fF", [(1, S(12, 13), 256), (1, S(15, 16), 1280), (2, S(12, 13), 2), (2, S(15, 16), 10), (4, S(15, 16), 2), (0, S(15, 16), -2),
-                (4, S(0, 4), 1), (4, S(8, 12), 1), (8, S(21, 23), 48), (8, S(30, 31), 48), (9, S(4, 6), 1), (9, S(20, 23), 1), (9, S(28, 31), 1),
-                (5, S(0, 1), PB), (5, S(20, 32, 8), PB), (12, S(1, 2), PB), (12, S(21, 32, 8), PB), (6, S(4, 13, 4), PB), (6, S(2, 3), -16), (13, S(10, 15, 4), PB),
-                (7, S(2, 3), -PB), (7, S(5, 14, 4), -PB), (7, S(22, 32, 8), -PB), (7, S(11, 16, 4), -2 * PB),
-                (10, S(0, 1), 2080), (10, S(1, 2), 2096), (10, S(2, 4), 2048), (10, S(4, 6), KO), (10, S(7, 8), 24), (10, S(12, 16), WS),
-                (10, S(20, 21), ZO), (10, S(21, 31, 9), 96), (10, S(22, 23), 112), (10, S(23, 32, 8), 16), (10, S(28, 30), ZO),
-                (11, S(3, 4), 1), (11, S(10, 12), 1), (11, S(15, 16), 786432), (15, S(15, 16), 2),
-                (14, S(4, 8), 4096), (14, S(12, 16), -WS), (14, S(20, 24), 4096), (14, S(28, 32), 4096)])
+                (4, S(0, 4), 1), (4, S(8, 12), 1), (8, S(21, 23), 48), (8, S(26, 31, 4), 48), (9, S(4, 7, 2), 1), (9, S(20, 23), 1), (9, S(25, 27), 1), (9, S(28, 31), 1),
+                (5, S(0, 1), PB), (5, S(20, 32, 8), PB), (12, S(1, 2), PB), (12, S(21, 32, 4), PB), (6, S(4, 13, 4), PB), (6, S(2, 3), -16), (6, S(26, 27), -PB),
+                (13, S(9, 14, 4), PB), (7, S(2, 32, 4), -PB), (7, S(11, 16, 4), -2 * PB),
+                (10, S(0, 1), 2080), (10, S(1, 2), 2096), (10, S(2, 4), 2048), (10, S(4, 7, 2), KO), (10, S(7, 8), 24), (10, S(12, 16), WS),
+                (10, S(20, 26, 5), ZO), (10, S(21, 31, 9), 96), (10, S(22, 27, 4), 112), (10, S(23, 32, 4), 16), (10, S(28, 30), ZO),
+                (11, S(3, 4), 1), (11, S(9, 12, 2), 1), (11, S(15, 16), 786432), (11, S(26, 27), -3 * PB), (15, S(15, 16), 2),
+                (14, S(4, 8), 4096), (14, S(12, 16), -WS), (14, S(20, 32), 4096)])
     ms(T.Tm[:, 2:5], 0.0, TN("pK") + TN("fZ") + TN("fTg"), 128 * 3)
     ms(T.Tm[:, 5:NT], 0.0, TN("wT") + TN("fOg") + TN("fC0") + TN("fC1") + TN("fOq") + TN("fTf"), 128 * (NT - 5))
     for h in range(2):
@@ -260,29 +259,25 @@ def build(g, core, T, topo):
     act(ea, E(0), AF.Identity, ["E16"], ["ea"], 1, scale=ALF)
     act(ena, E(0), AF.Identity, ["E16"], ["ena"], 1, scale=-ALF)
     for name, ents in (("pF", [(S(0, 16), cpF, "cpF")]), ("pK", [(S(0, 16), p2k, "p2k")]),
-                       ("fZ", [(S(0, 2), ea, "ea"), (S(4, 13, 4), ea, "ea"), (S(10, 15, 4), ea, "ea"), (S(20, 22), ea, "ea"), (S(28, 30), ea, "ea"),
-                               (S(2, 3), ena, "ena"), (S(5, 14, 4), ena, "ena"), (S(11, 16, 4), ena, "ena"), (S(22, 32, 8), ena, "ena")]),
-                       ("fTg", [(S(13, 14), 1.0, None), (S(2, 3), ALF, None), (S(5, 10, 4), ALF, None), (S(22, 32, 8), ALF, None), (S(11, 16, 4), -ALF, None)]),
-                       ("wT", [(S(0, 16), p2n, "p2n")]), ("fOg", [(S(13, 14), c256, "c256")]),
-                       ("fC0", [(S(2, 3), 16.0, None), (S(22, 23), -16.0, None)]), ("fC1", [(S(2, 31, 28), 16.0, None)]),
-                       ("fOq", [(S(14, 15), c256, "c256")]), ("fTf", [(S(14, 15), 1.0, None)])):
+                       ("fZ", [(S(0, 32, 4), ea, "ea"), (S(1, 32, 4), ea, "ea"), (S(2, 32, 4), ena, "ena"), (S(11, 16, 4), ena, "ena")]),
+                       ("fTg", [(S(2, 32, 4), ALF, None), (S(14, 15), 1.0, None), (S(11, 16, 4), -ALF, None)]),
+                       ("wT", [(S(0, 16), p2n, "p2n")]), ("fOg", [(S(14, 15), c256, "c256")]),
+                       ("fC0", [(S(2, 3), 16.0, None), (S(22, 23), -16.0, None), (S(26, 27), PB, None)]),
+                       ("fC1", [(S(2, 31, 28), 16.0, None), (S(26, 27), PB, None)]),
+                       ("fOq", [(S(13, 14), c256, "c256")]), ("fTf", [(S(13, 14), 1.0, None)])):
         k = tmx(name)
         for sl, v, nm in ents:
             wn = ["T%s:%d" % (name, y) for y in range(32)[sl]]
             act(T.Tm[:, k, :, :, sl], T.BP[:, :, :, 0:len(wn)], AF.Identity, ["BP0", "BP1"] + ([nm] if nm else []), wn, 8 * len(wn), scale=v)
-    scaled("Y0", "B", lin("cY0", [(7, -129), (5, -256)]), ["cY0"])
-    scaled("Y1", "B", lin("cY1", [(7, -129), (6, -256)]), ["cY1"])
 
     ts(T.NK[:], T.E16[:], -1.0, -KN, AL.add, AL.mult, ["E16"], ["NK"], 16)
     for q in range(16):
-        o = T.win[:, 0, WS + 256 * q:WS + 256 * q + 256]
+        o = T.win[:, WS + 256 * q:WS + 256 * q + 256]
         if q % 3 == 2:
             act(o, T.itl[:], AF.Identity, ["itl", "E16", "NK"], ["OH%d" % q], 256, scale=E(q), bias=T.NK[:, q:q + 1])
         else:
             ts(o, T.itl[:], E(q), T.NK[:, q:q + 1], AL.mult, AL.add, ["itl", "E16", "NK"], ["OH%d" % q], 128)
-    OHN = [["OH%d" % q for q in range(16)], ["OHc"]]
-    if NCH > 2:
-        op("S", lambda: g.sync.dma_start(T.win[:, 1, WS:WS + 4096], T.win[:, 0, WS:WS + 4096]), OHN[0] + ["stb"], ["OHc"], 0.1, sem=("oh", 16), lat=5.0)
+    OHN = ["OH%d" % q for q in range(16)]
     d2, d4, d8 = col(), col(), col()
     ts(d2, E(1), 2.0, E(3), AL.mult, AL.add, ["E16"], ["d2"], 1)
     act(d4, d2, AF.Identity, ["d2"], ["d4"], 1, scale=2.0)
@@ -291,9 +286,8 @@ def build(g, core, T, topo):
     for n, c, nm in ((128, E(1), "E16"), (256, d2, "d2"), (512, d4, "d4"), (1024, d8, "d8")):
         ts(T.TM[:, n:2 * n], T.TM[:, 0:n], c, None, AL.add, None, ["TM", nm], ["TM"], n // 2)
     ts(T.OHb[:, 0:256], T.itr[:], pcol, None, AL.is_equal, None, ["itr", "pcol"], ["OHb"], 128)
-    for n in (256, 512, 1024):
-        if n < 16 * W:
-            cp(T.OHb[:, n:2 * n], T.OHb[:, 0:n], ["OHb"], ["OHb"], n // 2)
+    for n in range(256, 16 * W, 256):
+        op("S", lambda n=n: g.sync.dma_start(T.OHb[:, n:n + 256], T.OHb[:, 0:256]), ["OHb", "stb"], ["OHc"] if n == 16 * W - 256 else [], 0.1, sem=("ohb", 16), lat=2.5)
     ms(T.OHb[:, 16 * W:16 * W + 16], 0.0, ["OHz"], 16)
     ms(T.Y[:, :, 16 * W:16 * W + 16], ZN, ["Yz"], 32)
     ms(T.pat[:], 1.0, ["pat"], W)
@@ -316,13 +310,12 @@ def build(g, core, T, topo):
     TAN = ["TM"] + ["TA%d" % q for q in range(4)]
 
     def wn_(ch, a, b):
-        o = (WS + 4096) * (ch % 2)
-        return T.win[:, ch // 2, o + a:o + b]
+        o = (WS + 4096) * ch
+        return T.win[:, o + a:o + b]
 
-    for par in range(2):
-        o = (WS + 4096) * par
-        ms(T.win[:, :, o:o + 24], AB, ["wa%d" % par], 24)
-        ms(T.win[:, :, o + 24:o + 64], KN, ["wk%d" % par], 40)
+    for ch in range(NCH):
+        ms(wn_(ch, 0, 24), AB, ["wa%d" % ch], 24)
+        ms(wn_(ch, 24, 64), KN, ["wk%d" % ch], 40)
 
     def sfv(ch, q):
         return T.sf[:, ch, q]
@@ -335,9 +328,7 @@ def build(g, core, T, topo):
     ms(T.eL[:, 0:NCH, MU:2 * MU], 2048, ["a%d" % q for q in range(NCH)], 16)
     ms(T.sb[:, :, 9], ZN / 16, ["tg%d" % q for q in range(NCH)], 128)
     for ch in range(NCH):
-        c = str(ch)
-        act(wn_(ch, KO, WS), T.win[:, 0, WS:WS + 4096].indirect(T.e0u[:, MU * ch:MU * ch + MU]), AF.Identity, OHN[0] + ["x0u"], ["K" + c], GW)
-        ms(T.sta[:, ch], AB, ["P_" + c], 2 * W)
+        act(wn_(ch, KO, WS), T.win[:, WS:WS + 4096].indirect(T.e0u[:, MU * ch:MU * ch + MU]), AF.Identity, OHN + ["x0u"], ["K%d" % ch], GW)
     for q in range(4):
         cp(T.ivf[:, q * 512:q * 512 + 512], T.ivi[:, q * 512:q * 512 + 512], ["ivi"], ["ivf%d" % q], 512)
     IVF = ["ivf%d" % q for q in range(4)]
@@ -367,10 +358,7 @@ def build(g, core, T, topo):
 
     def views(s, ch):
         n = NCH * s + ch
-        if NCH == 2:
-            place = {"R": (4 + ch, 0), "X": (4 + ch, 1), "T": (4 + ch, 2), "A": (6 + ch, 0), "B": (6 + ch, 1), "C": (6 + ch, 2), "N": (6 + ch, 3)}
-        else:
-            place = {"R": (4 + ch, 0), "X": (4 + ch, 1), "T": (4 + ch, 2), "A": (4 + ch, 4), "B": (4 + ch, 5), "C": (4 + ch, 6), "N": (3, 0)}
+        place = {"R": (4 + ch, 0), "X": (4 + ch, 1), "T": (4 + ch, 2), "A": (6 + ch, 0), "B": (6 + ch, 1), "C": (6 + ch, 2), "N": (6 + ch, 3)}
         r = {k: T["ps%d" % b][:, q] for k, (b, q) in place.items()}
         nm = {k: "ps%dq%d" % v for k, v in place.items()}
         lk = {k: "lk%d" % v[0] for k, v in place.items()}
@@ -402,13 +390,10 @@ def build(g, core, T, topo):
                 ts(T.Y[:, ch, 512 * q:512 * q + 512], src, -128.0, None, AL.add, None, ["stb", "c16" + c], ["Y%d" % q + c], 800)
             else:
                 act(T.Y[:, ch, 512 * q:512 * q + 512], src, AF.Identity, ["stb", "c16" + c], ["Y%d" % q + c], 800, bias=-128.0)
-        op("S", lambda: g.sync.dma_start(wn_(ch, 64, ZO), T.sta[:, n]), [PN], ["win" + c], 0.1, sem=("wn" + N, 16), lat=2.0)
-        mid, hh, F, rr = (sbv(ch, q) for q in (0, 1, 3, 4))
-        it = [(r["A"], wm("hI"), P0, W, "WhI"), (r["A"], wm("hI"), P1, W, "WhI")] if s > 1 else [(r["A"], wm("I"), P0, W, "WI")]
-        if s == 0:
-            pe([(r["A"], wm("midK"), K, W, "WmidK"), (r["A"], wm("midC"), one, W, "WmidC")] + it, [PN, "K" + c, "ones", lk["A"]], [nm["A"]])
-            tt(mid, r["A"], K, AL.max, [nm["A"], "K" + c], ["mid" + c], W)
-        else:
+        op("S", lambda: g.sync.dma_start(wn_(ch, 64, ZO), T.sta[:, n] if s else T.stb[:, 0:4 * W]), [PN if s else "stb"], ["win" + c], 0.1, sem=("wn" + N, 16), lat=2.0)
+        hh, F = sbv(ch, 1), sbv(ch, 3)
+        if s > 0:
+            it = [(r["A"], wm("hI"), P0, W, "WhI"), (r["A"], wm("hI"), P1, W, "WhI")] if s > 1 else [(r["A"], wm("I"), P0, W, "WI")]
             Kk, Ox = T.sta[:, n, :, 0], T.sta[:, n, :, 1]
             pe([(r["A"], wm("midK"), Kk, W, "WmidK"), (r["A"], wm("midK"), Ox, W, "WmidK"), (r["A"], wm("midC2"), one, W, "WmidC2")] + it,
                [PN, "ones", lk["A"]], [nm["A"]])
@@ -423,14 +408,15 @@ def build(g, core, T, topo):
         act(T.M[:, ch], T.TM[:, 0:2112].indirect(T.eL[:, n]), AF.Identity, TAN + [eln, "a" + N], ["M1" + c], 2 * GW)
         pe([(r["X"], wm("FM"), T.M[:, ch, 0:W], W, "WFM"), (r["X"], wm("FM"), MA, W, "WFM"), (r["X"], wm("I"), T.lanec[:], W, "WI")],
            ["M1" + c, "lanec", lk["X"]], [nm["X"]])
-        act(F, r["X"], AF.Identity, [nm["X"], "cF", "cF1"], ["F" + c], W, bias=(cF, cF1)[ch % 2])
+        act(F, r["X"], AF.Identity, [nm["X"], "cF", "cF1"], ["F" + c], W, bias=(cF, cF1)[ch])
         turn(place, nm, lk, [([("pK", K), ("pF", F)], ["K" + c, "F" + c])], ch, 0)
         dl = T.lu[:, ch, 0]
         ts(dl, T.tT[:, ch, 0, :, 16], float(W * ch), None, AL.add, None, ["tT0" + c], ["dl" + c], 8)
-        act(sfv(ch, 0), T.ivf[:, 0:2048].indirect(el), AF.Identity, IVF + [eln], ["c32" + c], GW)
+        ch16 = T.mh[:, ch, 2]
+        ts(ch16, T.c16[:, ch], -2048.0, None, AL.add, None, ["c16" + c], ["c32" + c], W // 2)
         act(sfv(ch, 1), T.ivf[:, 0:2048].indirect(dl), AF.Identity, IVF + ["dl" + c], ["old" + c], GW)
-        pe([(r["X"], T.I37[:, 1], sfv(ch, 0), 4 * W, "WI37"), (r["X"], wm("neA"), F, W, "WneA"), (r["X"], wm("c12"), one, W, "Wc12"), (r["X"], wm("nc12"), one, W, "Wnc12"),
-            (r["X"], T.I37[:, 0], sfv(ch, 0), 4 * W, "WI37"), (r["X"], wm("eA"), F, W, "WeA")], ["c32" + c, "F" + c, "ones", lk["X"]], [nm["X"]])
+        pe([(r["X"], T.I37[:, 1], ch16, W, "WI37"), (r["X"], wm("neA"), F, W, "WneA"), (r["X"], wm("c12"), one, W, "Wc12"), (r["X"], wm("nc12"), one, W, "Wnc12"),
+            (r["X"], T.I37[:, 0], ch16, W, "WI37"), (r["X"], wm("eA"), F, W, "WeA")], ["c32" + c, "F" + c, "ones", lk["X"]], [nm["X"]])
         tt(sfv(ch, 2), r["X"], sfv(ch, 1), AL.subtract, [nm["X"], "old" + c], ["diff" + c], W)
 
     def big(s, ch):
@@ -442,9 +428,9 @@ def build(g, core, T, topo):
             lh, kh = t // 2, t % 2
             lo, hi = 64 * lh, 64 * lh + 64
             it = [(ps[:, :, 7 - kk], wm("I"), T.Y[:, ch, 16 * lo + 8 * kh + kk:16 * hi:16], 64, "WI") for kk in range(8)]
-            it += [(ps[:, :, j], wm("nI"), T.sb[:, ch, 0, lo:hi], 64, "WnI") if s == 0 else (ps[:, :, j], T.nI16[:], T.mh[:, ch, 1, lo:hi], 64, "WnI16")
+            it += [(ps[:, :, j], wm("nI"), wn_(ch, KO + lo, KO + hi), 64, "WnI") if s == 0 else (ps[:, :, j], T.nI16[:], T.mh[:, ch, 1, lo:hi], 64, "WnI16")
                    for j in range(8)]
-            pe(it, ["Y%d" % q + c for q in (2 * lh, 2 * lh + 1)] + ["mid" + c], [pn])
+            pe(it, ["Y%d" % q + c for q in (2 * lh, 2 * lh + 1)] + ["mid" + c if s else "K" + c], [pn])
             m, mn = T.tm[:, ch, lo:hi, 8 - 8 * kh:16 - 8 * kh], "tm%d" % t + c
             if s > 0:
                 act(T.ab[:, u], ps[:], AF.Abs, [pn], ["ab%d" % u], 512)
@@ -485,22 +471,21 @@ def build(g, core, T, topo):
         Yw = T.Y[:, ch]
         tt(T.nb[:, ch, 0], r["R"], T.tT[:, ch, 0, :, 0:16], AL.not_equal, Rn + ["tT0" + c], ["nb" + c], W)
         first(ch, 0, ["nb" + c], jl, "jl" + c)
-        tt(sfv(ch, 3), T.OHb[:].indirect(jl), sfv(ch, 2), AL.mult, ["OHb", "OHz", "jl" + c, "diff" + c], ["ds" + c], GW)
+        tt(sfv(ch, 3), T.OHb[:].indirect(jl), sfv(ch, 2), AL.mult, ["OHb", "OHc", "OHz", "jl" + c, "diff" + c], ["ds" + c], GW)
         extra = ["yiA"] if lastst and ch == NCH - 1 else []
         tt(T.ivf[:, 0:2048].indirect(dl), sfv(ch, 1), sfv(ch, 3), AL.add, ["old" + c, "ds" + c, "dl" + c] + extra, IVF, 4 * W)
-        if lastst and ch >= NCH - 2:
-            a, b = (0, 256 - W) if ch == NCH - 2 else (256 - W, 256)
+        if lastst:
             for q in range(8):
-                op("S", lambda lo=256 * q + a, hi=256 * q + b: g.sync.dma_start(T.yi[:, lo:hi], T.ivf[:, lo:hi]), IVF, ["yiA"] if (a == 0 and q == 7) else [], 0.1,
-                   sem=("outA" if a == 0 else "out", 16), lat=2.5)
+                op("S", lambda lo=256 * q + W * ch: g.sync.dma_start(T.yi[:, lo:lo + W], T.ivf[:, lo:lo + W]), IVF, ["yiA"] if (ch == 0 and q == 7) else [], 0.1,
+                   sem=("outA" if ch == 0 else "out", 16), lat=2.5)
         act(z, Yw.indirect(jl), AF.Identity, Yn + ["jl" + c], ["z" + c], GW)
         parts = [([("fF", F), ("fZ", z)], ["F" + c, "z" + c])]
         if s > 1:
             pe([(r["B"], wm("hI"), P0, W, "WhI"), (r["B"], wm("hI"), P1, W, "WhI"), (r["B"], wm("nI"), hh, W, "WnI")], [PN, "h" + c, lk["B"]], [nm["B"]])
             tt(f, r["B"], z, AL.min, [nm["B"], "z" + c], ["f" + c], W)
-            pe([(r["A"], wm(x), y, W, "W" + x) for x, y in (("B", f), ("cqI", one), ("c4", one), ("nc4", one), ("nB", f), ("ncqI", one))],
-               ["f" + c, "ones", lk["A"]], [nm["A"]])
-            ts(oq, r["A"], 0.0, None, AL.is_equal, None, [nm["A"]], ["oq" + c], W)
+            pe([(r["X"], wm(x), y, W, "W" + x) for x, y in (("B", f), ("cqI", one), ("c4", one), ("nc4", one), ("nB", f), ("ncqI", one))],
+               ["f" + c, "ones", lk["X"]], [nm["X"]])
+            ts(oq, r["X"], 0.0, None, AL.is_equal, None, [nm["X"]], ["oq" + c], W)
             tt(tf, oq, f, AL.mult, ["oq" + c, "f" + c], ["tf" + c], W)
             parts += [([("fOq", oq), ("fTf", tf)], ["oq" + c, "tf" + c])]
         if s > 0:
@@ -513,36 +498,32 @@ def build(g, core, T, topo):
             tt(T.nb[:, ch, 1], r["C"], sfv(ch, 5), AL.is_le, [nm["C"], "u" + c], ["nb2" + c], W)
             first(ch, 1, ["nb2" + c], gl, "gl" + c)
             tt(tg, Yw.indirect(gl), Og, AL.mult, Yn + ["gl" + c, "Og" + c], ["tg" + c], GW)
-            k0, k1 = ("C", "N") if NCH == 2 else ("A", "B")
-            bank, q = T["ps%d" % place[k0][0]], place[k0][1]
+            bank, q = T["ps%d" % place["C"][0]], place["C"][1]
             it = [(bank[:, q:q + 2], wm("I"), T.sta[:, n, :, 2:4], 2 * W, "WI")]
             it += [(bank[:, q:q + 2, h:MU:2], wm("n512"), Og, W, "Wn512") for h in range(2)]
-            pe(it, [PN, "Og" + c], [nm[k0], nm[k1], lk[k0]], final=False)
-            pe([(bank[:, q:q + 2, h:MU:2], wm("nI"), tg, W, "WnI") for h in range(2)], ["tg" + c], [nm[k0], nm[k1], lk[k0]], first=False)
-            ts(T.cc[:, ch], bank[:, q:q + 2], C8 + 512.0, C8, AL.add, AL.is_equal, [nm[k0], nm[k1]], ["cc" + c], 2 * W)
+            pe(it, [PN, "Og" + c], [nm["C"], nm["N"], lk["C"]], final=False)
+            pe([(bank[:, q:q + 2, h:MU:2], wm("nI"), tg, W, "WnI") for h in range(2)], ["tg" + c], [nm["C"], nm["N"], lk["C"]], first=False)
+            ts(T.cc[:, ch], bank[:, q:q + 2], C8 + 512.0, C8, AL.add, AL.is_equal, [nm["C"], nm["N"]], ["cc" + c], 2 * W)
             parts[0] = (parts[0][0] + [("fOg", Og)], parts[0][1] + ["Og" + c])
             parts += [([("fTg", tg)], ["tg" + c]), ([("fC0", T.cc[:, ch, :, 0]), ("fC1", T.cc[:, ch, :, 1])], ["cc" + c])]
-            if NCH > 2:
-                parts = [(sum((x[0] for x in parts[:-1]), []), sum((x[1] for x in parts[:-1]), [])), parts[-1]]
         else:
             parts = [(parts[0][0] + [("fTg", tg)], parts[0][1] + ["tg" + c])]
         turn(place, nm, lk, parts, ch, 2)
         dv(lambda: g.vector.tensor_tensor_scan(T.sF[:, ch], T.seg[:], T.tF[:, ch], 0.0, AL.mult, AL.max), ["tT2" + c, "seg"], ["sF" + c], 2 * W)
         x = T.sF[:, ch, 15:2 * W:32]
-        xo = -0.25 - (WS / 2, 0.0)[ch % 2]
-        wrd = ["win" + c, "z" + c, "K" + c, "wa%d" % (ch % 2), "wk%d" % (ch % 2)] + OHN[ch // 2]
-        Ww = T.win[:, ch // 2, WS * (ch % 2):WS * (ch % 2) + WS + 4096]
+        xo = -0.25 - (WS / 2, 0.0)[ch]
+        if lastst:
+            ms(wn_(ch, 16, 24), -129.0, ["wa" + c], 8)
+        wrd = ["win" + c, "z" + c, "K" + c, "wa" + c, "wk" + c] + OHN
+        Ww = T.win[:, WS * ch:WS * ch + WS + 4096]
         if not lastst:
+            cp(T.la[:, ch], T.sF[:, ch, 7:2 * W:8], ["sF" + c], ["la" + c], 32)
             ts(T.eS[:, n, 0:MU], x, 0.5, xo, AL.mult, AL.add, ["sF" + c], ["eS" + N], 8)
             cp(T.eS[:, n, MU:2 * MU], T.sF[:, ch, 3:2 * W:32], ["sF" + c], ["aS" + N], 8)
-            cp(T.la[:, ch], T.sF[:, ch, 7:2 * W:8], ["sF" + c], ["la" + c], 32)
             act(T.snd[:, n], Ww.indirect(T.la[:, ch]), AF.Identity, wrd + ["la" + c], ["snd" + N], 4 * GW)
             n2 = n + NCH
-            calls = [(T.eS, T.eL, 1, (0,), "ar%d" % n2, ["eS" + N], ["e%d" % n2]), (T.snd, T.sta, 64, (0,), "ap%d" % n2, ["snd" + N], ["P_%d" % n2]),
-                     (T.eS, T.eL, 1, (MU,), "aa%d" % n2, ["aS" + N], ["a%d" % n2])]
-            if NCH > 2:
-                calls = [(T.eS, T.eL, 1, (0, MU), "ar%d" % n2, ["eS" + N, "aS" + N], ["e%d" % n2, "a%d" % n2]), calls[1]]
-            for src, dst, u, offs, sm, rd, nxt in calls:
+            for src, dst, u, offs, sm, rd, nxt in ((T.eS, T.eL, 1, (0, MU), "ar%d" % n2, ["eS" + N, "aS" + N], ["e%d" % n2, "a%d" % n2]),
+                                                   (T.snd, T.sta, 64, (0,), "ap%d" % n2, ["snd" + N], ["P_%d" % n2])):
                 mk = masks(rank, ch, len(offs))
                 got = sum(len(masks((rank - y[0]) % NR, ch, len(offs))[y]) for y in mk)
                 sent = sum(len(v) for v in mk.values())
@@ -562,16 +543,13 @@ def build(g, core, T, topo):
                 op("G", go, rd, nxt, GI, sem=(sm, got, sent), lat=LAT)
         else:
             lo = ch * W
-            for q, y, u, x2 in ((0, 3, 2, "kM"), (1, 23, 0, "mid"), (2, 31, 4, "rr"), (3, 7, 11, "kk"), (4, 15, 12, "v")):
-                ll = T.lu[:, ch, 3 + q]
-                cp(ll, T.sF[:, ch, y:2 * W:32], ["sF" + c], ["ll%d" % q + c], 8)
-                act(sbv(ch, u), (Ww if q else T.TM[:, 0:2112]).indirect(ll), AF.Identity, wrd + TAN + ["ll%d" % q + c], [x2 + c], GW, bias=128.0 if q > 2 else 0.0)
-            tt(sbv(ch, 11), sbv(ch, 11), sbv(ch, 12), AL.max, ["kk" + c, "v" + c], ["kk" + c], W)
-            ts(T.ok_[:, lo:lo + W], sbv(ch, 11), -1.0, None, AL.max, None, ["kk" + c], ["oK" + c], W // 2)
-            for q, u, x2, k in ((0, 0, "mid", "A"), (1, 4, "rr", "B")):
-                pe([(r[k], wm("Y%d" % q), sbv(ch, 2), W, "WY%d" % q)], ["kM" + c, lk[k]], [nm[k]])
-                tt(sbv(ch, 5 + q), r[k], sbv(ch, u), AL.min, [nm[k], x2 + c], [("f", "oq")[q] + c], W)
-                act(T.oy[:, q, lo:lo + W], sbv(ch, 5 + q), AF.Identity, [("f", "oq")[q] + c], ["oy%d" % q + c], W, bias=128.0)
+            for q, y in enumerate((7, 15, 23, 27)):
+                cp(T.lu[:, ch, 3 + q], T.sF[:, ch, y:2 * W:32], ["sF" + c], ["ll%d" % q + c], 8)
+            act(sbv(ch, 11), Ww.indirect(T.lu[:, ch, 3]), AF.Identity, wrd + ["ll0" + c], ["kk" + c], GW)
+            tt(sbv(ch, 12), Ww.indirect(T.lu[:, ch, 4]), sbv(ch, 11), AL.max, wrd + ["ll1" + c, "kk" + c], ["v" + c], GW)
+            ts(T.ok_[:, lo:lo + W], sbv(ch, 12), 128.0, -1.0, AL.add, AL.max, ["v" + c], ["oK" + c], W // 2)
+            for q in range(2):
+                act(T.oy[:, q, lo:lo + W], Ww.indirect(T.lu[:, ch, 5 + q]), AF.Identity, wrd + ["ll%d" % (2 + q) + c], ["oy%d" % q + c], GW, bias=128.0)
             o8 = slice(MU * ch, MU * ch + MU)
             ts(T.oe[:, 2, o8], x, 0.5, xo, AL.mult, AL.add, ["sF" + c], ["oh" + c], 8)
             ts(T.oe[:, 0, o8], T.oe[:, 2, o8], C1, -C1, AL.add, AL.add, ["oh" + c], ["oe" + c], 8)
@@ -600,35 +578,46 @@ def schedule(ops):
     def gap(i, j):
         return ops[i]["lat"] + (0.0 if ops[i]["eng"] == "P" and ops[j]["eng"] == "P" else HOP)
 
-    def where(v, x):
-        lo, hi = 0, len(v)
-        while lo < hi:
-            m = (lo + hi) // 2
-            if v[m] < x:
-                lo = m + 1
-            else:
-                hi = m
-        return lo
+    dur = [o["dur"] for o in ops]
+    lat = [o["lat"] for o in ops]
+    own = [[o["eng"]] + [(b, o["eng"]) for b in o["banks"]] for o in ops]
+    other = [[(b, e) for b in o["banks"] for e in "PDA" if e != o["eng"]] for o in ops]
+    edges = ([[(j, dur[j] + gap(j, i)) for j in pred[i]] for i in range(n)], [[(j, dur[j] + gap(i, j)) for j in succ[i]] for i in range(n)])
 
-    def place(keys, back):
-        before, after = (succ, pred) if back else (pred, succ)
-        left = [len(p) for p in before]
-        heap = sorted((keys[i], i) for i in range(n) if left[i] == 0)
-        busy = {}
+    def place(keys, back, old=None, since=0.0):
+        after = pred if back else succ
+        before = edges[back]
+        busy = {k: [] for o in own for k in o}
+        busy.update({k: [] for o in other for k in o})
         st = [0.0] * n
+        left = [len(p) for p in before]
+        kept = [False] * n
+        if old:
+            for i in old[1]:
+                if old[0][i] >= since:
+                    break
+                kept[i] = True
+                st[i] = old[0][i]
+                for k in own[i]:
+                    busy[k].append((st[i], st[i] + dur[i]))
+                for j in after[i]:
+                    left[j] -= 1
+        heap = sorted(((keys[i], i) for i in range(n) if left[i] == 0 and not kept[i]), reverse=True)
         while heap:
-            i = heap.pop(0)[1]
-            o = ops[i]
-            d = o["dur"]
-            t = o["lat"] if back else 0.0
-            for j in before[i]:
-                t = max(t, st[j] + ops[j]["dur"] + (gap(i, j) if back else gap(j, i)))
-            rows = [(busy.setdefault(o["eng"], []), 0.0)] + [(v, HOP) for b in o["banks"] for e, v in busy.setdefault(b, {}).items() if e != o["eng"]]
+            i = heap.pop()[1]
+            d = dur[i]
+            t = lat[i] if back else 0.0
+            for j, x in before[i]:
+                if st[j] + x > t:
+                    t = st[j] + x
+            rows = [(busy[own[i][0]], 0.0)] + [(busy[k], HOP) for k in other[i]]
             moved = True
             while moved:
                 moved = False
                 for v, m in rows:
-                    k = where(v, (t - m,))
+                    k = len(v)
+                    while k and v[k - 1][0] >= t - m:
+                        k -= 1
                     if k and v[k - 1][1] + m > t + 1e-9:
                         t = v[k - 1][1] + m
                         moved = True
@@ -636,13 +625,20 @@ def schedule(ops):
                         t = v[k][1] + m
                         moved = True
             st[i] = t
-            for v in [busy[o["eng"]]] + [busy[b].setdefault(o["eng"], []) for b in o["banks"]]:
-                v.insert(where(v, (t, t + d)), (t, t + d))
+            for k in own[i]:
+                v = busy[k]
+                q = len(v)
+                while q and v[q - 1][0] > t:
+                    q -= 1
+                v.insert(q, (t, t + d))
             for j in after[i]:
                 left[j] -= 1
                 if left[j] == 0:
-                    heap.insert(where(heap, (keys[j], j)), (keys[j], j))
-        return st, max(st[i] + ops[i]["dur"] + (0.0 if back else ops[i]["lat"]) for i in range(n))
+                    q = len(heap)
+                    while q and heap[q - 1][0] < keys[j]:
+                        q -= 1
+                    heap.insert(q, (keys[j], j))
+        return st, max(st[i] + dur[i] + (0.0 if back else lat[i]) for i in range(n))
 
     seed = [SEED[0]]
 
@@ -653,25 +649,27 @@ def schedule(ops):
     def search():
         keys = [0.0] * n
         for i in range(n - 1, -1, -1):
-            keys[i] = min([keys[j] - ops[i]["lat"] - HOP for j in succ[i]], default=-ops[i]["lat"]) - ops[i]["dur"]
+            keys[i] = min([keys[j] - lat[i] - HOP for j in succ[i]], default=-lat[i]) - dur[i]
         keys = [keys[i] - SEED[2].get(ops[i]["ph"], 0.0) for i in range(n)]
         best = None
         for r in range(ROUNDS[0]):
             st, end = place(keys, False)
             if best is None or end < best[1]:
                 best = (st, end)
-            sb = place([-(st[i] + ops[i]["dur"]) for i in range(n)], True)[0]
-            keys = [-(sb[i] + ops[i]["dur"]) + SEED[1] * rnd() for i in range(n)]
+            sb = place([-(st[i] + dur[i]) for i in range(n)], True)[0]
+            keys = [-(sb[i] + dur[i]) + SEED[1] * rnd() for i in range(n)]
         sends = [i for i in range(n) if ops[i]["eng"] == "G" and ops[i]["sem"]]
         st, end = best
+        old = (st, sorted(range(n), key=lambda i: st[i]))
         for r in range(ROUNDS[1]):
             k = list(st)
             kind = rnd()
+            i = int(n * rnd())
             if kind < 0.5:
-                for q in range(1 + int(3 * rnd())):
-                    k[int(n * rnd())] += 5 * rnd() - 2.5
+                k[i] += 5 * rnd() - 2.5
+                since = min(k[i], st[i])
             elif kind < 0.8:
-                i, d = int(n * rnd()), 0.3 + 2.7 * rnd()
+                d = 0.3 + 2.7 * rnd()
                 stack, seen = [i], set()
                 while stack:
                     a = stack.pop()
@@ -679,18 +677,21 @@ def schedule(ops):
                         seen.add(a)
                         k[a] -= d
                         stack.extend(pred[a])
+                since = st[i] - 3 * d
             else:
-                a, d, amp = end * rnd(), 1 + 5 * rnd(), 0.4 + 0.8 * rnd()
+                a, d, amp = st[i], 1 + 5 * rnd(), 0.4 + 0.8 * rnd()
                 k = [x + amp * (rnd() - 0.5) if a < x < a + d else x for x in k]
-            s2, e2 = place(k, False)
+                since = a - amp
+            s2, e2 = place(k, False, old, since)
             if e2 + 0.02 * sum(s2[i] for i in sends) <= end + 0.02 * sum(st[i] for i in sends):
                 st, end = s2, e2
+                old = (st, sorted(range(n), key=lambda i: st[i]))
         return st, end
 
     if not KEPT:
         KEPT.append(search())
     st, end = KEPT[0]
-    order = sorted(range(n), key=lambda i: (st[i], i))
+    order = sorted(range(n), key=lambda i: (i - 3 if i < 3 else st[i], i))
     bank = {}
     for i in order:
         ops[i]["t"] = st[i]

import math
from concourse.bass import DstId, RemoteDMATransfer
from concourse.mybir import dt, AluOpType, AxisListType, ActivationFunctionType

AL = AluOpType
AF = ActivationFunctionType
RO = 5
NCH = 2
W = 256 // NCH
MU = W // 16
NB = 8 // NCH
WS = 64 + 6 * W
NW = 34
NT = 11
YE = ['ADAAADAA'] * 5
SEED = [5158, 0.2, {'p0': 9.6, 'p1': 1.4, 'b0': 9.8, 'b1': -0.1, 'q0': 9.3, 'q1': 4.6, 'set': 11.9}]
ROUNDS = [6, 16000]
KEPT = []
SCL = 1.25
C8 = 100663304.0
C1 = 12582912.0
C16 = 201326592.0
KN = -2.0 ** 60
AB = 32768.0
ZN = -2.0 ** 23
PB = 8192.0
ALF = 2.0 ** -10
CO = 1432.0
TAU = 187.0
LB = math.log(1.8)
NTB = 4

SCRATCH = {
    "stb": ("sbuf", [128, 4096], "bfloat16"), "ivi": ("sbuf", [128, 2048], "int32"), "ivf": ("sbuf", [128, 2048], "float32"),
    "e0i": ("sbuf", [128, 16], "int32"), "e0u": ("sbuf", [128, 16], "uint16"),
    "sta": ("sbuf", [128, 5 * NCH, MU, 4, 16], "bfloat16"), "snd": ("sbuf", [128, 4 * NCH, 4 * W], "bfloat16"),
    "win": ("sbuf", [128, 2 * WS + 4096], "bfloat16"),
    "eL": ("sbuf", [128, 5 * NCH, 2 * MU], "uint16"), "eS": ("sbuf", [128, 4 * NCH, 2 * MU], "uint16"),
    "Wm": ("sbuf", [128, NW, 8, 16], "bfloat16"), "Tm": ("sbuf", [128, NT, 2, 4, 32], "bfloat16"), "BP": ("sbuf", [128, 2, 4, 16], "bfloat16"),
    "Z": ("sbuf", [128, 144], "bfloat16"), "I37": ("sbuf", [128, 2, 128], "float16"), "nI16": ("sbuf", [128, 128], "float16"),
    "ones": ("sbuf", [128, 128], "bfloat16"), "cols": ("sbuf", [128, 40], "float32"), "colb": ("sbuf", [128, 8], "bfloat16"), "coli": ("sbuf", [128, 8], "int32"),
    "E16": ("sbuf", [128, 16], "float32"), "NK": ("sbuf", [128, 16], "float32"),
    "itr": ("sbuf", [128, 256], "bfloat16"), "itl": ("sbuf", [128, 256], "bfloat16"), "itm": ("sbuf", [128, W], "bfloat16"),
    "TM": ("sbuf", [128, 2112], "bfloat16"), "M": ("sbuf", [128, NCH, 2 * W], "bfloat16"), "OHb": ("sbuf", [128, 16 * W + 16], "bfloat16"),
    "lanec": ("sbuf", [128, W], "bfloat16"), "pat": ("sbuf", [128, W], "float32"), "seg": ("sbuf", [128, 2 * W], "bfloat16"),
    "Y": ("sbuf", [128, NCH, 16 * W + 16], "bfloat16"), "tm": ("sbuf", [128, NCH, W, 16], "bfloat16"),
    "mis": ("sbuf", [128, NTB, 64, 8], "bfloat16"), "ab": ("sbuf", [128, NTB, 64, 8], "bfloat16"), "mh": ("sbuf", [128, NCH, 3, W], "float16"),
    "c16": ("sbuf", [128, NCH, W], "uint16"), "lu": ("sbuf", [128, NCH, 8, MU], "uint16"), "la": ("sbuf", [128, NCH, 4 * MU], "uint16"),
    "nb": ("sbuf", [128, NCH, 2, W], "bfloat16"), "sj": ("sbuf", [128, NCH, 2, W], "float32"),
    "tT": ("sbuf", [128, NCH, 2, MU, 32], "float32"), "tF": ("sbuf", [128, NCH, 2 * W], "float32"), "sF": ("sbuf", [128, NCH, 2 * W], "float32"),
    "sf": ("sbuf", [128, NCH, 6, W], "float32"), "sb": ("sbuf", [128, NCH, 13, W], "bfloat16"), "cc": ("sbuf", [128, NCH, MU, 2, 16], "bfloat16"),
    "ok_": ("sbuf", [128, 256], "bfloat16"), "oy": ("sbuf", [128, 2, 256], "bfloat16"), "oe": ("sbuf", [128, 3, 16], "float32"),
}
for _b in range(NTB):
    SCRATCH["ps%d" % _b] = ("psum", [128, 64, 8], "float32")
for _b in range(NTB, 8):
    SCRATCH["ps%d" % _b] = ("psum", [128, 512 // W, MU, 16], "float32")
SEMAPHORES = ["sP", "sD", "sA", "sG", "le0", "liv", "lst", "out", "outA", "loc", "ohb"] + ["wn%d" % _n for _n in range(5 * NCH)]
SEMAPHORES += [_k + str(_n) for _k in ("ar", "ap") for _n in range(NCH, 5 * NCH)]

LAT = 5.0
HOP = 0.17
GI = 1.0


def build(g, core, T, topo):
    ops = []
    last_w = {}
    readers = {}
    phase = ["set"]

    def op(eng, fn, rd, wr, dur, banks=(), sem=None, lat=0.0):
        n = len(ops)
        deps = set()
        for r in rd:
            if r in last_w:
                deps.add(last_w[r])
        for w in wr:
            if w in last_w:
                deps.add(last_w[w])
            deps.update(readers.get(w, ()))
        for r in rd:
            readers.setdefault(r, []).append(n)
        for w in wr:
            last_w[w] = n
            readers[w] = []
        deps.discard(n)
        ops.append({"ph": phase[0], "eng": eng, "fn": fn, "deps": deps, "dur": dur, "banks": tuple(banks), "sem": sem, "lat": lat, "wr": wr})
        return n

    def bk(*names):
        return tuple(sorted(set(int(x[2]) for x in names if x.startswith("ps"))))

    def dv(fn, rd, wr, cyc):
        return op("D", fn, rd, wr, 0.06 + max(cyc, 64) * 0.83e-3, bk(*rd, *wr))

    def ac(fn, rd, wr, cyc):
        return op("A", fn, rd, wr, 0.08 + max(cyc, 64) * 0.83e-3, bk(*rd, *wr))

    def po(fn, rd, wr, n):
        return op("G", fn, rd, wr, 0.17 + 2 * n * 0.83e-3)

    def ts(out, in0, s1, s2, o0, o1, rd, wr, cyc):
        if o1 is None:
            return dv(lambda: g.vector.tensor_scalar(out, in0, s1, None, o0), rd, wr, cyc)
        return dv(lambda: g.vector.tensor_scalar(out, in0, s1, s2, o0, o1), rd, wr, cyc)

    def tt(out, a, b, o, rd, wr, cyc):
        return dv(lambda: g.vector.tensor_tensor(out, a, b, o), rd, wr, cyc)

    def cp(out, a, rd, wr, cyc):
        return dv(lambda: g.vector.tensor_copy(out, a), rd, wr, cyc)

    def ms(ap, v, wr, cyc):
        return dv(lambda: g.vector.memset(ap, v), [], wr, cyc)

    def act(out, a, f, rd, wr, cyc, bias=0.0, scale=1.0):
        return ac(lambda: g.scalar.activation(out, a, f, bias=bias, scale=scale), rd, wr, cyc)

    def pe(items, rd, wr, first=True, final=True):
        def fn():
            r = None
            for q, it in enumerate(items):
                r = g.tensor.matmul(it[0], it[1], it[2], first and q == 0, final and q == len(items) - 1)
            return r
        cyc = sum(max(64, it[3]) for it in items)
        return op("P", fn, list(rd) + [it[4] for it in items], wr, 0.03 + cyc * 0.417e-3, bk(*wr))

    def iota(out, pat, base, cm, wr, n):
        return po(lambda: g.iota(out, pat, base, cm, allow_small_or_imprecise_dtypes=True), [], wr, n)

    GW = int(1.56 * W)

    op("S", lambda: g.sync.dma_start(T.e0i[:], T.e0[:]), [], ["e0i"], 0.1, sem=("le0", 16), lat=2.0)
    op("S", lambda: g.sync.dma_start(T.ivi[:], T.iv[:]), [], ["ivi"], 0.1, sem=("liv", 16), lat=5.5)
    op("S", lambda: g.sync.dma_start(T.stb[:], T.st[:]), [], ["stb"], 0.1, sem=("lst", 16), lat=6.8)

    slot = {}
    tslot = {}

    def wm(name):
        if name not in slot:
            slot[name] = len(slot)
        return T.Wm[:, slot[name]]

    def tmx(name):
        if name not in tslot:
            tslot[name] = len(tslot)
        return tslot[name]

    ncol = [0]

    def col():
        ncol[0] += 1
        return T.cols[:, ncol[0] - 1:ncol[0]]

    def E(r):
        return T.E16[:, r:r + 1]

    def TN(name):
        return ["T%s:%d" % (name, y) for y in range(32)]

    ms(T.ones[:], 1.0, ["ones"], 64)
    ms(T.Tm[:, 0:2], 0.0, TN("fF") + TN("pF"), 256)
    tmx("fF")
    tmx("pF")
    one = T.ones[:, 0:W]
    po(lambda: g.iota(T.coli[:, 0:1], [[0, 1]], 0, 1), [], ["coli0"], 1)
    iota(T.itr[:], [[0, 16], [1, 16]], 0, 0, ["itr"], 256)
    po(lambda: g.affine_select(wm("I"), T.ones[:], [[-1, 128]], AL.is_equal, 0.0, 0, 1), ["ones"], ["WI"], 128)
    po(lambda: g.affine_select(wm("B0"), T.ones[:], [[-16, 8], [0, 16]], AL.is_ge, 0.0, 0, 1), ["ones"], ["WB0"], 128)
    po(lambda: g.affine_select(wm("B"), wm("B0"), [[16, 8], [0, 16]], AL.is_ge, 0.0, 15, -1), ["WB0"], ["WB"], 128)
    iota(T.itl[:], [[1, 256]], -128, 0, ["itl"], 256)
    ts(T.coli[:, 1:2], T.coli[:, 0:1], 15, None, AL.bitwise_and, None, ["coli0"], ["coli1"], 1)
    pcol = col()
    cp(pcol, T.coli[:, 1:2], ["coli1"], ["pcol"], 1)
    ts(T.E16[:], T.itr[:, 0:16], pcol, None, AL.is_equal, None, ["itr", "pcol"], ["E16"], 16)
    act(T.colb[:, 0:1], pcol, AF.Exp, ["pcol"], ["p2b"], 1, scale=math.log(2.0))
    act(T.colb[:, 1:2], pcol, AF.Exp, ["pcol"], ["p2nb"], 1, scale=-math.log(2.0), bias=-math.log(2.0))
    p2, p2n, p2k, cq, cx, cF, cF1, c256, r16 = (col() for _ in range(9))
    act(p2, T.colb[:, 0:1], AF.Identity, ["p2b"], ["p2"], 1)
    act(p2n, T.colb[:, 1:2], AF.Identity, ["p2nb"], ["p2n"], 1)
    act(p2k, T.colb[:, 0:1], AF.Identity, ["p2b"], ["p2k"], 1, scale=2.0 ** -60)
    act(cq, pcol, AF.Identity, ["pcol"], ["cq"], 1, scale=-1.0)
    act(cx, pcol, AF.Identity, ["pcol"], ["cx"], 1, scale=-LB, bias=LB * (15 - 135.5 - 320))
    act(cF, E(0), AF.Identity, ["E16"], ["cF"], 1, scale=393216.0 - 1022.5)
    act(cF1, E(14), AF.Identity, ["E16", "cF"], ["cF1"], 1, bias=cF)
    act(c256, pcol, AF.Identity, ["pcol"], ["c256"], 1, scale=256.0, bias=128.0)
    act(r16, pcol, AF.Identity, ["pcol"], ["r16"], 1, scale=16.0, bias=4096.0)

    def scaled(name, base, v, rd=(), eng="A"):
        if eng == "A":
            act(wm(name), wm(base), AF.Identity, ["W" + base] + list(rd), ["W" + name], 128, scale=v)
        else:
            ts(wm(name), wm(base), v, None, AL.mult, None, ["W" + base] + list(rd), ["W" + name], 64)

    for nm, v in (("nI", -1.0), ("hI", 0.5), ("FM", 1.0)):
        scaled(nm, "I", v, eng="D")
    for nm, v in (("midK", -2.0 ** -44), ("midC2", -131072.0), ("vK", 2.0 ** -37), ("vC", 2.0 ** 23), ("sI", SCL), ("cntK", -20 * 2.0 ** -60), ("n512", -512.0),
                  ("I25", 2.5), ("nhI", -0.5), ("c12", 1.5 * 2.0 ** 35), ("nc12", -1.5 * 2.0 ** 35), ("c4", C16), ("nc4", -C16)):
        scaled(nm, "I", v)
    scaled("cqI", "I", cq, ["cq"])
    scaled("ncqI", "I", pcol, ["pcol"])
    scaled("nB", "B", -1.0)
    ts(T.nI16[:], wm("I"), -1.0, None, AL.mult, None, ["WI"], ["WnI16"], 64)
    for nm, v, d in (("t1", -512.0, -2304.0), ("t2", -2.0, 219 * 256.0), ("v", TAU * 2.0 ** -22, -SCL)):
        scaled(nm, "B", v)
        po(lambda nm=nm, d=d: g.affine_select(wm(nm), wm(nm), [[-1, 128]], AL.not_equal, d, 0, 1), ["W" + nm], ["W" + nm], 128)
    for q in range(2):
        ts(T.I37[:, q], wm("I"), 37.0 - 74.0 * q, None, AL.mult, None, ["WI"], ["WI37"], 64)
    tt(wm("S25"), wm("I25"), wm("B"), AL.subtract, ["WI25", "WB"], ["WS25"], 128)
    G8 = T.Wm[:, slot["B"], :, 0]
    ms(T.Z[:], 0.0, ["Z"], 72)
    ts(T.Z[:, 15:128:16], G8, p2, None, AL.mult, None, ["WB", "Z", "p2"], ["Z"], 8)

    def ent(name, ents):
        k = slot[name]
        for r0, a, b, v in ents:
            ap = T.Wm[:, k, :, a:b]
            po(lambda ap=ap, a=a, b=b, v=v, r0=r0: g.affine_select(ap, ap, [[-16, 8], [0, b - a]], AL.not_equal, float(v), -r0, 1),
               ["W" + name], ["W" + name], 8 * (b - a))

    def tent(name, ents):
        k = tmx(name)
        for r0, sl, v in ents:
            ap = T.Tm[:, k, :, :, sl]
            nm = ["T%s:%d" % (name, y) for y in range(32)[sl]]
            po(lambda ap=ap, n=len(nm), v=v, r0=r0: g.affine_select(ap, ap, [[-16, 2], [-32, 4], [0, n]], AL.not_equal, float(v), -r0, 1), nm, nm, 8 * len(nm))

    def lin(name, terms):
        c = col()
        for q, (r0, v) in enumerate(terms):
            act(c, E(r0), AF.Identity, ["E16", name], [name], 1, scale=float(v), bias=c if q else 0.0)
        return c

    S = slice
    ZO, KO = 64 + 4 * W, 64 + 5 * W
    ent("FM", [(1, 0, 1, 640), (2, 0, 1, 5), (4, 0, 1, 1)])
    ceA = lin("ceA", [(1, 128), (2, 1), (4, 1), (11, 2048)])
    scaled("eA", "B", ceA, ["ceA"])
    cneA = lin("cneA", [(7, 2048), (10, -0.5)])
    act(cneA, ceA, AF.Identity, ["ceA", "cneA"], ["cneA"], 1, scale=-1.0, bias=cneA)
    scaled("neA", "B", cneA, ["cneA"])
    tent("pF", [(3, S(16, 17), 256), (9, S(16, 17), 1)])
    tent("fF", [(1, S(12, 13), 256), (1, S(15, 16), 1280), (2, S(12, 13), 2), (2, S(15, 16), 10), (4, S(15, 16), 2), (0, S(15, 16), -2),
                (4, S(0, 4), 1), (4, S(8, 12), 1), (8, S(21, 23), 48), (8, S(26, 31, 4), 48), (9, S(4, 7, 2), 1), (9, S(20, 23), 1), (9, S(25, 27), 1), (9, S(28, 31), 1),
                (5, S(0, 1), PB), (5, S(20, 32, 8), PB), (12, S(1, 2), PB), (12, S(21, 32, 4), PB), (6, S(4, 13, 4), PB), (6, S(2, 3), -16), (6, S(26, 27), -PB),
                (13, S(9, 14, 4), PB), (7, S(2, 32, 4), -PB), (7, S(11, 16, 4), -2 * PB),
                (10, S(0, 1), 2080), (10, S(1, 2), 2096), (10, S(2, 4), 2048), (10, S(4, 7, 2), KO), (10, S(7, 8), 24), (10, S(12, 16), WS),
                (10, S(20, 26, 5), ZO), (10, S(21, 31, 9), 96), (10, S(22, 27, 4), 112), (10, S(23, 32, 4), 16), (10, S(28, 30), ZO),
                (11, S(3, 4), 1), (11, S(9, 12, 2), 1), (11, S(15, 16), 786432), (11, S(26, 27), -3 * PB), (15, S(15, 16), 2),
                (14, S(4, 8), 4096), (14, S(12, 16), -WS), (14, S(20, 32), 4096)])
    ms(T.Tm[:, 2:5], 0.0, TN("pK") + TN("fZ") + TN("fTg"), 128 * 3)
    ms(T.Tm[:, 5:NT], 0.0, TN("wT") + TN("fOg") + TN("fC0") + TN("fC1") + TN("fOq") + TN("fTf"), 128 * (NT - 5))
    for h in range(2):
        act(T.BP[:, h], T.Wm[:, slot["B"], h:8:2], AF.Identity, ["WB"], ["BP%d" % h], 64)
    cpF = lin("cpF", [(7, 65536), (10, -0.5)])
    ea, ena = col(), col()
    act(ea, E(0), AF.Identity, ["E16"], ["ea"], 1, scale=ALF)
    act(ena, E(0), AF.Identity, ["E16"], ["ena"], 1, scale=-ALF)
    for name, ents in (("pF", [(S(0, 16), cpF, "cpF")]), ("pK", [(S(0, 16), p2k, "p2k")]),
                       ("fZ", [(S(0, 32, 4), ea, "ea"), (S(1, 32, 4), ea, "ea"), (S(2, 32, 4), ena, "ena"), (S(11, 16, 4), ena, "ena")]),
                       ("fTg", [(S(2, 32, 4), ALF, None), (S(14, 15), 1.0, None), (S(11, 16, 4), -ALF, None)]),
                       ("wT", [(S(0, 16), p2n, "p2n")]), ("fOg", [(S(14, 15), c256, "c256")]),
                       ("fC0", [(S(2, 3), 16.0, None), (S(22, 23), -16.0, None), (S(26, 27), PB, None)]),
                       ("fC1", [(S(2, 31, 28), 16.0, None), (S(26, 27), PB, None)]),
                       ("fOq", [(S(13, 14), c256, "c256")]), ("fTf", [(S(13, 14), 1.0, None)])):
        k = tmx(name)
        for sl, v, nm in ents:
            wn = ["T%s:%d" % (name, y) for y in range(32)[sl]]
            act(T.Tm[:, k, :, :, sl], T.BP[:, :, :, 0:len(wn)], AF.Identity, ["BP0", "BP1"] + ([nm] if nm else []), wn, 8 * len(wn), scale=v)

    ts(T.NK[:], T.E16[:], -1.0, -KN, AL.add, AL.mult, ["E16"], ["NK"], 16)
    for q in range(16):
        o = T.win[:, WS + 256 * q:WS + 256 * q + 256]
        if q % 3 == 2:
            act(o, T.itl[:], AF.Identity, ["itl", "E16", "NK"], ["OH%d" % q], 256, scale=E(q), bias=T.NK[:, q:q + 1])
        else:
            ts(o, T.itl[:], E(q), T.NK[:, q:q + 1], AL.mult, AL.add, ["itl", "E16", "NK"], ["OH%d" % q], 128)
    OHN = ["OH%d" % q for q in range(16)]
    d2, d4, d8 = col(), col(), col()
    ts(d2, E(1), 2.0, E(3), AL.mult, AL.add, ["E16"], ["d2"], 1)
    act(d4, d2, AF.Identity, ["d2"], ["d4"], 1, scale=2.0)
    act(d8, d2, AF.Identity, ["d2"], ["d8"], 1, scale=4.0)
    ts(T.TM[:, 0:128], T.itl[:, 128:256], E(2), None, AL.mult, None, ["itl", "E16"], ["TM"], 64)
    for n, c, nm in ((128, E(1), "E16"), (256, d2, "d2"), (512, d4, "d4"), (1024, d8, "d8")):
        ts(T.TM[:, n:2 * n], T.TM[:, 0:n], c, None, AL.add, None, ["TM", nm], ["TM"], n // 2)
    ts(T.OHb[:, 0:256], T.itr[:], pcol, None, AL.is_equal, None, ["itr", "pcol"], ["OHb"], 128)
    for n in range(256, 16 * W, 256):
        op("S", lambda n=n: g.sync.dma_start(T.OHb[:, n:n + 256], T.OHb[:, 0:256]), ["OHb", "stb"], ["OHc"] if n == 16 * W - 256 else [], 0.1, sem=("ohb", 16), lat=2.5)
    ms(T.OHb[:, 16 * W:16 * W + 16], 0.0, ["OHz"], 16)
    ms(T.Y[:, :, 16 * W:16 * W + 16], ZN, ["Yz"], 32)
    ms(T.pat[:], 1.0, ["pat"], W)
    ts(T.pat[:, 15:W:16], T.itr[:, 0:MU], 256.0, r16, AL.mult, AL.add, ["itr", "r16", "pat"], ["pat"], 8)
    ms(T.seg[:], 1.0, ["seg"], W)
    ms(T.seg[:, 0:2 * W:4], 0.0, ["seg"], 64)
    iota(T.itm[:], [[1, MU], [0, 16]], 0, 0, ["itm"], W)
    ts(T.lanec[:], T.itl[:, 128:128 + W], E(9), None, AL.mult, None, ["itl", "E16"], ["lanec"], 64)
    ts(T.itm[:], T.itm[:], E(8), None, AL.mult, None, ["itm", "E16"], ["itm"], 64)
    tt(T.lanec[:], T.lanec[:], T.itm[:], AL.add, ["itm", "lanec"], ["lanec"], W)
    kb, k2, k0, k3 = (col() for _ in range(4))
    ts(kb, E(7), E(10), E(11), AL.add, AL.add, ["E16"], ["kb"], 1)
    ts(kb, kb, E(15), None, AL.add, None, ["E16", "kb"], ["kb"], 1)
    ts(k0, kb, E(12), E(13), AL.subtract, AL.subtract, ["E16", "kb"], ["k0"], 1)
    ts(k2, kb, E(5), E(13), AL.subtract, AL.subtract, ["E16", "kb"], ["k2"], 1)
    ts(k3, kb, E(5), E(6), AL.subtract, AL.subtract, ["E16", "kb"], ["k3"], 1)
    ts(k3, k3, E(12), None, AL.subtract, None, ["E16", "k3"], ["k3"], 1)
    for q, c, nm in ((0, k0, "k0"), (1, k0, "k0"), (2, k2, "k2"), (3, k3, "k3")):
        ts(T.TM[:, 2048 + 16 * q:2064 + 16 * q], T.itr[:, 0:16], E(4), c, AL.mult, AL.add, ["itr", "E16", nm], ["TA%d" % q], 16)
    TAN = ["TM"] + ["TA%d" % q for q in range(4)]

    def wn_(ch, a, b):
        o = (WS + 4096) * ch
        return T.win[:, o + a:o + b]

    for ch in range(NCH):
        ms(wn_(ch, 0, 24), AB, ["wa%d" % ch], 24)
        ms(wn_(ch, 24, 64), KN, ["wk%d" % ch], 40)

    def sfv(ch, q):
        return T.sf[:, ch, q]

    def sbv(ch, q):
        return T.sb[:, ch, q]

    ts(T.e0u[:], T.e0i[:], 2.0, None, AL.mult, None, ["e0i"], ["x0u"], 16)
    cp(T.eL[:, 0:NCH, 0:MU], T.e0i[:], ["e0i"], ["e%d" % q for q in range(NCH)], 16)
    ms(T.eL[:, 0:NCH, MU:2 * MU], 2048, ["a%d" % q for q in range(NCH)], 16)
    ms(T.sb[:, :, 9], ZN / 16, ["tg%d" % q for q in range(NCH)], 128)
    for ch in range(NCH):
        act(wn_(ch, KO, WS), T.win[:, WS:WS + 4096].indirect(T.e0u[:, MU * ch:MU * ch + MU]), AF.Identity, OHN + ["x0u"], ["K%d" % ch], GW)
    for q in range(4):
        cp(T.ivf[:, q * 512:q * 512 + 512], T.ivi[:, q * 512:q * 512 + 512], ["ivi"], ["ivf%d" % q], 512)
    IVF = ["ivf%d" % q for q in range(4)]

    rank = T.rank_of(core)
    cores = list(T.cores)
    NR = len(cores)
    tile = [0]

    def masks(src, ch, copies):
        ds = [(b, q) for b in range(NB * ch, NB * ch + NB) if b % NR for q in range(copies)]
        en = {x: topo.engines(cores[src], cores[(src + x[0]) % NR]) for x in ds}
        few = min(en.values(), key=len)
        res = {}
        for pool, xs in ((few, [x for x in ds if len(en[x]) == len(few)]), (None, [x for x in ds if len(en[x]) > len(few)])):
            if xs:
                pool = list(pool or [e for e in en[xs[0]] if e not in few])
                left = len(xs)
                for x in reversed(xs):
                    n = 1
                    while 2 * n * left <= len(pool):
                        n *= 2
                    res[x] = pool[:n]
                    pool = pool[n:]
                    left -= 1
        return res

    def views(s, ch):
        n = NCH * s + ch
        place = {"R": (4 + ch, 0), "X": (4 + ch, 1), "T": (4 + ch, 2), "A": (6 + ch, 0), "B": (6 + ch, 1), "C": (6 + ch, 2), "N": (6 + ch, 3)}
        r = {k: T["ps%d" % b][:, q] for k, (b, q) in place.items()}
        nm = {k: "ps%dq%d" % v for k, v in place.items()}
        lk = {k: "lk%d" % v[0] for k, v in place.items()}
        st = [wn_(ch, KO, WS), T.M[:, ch, W:2 * W], T.sta[:, n, :, 2], T.sta[:, n, :, 3]]
        return n, str(ch), str(n), place, r, nm, lk, st

    def turn(place, nm, lk, parts, ch, u):
        bank, q = T["ps%d" % place["T"][0]], place["T"][1]
        for i, (terms, rd) in enumerate(parts):
            it = [(bank[:, q:q + 2, h:MU:2], T.Tm[:, tslot[x], h], rhs, W, "WI") for h in range(2) for x, rhs in terms]
            rd = rd + [y for x, rhs in terms for y in TN(x)]
            if len(parts) == 1:
                pe(it, rd + [lk["T"]], [nm["T"]])
            else:
                pe(it, rd, [nm["T"], lk["T"]], first=i == 0, final=i == len(parts) - 1)
        dv(lambda: g.vector.transpose(T.tT[:, ch, u] if u < 2 else T.tF[:, ch], bank[:, q:q + 2]), [nm["T"]], ["tT%d%d" % (u, ch)], 2 * W)

    def prep(s, ch):
        n, c, N, place, r, nm, lk, (K, MA, P0, P1) = views(s, ch)
        PN = "P_" + N
        el, eln = T.eL[:, n, 0:MU], "e" + N
        if s == 0:
            cp(T.c16[:, ch], T.ivi[:, 0:2048].indirect(el), ["ivi", eln], ["c16" + c], GW)
        else:
            cp(T.c16[:, ch], T.ivf[:, 0:2048].indirect(el), IVF + [eln], ["c16" + c], GW)
        for q in range(NB):
            src = T.stb[:, 0:4096].indirect(T.c16[:, ch, 32 * q:32 * q + 32])
            if YE[s][NB * ch + q] == "D":
                ts(T.Y[:, ch, 512 * q:512 * q + 512], src, -128.0, None, AL.add, None, ["stb", "c16" + c], ["Y%d" % q + c], 800)
            else:
                act(T.Y[:, ch, 512 * q:512 * q + 512], src, AF.Identity, ["stb", "c16" + c], ["Y%d" % q + c], 800, bias=-128.0)
        op("S", lambda: g.sync.dma_start(wn_(ch, 64, ZO), T.sta[:, n] if s else T.stb[:, 0:4 * W]), [PN if s else "stb"], ["win" + c], 0.1, sem=("wn" + N, 16), lat=2.0)
        hh, F = sbv(ch, 1), sbv(ch, 3)
        if s > 0:
            it = [(r["A"], wm("hI"), P0, W, "WhI"), (r["A"], wm("hI"), P1, W, "WhI")] if s > 1 else [(r["A"], wm("I"), P0, W, "WI")]
            Kk, Ox = T.sta[:, n, :, 0], T.sta[:, n, :, 1]
            pe([(r["A"], wm("midK"), Kk, W, "WmidK"), (r["A"], wm("midK"), Ox, W, "WmidK"), (r["A"], wm("midC2"), one, W, "WmidC2")] + it,
               [PN, "ones", lk["A"]], [nm["A"]])
            tt(K, Kk, Ox, AL.max, [PN], ["K" + c], W)
            ts(T.mh[:, ch, 0], K, -CO, -60000.0, AL.add, AL.max, ["K" + c], ["ko" + c], W // 2)
            tt(T.mh[:, ch, 1], r["A"], T.mh[:, ch, 0], AL.max, [nm["A"], "ko" + c], ["mid" + c], W)
        if s > 1:
            pe([(r["B"], wm("hI"), P0, W, "WhI"), (r["B"], wm("nhI"), P1, W, "WnhI")], [PN, lk["B"]], [nm["B"]])
            act(hh, r["B"], AF.Abs, [nm["B"]], ["h" + c], W)
            pe([(r["C"], wm("vK"), K, W, "WvK"), (r["C"], wm("vC"), one, W, "WvC"), (r["C"], wm("I"), hh, W, "WI")], ["K" + c, "ones", "h" + c, lk["C"]], [nm["C"]])
            act(sbv(ch, 12), r["C"], AF.Identity, [nm["C"]], ["v" + c], W)
        act(T.M[:, ch], T.TM[:, 0:2112].indirect(T.eL[:, n]), AF.Identity, TAN + [eln, "a" + N], ["M1" + c], 2 * GW)
        pe([(r["X"], wm("FM"), T.M[:, ch, 0:W], W, "WFM"), (r["X"], wm("FM"), MA, W, "WFM"), (r["X"], wm("I"), T.lanec[:], W, "WI")],
           ["M1" + c, "lanec", lk["X"]], [nm["X"]])
        act(F, r["X"], AF.Identity, [nm["X"], "cF", "cF1"], ["F" + c], W, bias=(cF, cF1)[ch])
        turn(place, nm, lk, [([("pK", K), ("pF", F)], ["K" + c, "F" + c])], ch, 0)
        dl = T.lu[:, ch, 0]
        ts(dl, T.tT[:, ch, 0, :, 16], float(W * ch), None, AL.add, None, ["tT0" + c], ["dl" + c], 8)
        ch16 = T.mh[:, ch, 2]
        ts(ch16, T.c16[:, ch], -2048.0, None, AL.add, None, ["c16" + c], ["c32" + c], W // 2)
        act(sfv(ch, 1), T.ivf[:, 0:2048].indirect(dl), AF.Identity, IVF + ["dl" + c], ["old" + c], GW)
        pe([(r["X"], T.I37[:, 1], ch16, W, "WI37"), (r["X"], wm("neA"), F, W, "WneA"), (r["X"], wm("c12"), one, W, "Wc12"), (r["X"], wm("nc12"), one, W, "Wnc12"),
            (r["X"], T.I37[:, 0], ch16, W, "WI37"), (r["X"], wm("eA"), F, W, "WeA")], ["c32" + c, "F" + c, "ones", lk["X"]], [nm["X"]])
        tt(sfv(ch, 2), r["X"], sfv(ch, 1), AL.subtract, [nm["X"], "old" + c], ["diff" + c], W)

    def big(s, ch):
        n, c, N, place, r, nm, lk, (K, MA, P0, P1) = views(s, ch)
        for t in range(NB):
            u = tile[0] % NTB
            tile[0] += 1
            ps, pn = T["ps%d" % u], "ps%d" % u
            lh, kh = t // 2, t % 2
            lo, hi = 64 * lh, 64 * lh + 64
            it = [(ps[:, :, 7 - kk], wm("I"), T.Y[:, ch, 16 * lo + 8 * kh + kk:16 * hi:16], 64, "WI") for kk in range(8)]
            it += [(ps[:, :, j], wm("nI"), wn_(ch, KO + lo, KO + hi), 64, "WnI") if s == 0 else (ps[:, :, j], T.nI16[:], T.mh[:, ch, 1, lo:hi], 64, "WnI16")
                   for j in range(8)]
            pe(it, ["Y%d" % q + c for q in (2 * lh, 2 * lh + 1)] + ["mid" + c if s else "K" + c], [pn])
            m, mn = T.tm[:, ch, lo:hi, 8 - 8 * kh:16 - 8 * kh], "tm%d" % t + c
            if s > 0:
                act(T.ab[:, u], ps[:], AF.Abs, [pn], ["ab%d" % u], 512)
                ts(T.mis[:, u], T.ab[:, u], CO, TAU if s > 1 else 1.0, AL.is_equal, AL.mult, ["ab%d" % u], ["mis%d" % u], 256)
                it = [(ps[:], wm("sI"), T.ab[:, u], 512, "WsI")]
                if s > 1:
                    it += [(ps[:, :, j], wm("v"), T.sb[:, ch, 12, lo:hi], 64, "Wv") for j in range(8)]
                pe(it, ["ab%d" % u, "v" + c], [pn], final=False)
                tn = "t2" if s > 1 else "t1"
                pe([(ps[:], wm(tn), T.mis[:, u], 512, "W" + tn)], ["mis%d" % u], [pn], first=False)
            ts(m, ps[:], C8 + (512.0 if s == 1 else 0.0), C8, AL.add, AL.is_equal, [pn], [mn], 512)
            if s > 0:
                b, q = place["N"]
                it = [(r["N"], wm("cntK"), K, W, "WcntK")] if t == 0 else []
                it += [(T["ps%d" % b][:, q, 4 * lh:4 * lh + 4], wm("I"), T.tm[:, ch, lo:hi, 8 - 8 * kh + j], 64, "WI") for j in range(8)]
                pe(it, [mn, "K" + c], [nm["N"], lk["N"]], first=t == 0, final=t == NB - 1)
            if kh:
                b, q = place["R"]
                o = T["ps%d" % b][:, q, 4 * lh:4 * lh + 4]
                it = [(o, wm("hI"), T.ones[:, 0:64], 64, "WhI")]
                it += [(o, T.Z[:, 15 - x:143 - x], T.tm[:, ch, lo + x:hi:16], 64, "Z") for x in range(16)]
                pe(it, ["tm%d" % (t - 1) + c, mn, "ones", lk["R"]], [nm["R"] + "h%d" % lh])

    def first(ch, u, rd, lst, nm):
        dv(lambda: g.vector.tensor_tensor_scan(T.sj[:, ch, u], T.nb[:, ch, u], T.pat[:], 4096.0, AL.mult, AL.add), rd + ["pat"], ["sj%d%d" % (u, ch)], W)
        ts(lst, T.sj[:, ch, u, 15:W:16], -4096.0, 16.0 * W, AL.add, AL.min, ["sj%d%d" % (u, ch)], [nm], 8)

    def post(s, ch):
        n, c, N, place, r, nm, lk, (K, MA, P0, P1) = views(s, ch)
        PN = "P_" + N
        lastst = s == RO - 1
        Yn = ["Y%d" % q + c for q in range(NB)] + ["Yz"]
        Rn = [nm["R"] + "h%d" % q for q in range(NB // 2)]
        hh, F = sbv(ch, 1), sbv(ch, 3)
        f, oq, tf, wx, tg, Og = (sbv(ch, q) for q in (5, 6, 7, 8, 9, 10))
        z = wn_(ch, ZO, KO)
        dl, jl, gl = (T.lu[:, ch, q] for q in range(3))
        Yw = T.Y[:, ch]
        tt(T.nb[:, ch, 0], r["R"], T.tT[:, ch, 0, :, 0:16], AL.not_equal, Rn + ["tT0" + c], ["nb" + c], W)
        first(ch, 0, ["nb" + c], jl, "jl" + c)
        tt(sfv(ch, 3), T.OHb[:].indirect(jl), sfv(ch, 2), AL.mult, ["OHb", "OHc", "OHz", "jl" + c, "diff" + c], ["ds" + c], GW)
        extra = ["yiA"] if lastst and ch == NCH - 1 else []
        tt(T.ivf[:, 0:2048].indirect(dl), sfv(ch, 1), sfv(ch, 3), AL.add, ["old" + c, "ds" + c, "dl" + c] + extra, IVF, 4 * W)
        if lastst:
            for q in range(8):
                op("S", lambda lo=256 * q + W * ch: g.sync.dma_start(T.yi[:, lo:lo + W], T.ivf[:, lo:lo + W]), IVF, ["yiA"] if (ch == 0 and q == 7) else [], 0.1,
                   sem=("outA" if ch == 0 else "out", 16), lat=2.5)
        act(z, Yw.indirect(jl), AF.Identity, Yn + ["jl" + c], ["z" + c], GW)
        parts = [([("fF", F), ("fZ", z)], ["F" + c, "z" + c])]
        if s > 1:
            pe([(r["B"], wm("hI"), P0, W, "WhI"), (r["B"], wm("hI"), P1, W, "WhI"), (r["B"], wm("nI"), hh, W, "WnI")], [PN, "h" + c, lk["B"]], [nm["B"]])
            tt(f, r["B"], z, AL.min, [nm["B"], "z" + c], ["f" + c], W)
            pe([(r["X"], wm(x), y, W, "W" + x) for x, y in (("B", f), ("cqI", one), ("c4", one), ("nc4", one), ("nB", f), ("ncqI", one))],
               ["f" + c, "ones", lk["X"]], [nm["X"]])
            ts(oq, r["X"], 0.0, None, AL.is_equal, None, [nm["X"]], ["oq" + c], W)
            tt(tf, oq, f, AL.mult, ["oq" + c, "f" + c], ["tf" + c], W)
            parts += [([("fOq", oq), ("fTf", tf)], ["oq" + c, "tf" + c])]
        if s > 0:
            act(wx, r["N"], AF.Exp, [nm["N"], "cx"], ["wx" + c], W, scale=16 * LB, bias=cx)
            pe([(r["C"], wm("S25"), wx, W, "WS25")], ["wx" + c, lk["C"]], [nm["C"]])
            ts(Og, r["C"], 0.0, None, AL.is_gt, None, [nm["C"]], ["Og" + c], W)
            turn(place, nm, lk, [([("wT", Og)], ["Og" + c])], ch, 1)
            tt(sfv(ch, 5), r["R"], T.tT[:, ch, 1, :, 0:16], AL.mult, Rn + ["tT1" + c], ["u" + c], W)
            ts(r["C"], sfv(ch, 5), C1, -C1, AL.add, AL.add, ["u" + c], [nm["C"]], W)
            tt(T.nb[:, ch, 1], r["C"], sfv(ch, 5), AL.is_le, [nm["C"], "u" + c], ["nb2" + c], W)
            first(ch, 1, ["nb2" + c], gl, "gl" + c)
            tt(tg, Yw.indirect(gl), Og, AL.mult, Yn + ["gl" + c, "Og" + c], ["tg" + c], GW)
            bank, q = T["ps%d" % place["C"][0]], place["C"][1]
            it = [(bank[:, q:q + 2], wm("I"), T.sta[:, n, :, 2:4], 2 * W, "WI")]
            it += [(bank[:, q:q + 2, h:MU:2], wm("n512"), Og, W, "Wn512") for h in range(2)]
            pe(it, [PN, "Og" + c], [nm["C"], nm["N"], lk["C"]], final=False)
            pe([(bank[:, q:q + 2, h:MU:2], wm("nI"), tg, W, "WnI") for h in range(2)], ["tg" + c], [nm["C"], nm["N"], lk["C"]], first=False)
            ts(T.cc[:, ch], bank[:, q:q + 2], C8 + 512.0, C8, AL.add, AL.is_equal, [nm["C"], nm["N"]], ["cc" + c], 2 * W)
            parts[0] = (parts[0][0] + [("fOg", Og)], parts[0][1] + ["Og" + c])
            parts += [([("fTg", tg)], ["tg" + c]), ([("fC0", T.cc[:, ch, :, 0]), ("fC1", T.cc[:, ch, :, 1])], ["cc" + c])]
        else:
            parts = [(parts[0][0] + [("fTg", tg)], parts[0][1] + ["tg" + c])]
        turn(place, nm, lk, parts, ch, 2)
        dv(lambda: g.vector.tensor_tensor_scan(T.sF[:, ch], T.seg[:], T.tF[:, ch], 0.0, AL.mult, AL.max), ["tT2" + c, "seg"], ["sF" + c], 2 * W)
        x = T.sF[:, ch, 15:2 * W:32]
        xo = -0.25 - (WS / 2, 0.0)[ch]
        if lastst:
            ms(wn_(ch, 16, 24), -129.0, ["wa" + c], 8)
        wrd = ["win" + c, "z" + c, "K" + c, "wa" + c, "wk" + c] + OHN
        Ww = T.win[:, WS * ch:WS * ch + WS + 4096]
        if not lastst:
            cp(T.la[:, ch], T.sF[:, ch, 7:2 * W:8], ["sF" + c], ["la" + c], 32)
            ts(T.eS[:, n, 0:MU], x, 0.5, xo, AL.mult, AL.add, ["sF" + c], ["eS" + N], 8)
            cp(T.eS[:, n, MU:2 * MU], T.sF[:, ch, 3:2 * W:32], ["sF" + c], ["aS" + N], 8)
            act(T.snd[:, n], Ww.indirect(T.la[:, ch]), AF.Identity, wrd + ["la" + c], ["snd" + N], 4 * GW)
            n2 = n + NCH
            for src, dst, u, offs, sm, rd, nxt in ((T.eS, T.eL, 1, (0, MU), "ar%d" % n2, ["eS" + N, "aS" + N], ["e%d" % n2, "a%d" % n2]),
                                                   (T.snd, T.sta, 64, (0,), "ap%d" % n2, ["snd" + N], ["P_%d" % n2])):
                mk = masks(rank, ch, len(offs))
                got = sum(len(masks((rank - y[0]) % NR, ch, len(offs))[y]) for y in mk)
                sent = sum(len(v) for v in mk.values())

                def go(src=src, dst=dst, u=u, offs=offs, sm=sm, mk=mk):
                    trs = []
                    for b, q in sorted(mk):
                        rid, pid, _ = topo.addr(cores[(rank + b) % NR])
                        lo = offs[q] + 2 * (b - NB * ch)
                        trs.append(RemoteDMATransfer(dst_ids=[DstId(rid=rid, pnc=pid)], dma_engine_mask=sum(1 << e for e in mk[b, q]), remote_sem=T.sem[sm],
                                                     src=src[:, n, u * lo:u * (lo + 2)], dst=dst[:, n2, lo:lo + 2]))
                    g.remote_dma_fused(trs, local_sem=T.sem.loc)
                    return None
                if ch == 0:
                    for o in offs:
                        op("S", lambda src=src, dst=dst, u=u, o=o: g.sync.dma_start(dst[:, n2, o:o + 2], src[:, n, o:o + 2 * u]), rd, [], 0.1, sem=(sm, 16), lat=2.0)
                op("G", go, rd, nxt, GI, sem=(sm, got, sent), lat=LAT)
        else:
            lo = ch * W
            for q, y in enumerate((7, 15, 23, 27)):
                cp(T.lu[:, ch, 3 + q], T.sF[:, ch, y:2 * W:32], ["sF" + c], ["ll%d" % q + c], 8)
            act(sbv(ch, 11), Ww.indirect(T.lu[:, ch, 3]), AF.Identity, wrd + ["ll0" + c], ["kk" + c], GW)
            tt(sbv(ch, 12), Ww.indirect(T.lu[:, ch, 4]), sbv(ch, 11), AL.max, wrd + ["ll1" + c, "kk" + c], ["v" + c], GW)
            ts(T.ok_[:, lo:lo + W], sbv(ch, 12), 128.0, -1.0, AL.add, AL.max, ["v" + c], ["oK" + c], W // 2)
            for q in range(2):
                act(T.oy[:, q, lo:lo + W], Ww.indirect(T.lu[:, ch, 5 + q]), AF.Identity, wrd + ["ll%d" % (2 + q) + c], ["oy%d" % q + c], GW, bias=128.0)
            o8 = slice(MU * ch, MU * ch + MU)
            ts(T.oe[:, 2, o8], x, 0.5, xo, AL.mult, AL.add, ["sF" + c], ["oh" + c], 8)
            ts(T.oe[:, 0, o8], T.oe[:, 2, o8], C1, -C1, AL.add, AL.add, ["oh" + c], ["oe" + c], 8)
            ts(T.oe[:, 1, o8], T.sF[:, ch, 11:2 * W:32], C1, -C1, AL.add, AL.add, ["sF" + c], ["oa" + c], 8)
            if ch == NCH - 1:
                for eng, q, dst, src, rd in (("A", g.scalar, T.yk, T.ok_[:], "oK"), ("S", g.sync, T.y0, T.oy[:, 0], "oy0"), ("A", g.scalar, T.y1, T.oy[:, 1], "oy1"),
                                             ("S", g.sync, T.ye, T.oe[:, 0], "oe"), ("S", g.sync, T.ya, T.oe[:, 1], "oa")):
                    op(eng, lambda q=q, dst=dst, src=src: q.dma_start(dst[:], src), [rd + str(y) for y in range(NCH)], [], 0.1, sem=("out", 16), lat=2.0)

    for s in range(RO):
        for nm, fn, ch in [("p", prep, ch) for ch in range(NCH)] + [x for ch in range(NCH) for x in (("b", big, ch), ("q", post, ch))]:
            phase[0] = nm + str(ch)
            fn(s, ch)
    assert len(slot) <= NW and len(tslot) <= NT
    return ops


def schedule(ops):
    n = len(ops)
    pred = [sorted(o["deps"]) for o in ops]
    succ = [[] for _ in range(n)]
    for i in range(n):
        for d in pred[i]:
            succ[d].append(i)

    def gap(i, j):
        return ops[i]["lat"] + (0.0 if ops[i]["eng"] == "P" and ops[j]["eng"] == "P" else HOP)

    dur = [o["dur"] for o in ops]
    lat = [o["lat"] for o in ops]
    own = [[o["eng"]] + [(b, o["eng"]) for b in o["banks"]] for o in ops]
    other = [[(b, e) for b in o["banks"] for e in "PDA" if e != o["eng"]] for o in ops]
    edges = ([[(j, dur[j] + gap(j, i)) for j in pred[i]] for i in range(n)], [[(j, dur[j] + gap(i, j)) for j in succ[i]] for i in range(n)])

    def place(keys, back, old=None, since=0.0):
        after = pred if back else succ
        before = edges[back]
        busy = {k: [] for o in own for k in o}
        busy.update({k: [] for o in other for k in o})
        st = [0.0] * n
        left = [len(p) for p in before]
        kept = [False] * n
        if old:
            for i in old[1]:
                if old[0][i] >= since:
                    break
                kept[i] = True
                st[i] = old[0][i]
                for k in own[i]:
                    busy[k].append((st[i], st[i] + dur[i]))
                for j in after[i]:
                    left[j] -= 1
        heap = sorted(((keys[i], i) for i in range(n) if left[i] == 0 and not kept[i]), reverse=True)
        while heap:
            i = heap.pop()[1]
            d = dur[i]
            t = lat[i] if back else 0.0
            for j, x in before[i]:
                if st[j] + x > t:
                    t = st[j] + x
            rows = [(busy[own[i][0]], 0.0)] + [(busy[k], HOP) for k in other[i]]
            moved = True
            while moved:
                moved = False
                for v, m in rows:
                    k = len(v)
                    while k and v[k - 1][0] >= t - m:
                        k -= 1
                    if k and v[k - 1][1] + m > t + 1e-9:
                        t = v[k - 1][1] + m
                        moved = True
                    elif k < len(v) and v[k][0] < t + d + m - 1e-9:
                        t = v[k][1] + m
                        moved = True
            st[i] = t
            for k in own[i]:
                v = busy[k]
                q = len(v)
                while q and v[q - 1][0] > t:
                    q -= 1
                v.insert(q, (t, t + d))
            for j in after[i]:
                left[j] -= 1
                if left[j] == 0:
                    q = len(heap)
                    while q and heap[q - 1][0] < keys[j]:
                        q -= 1
                    heap.insert(q, (keys[j], j))
        return st, max(st[i] + dur[i] + (0.0 if back else lat[i]) for i in range(n))

    seed = [SEED[0]]

    def rnd():
        seed[0] = (seed[0] * 1103515245 + 12345) % 2147483648
        return seed[0] / 2147483648

    def search():
        keys = [0.0] * n
        for i in range(n - 1, -1, -1):
            keys[i] = min([keys[j] - lat[i] - HOP for j in succ[i]], default=-lat[i]) - dur[i]
        keys = [keys[i] - SEED[2].get(ops[i]["ph"], 0.0) for i in range(n)]
        best = None
        for r in range(ROUNDS[0]):
            st, end = place(keys, False)
            if best is None or end < best[1]:
                best = (st, end)
            sb = place([-(st[i] + dur[i]) for i in range(n)], True)[0]
            keys = [-(sb[i] + dur[i]) + SEED[1] * rnd() for i in range(n)]
        sends = [i for i in range(n) if ops[i]["eng"] == "G" and ops[i]["sem"]]
        st, end = best
        old = (st, sorted(range(n), key=lambda i: st[i]))
        for r in range(ROUNDS[1]):
            k = list(st)
            kind = rnd()
            i = int(n * rnd())
            if kind < 0.5:
                k[i] += 5 * rnd() - 2.5
                since = min(k[i], st[i])
            elif kind < 0.8:
                d = 0.3 + 2.7 * rnd()
                stack, seen = [i], set()
                while stack:
                    a = stack.pop()
                    if a not in seen and st[a] >= st[i] - 2 * d:
                        seen.add(a)
                        k[a] -= d
                        stack.extend(pred[a])
                since = st[i] - 3 * d
            else:
                a, d, amp = st[i], 1 + 5 * rnd(), 0.4 + 0.8 * rnd()
                k = [x + amp * (rnd() - 0.5) if a < x < a + d else x for x in k]
                since = a - amp
            s2, e2 = place(k, False, old, since)
            if e2 + 0.02 * sum(s2[i] for i in sends) <= end + 0.02 * sum(st[i] for i in sends):
                st, end = s2, e2
                old = (st, sorted(range(n), key=lambda i: st[i]))
        return st, end

    if not KEPT:
        KEPT.append(search())
    st, end = KEPT[0]
    order = sorted(range(n), key=lambda i: (i - 3 if i < 3 else st[i], i))
    bank = {}
    for i in order:
        ops[i]["t"] = st[i]
        for b in ops[i]["banks"]:
            ops[i]["deps"].update(j for e, j in bank.get(b, {}).items() if e != ops[i]["eng"])
            bank.setdefault(b, {})[ops[i]["eng"]] = i
    return order, end


def emit(g, T, ops, order):
    qs = {"P": g.tensor, "D": g.vector, "A": g.scalar, "G": g, "S": g.sync}
    total = {}
    for o in ops:
        if o["sem"]:
            total[o["sem"][0]] = total.get(o["sem"][0], 0) + o["sem"][1]
    pos = {i: k for k, i in enumerate(order)}
    need = set()
    seen = {}
    plan = {}
    for i in order:
        o = ops[i]
        best = {}
        w = []
        for d in o["deps"]:
            p = ops[d]
            if p["sem"]:
                key = (o["eng"], p["sem"][0])
                if key not in seen:
                    seen[key] = 1
                    w.append(("sem", p["sem"][0]))
            elif not (o["eng"] == "P" and p["eng"] == "P"):
                if pos[d] > best.get(p["eng"], (-1, 0))[0]:
                    best[p["eng"]] = (pos[d], d)
        for e, (k, d) in best.items():
            key = (o["eng"], "q" + e)
            if k > seen.get(key, -1):
                seen[key] = k
                need.add(d)
                w.append(("op", d))
        plan[i] = w
    cnt = {}
    val = {}
    for i in order:
        if i in need:
            e = ops[i]["eng"]
            cnt[e] = cnt.get(e, 0) + 1
            val[i] = cnt[e]
    sent = 0
    for i in order:
        o = ops[i]
        q = qs[o["eng"]]
        for kind, x in plan[i]:
            if kind == "sem":
                q.wait_ge(T.sem[x], total[x])
            else:
                q.wait_ge(T.sem["s" + ops[x]["eng"]], val[x])
        r = o["fn"]()
        if o["sem"]:
            if r is not None:
                r.then_inc(T.sem[o["sem"][0]], 16)
            else:
                sent += o["sem"][2]
        elif i in need:
            r.then_inc(T.sem["s" + o["eng"]], 1)
    g.wait_ge(T.sem.loc, sent)
    for e, c in cnt.items():
        g.wait_ge(T.sem["s" + e], c)
    for x in ("outA", "out"):
        g.wait_ge(T.sem[x], total[x])


def rank_program(g, core, T, topo):
    if T.rank_of(core) is None:
        return
    ops = build(g, core, T, topo)
    order, _ = schedule(ops)
    emit(g, T, ops, order)
